import numpy as np, ml_dtypes
CORES = [35,38,43,46]
N = 4
BF = ml_dtypes.bfloat16
def gentries(a):
    return np.ascontiguousarray(a.reshape(8, 16, -1).transpose(0, 2, 1)).reshape(8, -1)
def gtable(e):
    e = np.asarray(e); return np.ascontiguousarray(e.reshape(8, -1, 16).transpose(0, 2, 1)).reshape(128, -1).astype(np.int32)
W, C, RO = 4096, 256, 4
LA, LB, LE, WD = 864, 1024, 1024, 32
def parts(rng):
    x = rng.integers(0, 256, (N, 8, 16, W)); a = rng.integers(0, W, (N, 8, C, 16)); p = rng.integers(0, W, (N, 8, C, 16))
    pool = rng.integers(0, W, (N, 8, 32)); hot = np.take_along_axis(pool, rng.integers(0, 32, (N, 8, C * 16)), 2).reshape(N, 8, C, 16)
    return x, a, np.where(rng.random((N, 8, C, 16)) < 0.3, hot, p)
def pack(x, a, p):
    return {"x0": np.ascontiguousarray(x.reshape(N, 128, W)).astype(np.float32).astype(BF), "ka": np.stack([gtable(v.reshape(8, -1)) for v in a]), "ph": np.stack([gtable(v.reshape(8, -1)) for v in p])}
def alike(rng, a, p, share):
    m = (rng.random((N, 8, C, 1)) < share) & (np.arange(16) == rng.integers(0, 16, (N, 8, C, 1)))
    return np.where(m, a, p)
def setup_inputs(rng):
    x, a, p = parts(rng)
    return pack(x, a, alike(rng, a, p, 0.08))
def setup_inputs_spread(rng):
    x, a, p = parts(rng)
    v = np.minimum((np.exp2(8 * rng.random((N, 8, 1, W))) * rng.random(x.shape)).astype(np.int64), 255)
    x = np.where(rng.random(x.shape) < 0.5, v, 255 - v)
    a = np.minimum((W * rng.random(a.shape) ** 2).astype(np.int64), W - 1); u = np.minimum((W * rng.random(a.shape) ** 3).astype(np.int64), W - 1)
    return pack(x, a, np.where(rng.random(a.shape) < 0.5, u, p))
def setup_inputs_ends(rng):
    x, a, p = parts(rng); x = 255 * rng.integers(0, 2, x.shape)
    h = rng.choice(np.array([3, 4, 4, 5, 16]), (N, 8)); h[N - 1, 7] = 16; h[0, 7] = 4; h[0, 0] = 4; h[0, 1] = 3; h[N - 1, 6] = 4
    for r in range(N):
        for g in range(8):
            w = x[r, g]; w[:, W - 1] = w[:, 0]; o = rng.permutation(16)[:h[r, g]]
            if h[r, g] == 16: w[:, 0] = 0
            w[o, W - 1] = 255 - w[o, 0]
    kind = rng.choice(np.array([0, 1, 2]), (N, 8, C, 1), p=[0.4, 0.34, 0.26]); kind[:, :, [0, 1, 3, C - 2, C - 1]] = 0
    e = rng.integers(0, 2, (N, 8, C, 1))
    a = np.where(kind == 0, e * (W - 1), np.where(kind == 1, (W - 1) * rng.integers(0, 2, a.shape), a))
    p = np.where(kind == 0, (1 - e) * (W - 1), np.where(kind == 1, (W - 1) * rng.integers(0, 2, a.shape), p))
    return pack(x, a, p)
def setup_inputs_corners(rng):
    x = np.zeros((N, 8, 16, W), np.int64); a = np.zeros((N, 8, C, 16), np.int64); p = np.zeros((N, 8, C, 16), np.int64)
    far = np.array([LA - 1, LA, LA + 1, LB - 1, LB, LB + 3, LB + 4, LB + 59, LB + 60]); h = W // 2; M = 36; lane = np.arange(16)
    signs = np.stack([np.ones(16, np.int64), -np.ones(16, np.int64), 1 - 2 * (lane & 1)])
    for g in range(8):
        q = rng.permutation(W); low = q[1:h]; high = q[h + M:]; mids = q[h:h + M]
        m0 = rng.choice(np.array([-1, 0, 15, 15, 6]), C); o = lane[None, :] == m0[:, None]; o = o ^ (rng.random((C, 1)) < 0.5)
        k = rng.integers(0, 16, C); k = np.where(k == m0, (k + 1) & 15, k); swap = rng.random(C) < 0.5
        for r in range(N):
            w = x[r, g]; w[:, low] = rng.integers(0, 31, (16, len(low))); w[:, high] = rng.integers(215, 256, (16, len(high)))
            b = rng.integers(100, 151, 16); w[:, q[0]] = b; T = rng.permutation(np.resize(far, M))
            am = T[None, :] // 16 + (lane[:, None] < T[None, :] % 16); w[:, mids] = b[:, None] + am * signs[rng.integers(0, 3, M)].T
            lo1 = low[rng.integers(0, len(low), (C, 16))]; lo2 = low[rng.integers(0, len(low), (C, 16))]; hi1 = high[rng.integers(0, len(high), (C, 16))]; hi2 = high[rng.integers(0, len(high), (C, 16))]
            u = np.where(o, hi1, lo1); v = np.where(o, lo2, hi2)
            n = (0, 16, 15, C, 1, 17, 14, 31)[(g + 3 * r) % 8]; oc = rng.permutation(C); die = oc[:n]; rest = oc[n:]
            v[die, k[die]] = np.where(o[die, k[die]], hi2[die, k[die]], lo2[die, k[die]])
            edge = die[1::2]; under = mids[T == LA - 1]; md = under[rng.integers(0, len(under), len(edge))]
            u[edge, k[edge]] = np.where(swap[edge], md, q[0]); v[edge, k[edge]] = np.where(swap[edge], q[0], md)
            over = mids[T >= LA]; md = over[rng.integers(0, len(over), len(rest))]
            u[rest, k[rest]] = np.where(swap[rest], md, q[0]); v[rest, k[rest]] = np.where(swap[rest], q[0], md)
            assert int(np.sum(np.min(np.add.reduce(np.abs(w[:, u] - w[:, v]), axis=0), axis=1) < LA)) == n
            a[r, g] = u; p[r, g] = v
    return pack(x, a, p)
def setup_inputs_full(rng):
    x, a, p = parts(rng); lane = np.arange(16); h = W // 2; u = W // 4; z = int(rng.integers(0, N)); dead = int(rng.integers(0, 8))
    for g in range(8):
        if g == dead: continue
        for r in range(N):
            w = x[r, g]; q = rng.permutation(W); right = q[:h]; left = q[h:h + u]; out = q[h + u:]; b = rng.integers(100, 151, (16, 1))
            w[:, right] = b + rng.integers(0, 4, (16, h))
            far = np.where(rng.random((16, u)) < 0.5, 78 + rng.integers(0, 3, (16, u)), -75 - rng.integers(0, 3, (16, u)))
            near = np.argsort(rng.random((16, u)), axis=0) < 4
            w[:, left] = b + np.where(near, rng.integers(-8, 12, (16, u)), far)
            w[:, out] = b + rng.integers(90, 100, (16, len(out))) * (1 - 2 * rng.integers(0, 2, (16, len(out))))
            i = (rng.permutation(h)[:C], np.full(C, int(rng.integers(0, h))), rng.integers(0, 6, C))[(g + r) % 3]
            here = lane[None, :] == rng.integers(0, 16, (C, 1))
            a[r, g] = np.where(here, left[rng.integers(0, u, (C, 16))], right[rng.integers(0, h, (C, 16))])
            p[r, g] = np.where(here, right[i][:, None], out[rng.integers(0, len(out), (C, 16))])
    q = rng.permutation(np.arange(1, W)); s1 = q[:h]; s2 = q[h:h + u]; s0 = np.append(q[h + u:], 0)
    a[:, dead] = 0; p[:, dead] = s0[rng.integers(0, len(s0), (N, C, 16))]
    far = np.array([LB - 1, LB, LB + 1, LB + 3, LB + 4, LB + 31, LB + 59, LB + 60]); T = far[np.arange(h) % 8]
    cl = np.minimum(rng.integers(0, 8, (C, 1)) + rng.integers(0, 3, (C, 16)), 7)
    a[(z - 2) % N, dead] = s1[cl + 8 * rng.integers(0, h // 8, (C, 16))]; p[(z + 2) % N, dead] = s2[rng.integers(0, u, (C, 16))]
    x[:, dead] = rng.integers(215, 256, (N, 16, W))
    for r in range(N):
        w = x[r, dead]; w[:, s1] = rng.integers(0, 31, (16, h))
        if r == z:
            b = rng.integers(100, 151, (16, 1)); w[:] = b + rng.integers(0, 4, (16, W)); w[:, s2] = b
            w[:, s1] = b + (T[None, :] // 16 + (lane[:, None] < T[None, :] % 16)) * (1 - 2 * rng.integers(0, 2, (16, h)))
    return pack(x, a, p)
def setup_inputs_ties(rng):
    x, a, p = parts(rng); x = rng.integers(0, 176, x.shape)
    pool = rng.integers(0, W, (N, 8, 8)); pool[..., 0] = 0; pool[..., 7] = W - 1
    hot = np.take_along_axis(pool, rng.integers(0, 8, (N, 8, C * 16)), 2).reshape(N, 8, C, 16); p[:, 1::2] = hot[:, 1::2]
    src = np.arange(16) % rng.choice(np.array([1, 1, 1, 2, 4, 16]), (N, 8, C, 1))
    return pack(x, np.take_along_axis(a, src, 3), np.take_along_axis(p, src, 3))
def check_inputs(d):
    bad = []
    for k, lo, hi in (("x0", 0, 255), ("ka", 0, W - 1), ("ph", 0, W - 1)):
        v = np.asarray(d[k]).astype(np.float64)
        if not (np.min(v) >= lo and np.max(v) <= hi): bad.append("range of " + k)
    v = np.asarray(d["x0"]).astype(np.float64)
    if np.any(v != np.floor(v)): bad.append("whole numbers of x0")
    return bad
def reference(x0, ka, ph):
    X = x0.astype(np.float32).astype(np.int32).reshape(N, 8, 16, W)
    K = np.stack([gentries(v) for v in ka]).astype(np.int64).reshape(N, 8, C, 16)
    P = np.stack([gentries(v) for v in ph]).astype(np.int64).reshape(N, 8, C, 16)
    A = np.zeros((N, 8, 1), np.int64); place = np.arange(16)
    for t in range(RO):
        if t > 0: K = np.roll(K, 1, axis=0); P = np.roll(P, -1, axis=0)
        for r in range(N):
            x, a, p = X[r], K[r].copy(), P[r].copy()
            s = np.take_along_axis(x, a.reshape(8, 1, C * 16), 2).reshape(8, 16, C, 16); y = np.take_along_axis(x, p.reshape(8, 1, C * 16), 2).reshape(8, 16, C, 16)
            D = np.add.reduce(np.abs(s - y), axis=1)
            k = np.argmin(D, axis=2)
            d = np.take_along_axis(D, k[:, :, None], 2)[:, :, 0]
            sk = np.take_along_axis(s, k[:, None, :, None], 3)[..., 0]; yk = np.take_along_axis(y, k[:, None, :, None], 3)[..., 0]
            kill = d < LA; prime = ~kill & (d < LB + 4 * (A[r] & 15))
            step = np.where(np.add.reduce(sk, axis=1) > np.add.reduce(yk, axis=1), 1, -1) * (1 + (d & 3))
            n = np.take_along_axis(p, ((k + step) & 15)[:, :, None], 2)[:, :, 0]
            xn = np.take_along_axis(x, n[:, None, :], 2)
            near = np.add.reduce(np.abs(s - xn[..., None]), axis=1) < LE
            m = np.where(np.any(near, axis=2), np.argmax(near, axis=2), -1)
            fresh = np.take_along_axis(a, np.clip(m[:, :, None] + place, 0, 15), 2); fresh[:, :, 0] = n
            v = np.take_along_axis(p, k[:, :, None], 2)[:, :, 0]; new = np.where(np.abs(sk - yk) <= WD, (yk + 128) & 255, yk)
            for g in range(8):
                c = np.nonzero(prime[g])[0]; w = c[np.unique(v[g, c], return_index=True)[1]]
                x[g][:, v[g, w]] = new[g][:, w]
            P[r] = np.where(kill[:, :, None], (((a * p) >> 5) + p) & (W - 1), p)
            K[r] = np.where(prime[:, :, None], fresh, a)
            A[r] = A[r] + np.add.reduce(kill.astype(np.int64), axis=1)[:, None]
    return {"yk": np.stack([gtable(v.reshape(8, -1)) for v in K]).astype(np.float32), "yp": np.stack([gtable(v.reshape(8, -1)) for v in P]).astype(np.float32), "yx": X.reshape(N, 128, W).astype(np.float32).astype(BF)}

@@ -1,0 +1,495 @@
+import numpy as np
+from concourse.mybir import AluOpType as A, ActivationFunctionType as F
+
+R, H, LO = 4, 128, 16
+NB1 = 0
+CH = 4
+BIG = float(2 ** 30)
+OFF = 65536.0
+FW, WW, XW = 18 * 256, 18 * 256, 4352
+
+SCRATCH = {
+    "X": ("sbuf", [128, XW], "bfloat16"),
+    "KI": ("sbuf", [128, 256], "int32"), "PI": ("sbuf", [128, 256], "int32"),
+    "KF": ("sbuf", [128, 256], "float32"), "PF": ("sbuf", [128, 256], "float32"),
+    "Y0": ("sbuf", [128, 2048], "bfloat16"), "D0": ("sbuf", [128, 2048], "bfloat16"), "R0": ("sbuf", [128, 2048], "bfloat16"),
+    "S1": ("sbuf", [128, 2048], "bfloat16"), "D1": ("sbuf", [128, 2048], "bfloat16"), "R1": ("sbuf", [128, 2048], "bfloat16"),
+    "A0": ("sbuf", [128, 2048], "bfloat16"), "A1": ("sbuf", [128, 2048], "bfloat16"), "M1": ("sbuf", [128, 2048], "bfloat16"),
+    "KM": ("sbuf", [128, 256], "float32"), "KC": ("sbuf", [128, 256], "float32"), "QM": ("sbuf", [128, 256], "float32"),
+    "KB": ("sbuf", [128, 256], "bfloat16"),
+    "LI": ("sbuf", [128, 256], "int32"), "LF": ("sbuf", [128, 336], "float32"),
+    "uf0": ("sbuf", [128, 8], "uint16"), "uf1": ("sbuf", [128, 8], "uint16"), "uk": ("sbuf", [128, 16], "uint16"),
+    "uu": ("sbuf", [128, 16], "uint16"), "uWV": ("sbuf", [128, 32], "uint16"), "uX": ("sbuf", [128, 16], "uint16"),
+    "XN0": ("sbuf", [128, 128], "bfloat16"), "XN1": ("sbuf", [128, 128], "bfloat16"), "SF1": ("sbuf", [128, 128], "bfloat16"),
+    "SK1": ("sbuf", [128, 128], "bfloat16"), "YK": ("sbuf", [128, 256], "bfloat16"), "AD": ("sbuf", [128, 256], "bfloat16"),
+    "w2": ("sbuf", [128, 256], "bfloat16"), "wg": ("sbuf", [128, 256], "bfloat16"),
+    "pen": ("sbuf", [128, 256], "bfloat16"), "ts": ("sbuf", [128, 256], "bfloat16"), "tb": ("sbuf", [128, 256], "bfloat16"), "tm": ("sbuf", [128, 256], "bfloat16"),
+    "kp": ("sbuf", [128, 256], "int32"), "kq": ("sbuf", [128, 256], "int32"), "p1": ("sbuf", [128, 256], "int32"), "p2": ("sbuf", [128, 256], "int32"), "p3": ("sbuf", [128, 256], "int32"),
+    "KD": ("sbuf", [128, 256], "float32"), "K15": ("sbuf", [128, 256], "float32"), "BA": ("sbuf", [128, 256], "float32"), "KN": ("sbuf", [128, 256], "float32"),
+    "W": ("sbuf", [128, WW], "float32"), "FF": ("sbuf", [128, FW], "float32"), "kd": ("dram", [8, 17, 256], "float32"),
+    "VG": ("sbuf", [128, 256], "float32"), "RU": ("sbuf", [128, 256], "float32"), "Vu": ("sbuf", [128, 256], "uint16"),
+    "FD": ("sbuf", [128, 256], "bfloat16"), "EQ": ("sbuf", [128, 15 * 256], "bfloat16"), "SE": ("sbuf", [128, 256], "float32"),
+    "KJ": ("sbuf", [128, 256], "bfloat16"),
+    "ia": ("sbuf", [128, 256], "int32"), "ib": ("sbuf", [128, 256], "int32"), "ic": ("sbuf", [128, 256], "int32"), "idd": ("sbuf", [128, 256], "int32"),
+    "If": ("sbuf", [128, 128], "float32"), "Ib": ("sbuf", [128, 128], "bfloat16"), "In": ("sbuf", [128, 128], "bfloat16"),
+    "mf": ("sbuf", [128, 128], "float32"), "mb": ("sbuf", [128, 128], "bfloat16"), "OD": ("sbuf", [128, 256], "bfloat16"),
+    "B8f": ("sbuf", [128, 8], "float32"), "B8": ("sbuf", [128, 8], "bfloat16"), "B8n": ("sbuf", [128, 8], "bfloat16"), "B82": ("sbuf", [128, 8], "bfloat16"),
+    "WN": ("sbuf", [128, 8], "bfloat16"), "WR": ("sbuf", [128, 8], "bfloat16"), "WP": ("sbuf", [128, 8], "bfloat16"),
+    "BKf": ("sbuf", [128, 128], "float32"), "BKn": ("sbuf", [128, 128], "bfloat16"), "BK8": ("sbuf", [128, 128], "bfloat16"),
+    "L0": ("sbuf", [128, 128], "float32"), "L15": ("sbuf", [128, 128], "float32"), "LD": ("sbuf", [128, 128], "float32"),
+    "RS": ("sbuf", [128, 256], "float32"), "RN": ("sbuf", [128, 128], "bfloat16"), "RB": ("sbuf", [128, 128], "bfloat16"),
+    "NB": ("sbuf", [128, 128], "bfloat16"), "J4": ("sbuf", [128, 128], "bfloat16"), "Z": ("sbuf", [128, 512], "bfloat16"), "c15": ("sbuf", [128, 8], "bfloat16"),
+    "cb": ("sbuf", [128, 1], "float32"), "cy": ("sbuf", [128, 1], "float32"), "Hb": ("sbuf", [128, 128], "bfloat16"), "HH": ("sbuf", [128, 128], "bfloat16"),
+    "b0": ("psum", [128, 512], "float32"), "b1": ("psum", [128, 512], "float32"), "b2": ("psum", [128, 512], "float32"), "b3": ("psum", [128, 512], "float32"),
+    "b4": ("psum", [128, 512], "float32"), "b5": ("psum", [128, 512], "float32"), "b6": ("psum", [128, 512], "float32"), "b7": ("psum", [128, 512], "float32"),
+}
+SMALL = {}
+for _b, _l in (("LI", "q r sg a s2 a1 dl fs f k o1 o2 CL C16 Ai Am"), ("LF", "lt nk pr prb fx fx2 fm fm2 fo fo2 uy uz ow CW CK CU CF CF2 cnt Af thr")):
+    for _i, _n in enumerate(_l.split()):
+        SMALL[_n] = (_b, 16 * _i, 16 * _i + (1 if _n in ("Ai", "Am", "cnt", "Af", "thr") else 16))
+for _n, _a, _z in (("fk", "f", "k"), ("pp", "pr", "prb"), ("fxx", "fx", "fx2"), ("fmm", "fm", "fm2"), ("foo", "fo", "fo2"), ("CWK", "CW", "CK"), ("CFF", "CF", "CF2")):
+    SMALL[_n] = (SMALL[_a][0], SMALL[_a][1], SMALL[_z][2])
+for _n in ("K", "P"):
+    for _t in range(R):
+        SCRATCH["%sl%d" % (_n, _t)] = ("sbuf", [128, 256], "uint16")
+        if _t < R - 1:
+            SCRATCH["%so%d" % (_n, _t)] = ("sbuf", [128, 256], "uint16")
+
+SEMAPHORES = ["v", "s", "t", "p", "ls", "dx", "dk", "dp", "dw", "dw2", "dkd", "df", "dy1", "dy2", "dy3"] + ["%sa%d" % (n, t) for n in "KP" for t in range(1, R)]
+
+
+def rank_program(g, core, T, topo):
+    rank = T.rank_of(core)
+    if rank is None:
+        return
+    nxt, prv = T.cores[(rank + 1) % 4], T.cores[(rank + 3) % 4]
+    queues = {"v": g.vector, "s": g.scalar, "t": g.tensor, "p": g, "y": g.sync}
+    cnt = {}
+    known = {q: {} for q in queues}
+    snaps = {}
+    recs = {}
+
+    def bank(b):
+        return len(b) == 2 and b[0] == "b" and b[1].isdigit()
+
+    def key(x):
+        return x if isinstance(x, tuple) else (x, 0, 1 << 30)
+
+    def sync(q, reads, writes):
+        need = {}
+        for accs, wr in ((reads, False), (writes, True)):
+            for x in accs:
+                b, lo, hi = key(x)
+                for (l2, h2, q2, sm, val, w2) in recs.get(b, ()):
+                    if bank(b):
+                        hit = q2 != q or (q != "t" and (wr or w2) and l2 < hi and lo < h2)
+                    else:
+                        hit = (wr or w2) and l2 < hi and lo < h2 and not q2 == q == "t"
+                    if hit and val > known[q].get(sm, 0):
+                        need[sm] = max(need.get(sm, 0), val)
+        kn = known[q]
+        for sm in sorted(need):
+            if any(o != sm and snaps.get((o, need[o]), {}).get(sm, 0) >= need[sm] for o in need):
+                continue
+            queues[q].wait_ge(T.sem[sm], need[sm])
+        for sm, val in need.items():
+            for o, x in snaps.get((sm, val), {}).items():
+                kn[o] = max(kn.get(o, 0), x)
+            kn[sm] = max(kn.get(sm, 0), val)
+
+    def note(q, reads, writes, sm, val):
+        snap = dict(known[q])
+        snap[sm] = max(snap.get(sm, 0), val)
+        snaps[(sm, val)] = snap
+        for accs, wr in ((reads, False), (writes, True)):
+            for x in accs:
+                b, lo, hi = key(x)
+                old = recs.get(b, [])
+                if wr and not bank(b):
+                    old = [e for e in old if not (lo <= e[0] and e[1] <= hi)]
+                old = [e for e in old if not (e[2] == q and e[3] == sm and e[0] >= lo and e[1] <= hi and (wr or not e[5]))]
+                recs[b] = old + [(lo, hi, q, sm, val, wr)]
+
+    def op(q, call, reads, writes):
+        sync(q, reads, writes)
+        cnt[q] = cnt.get(q, 0) + 1
+        call().then_inc(T.sem[q], 1)
+        note(q, reads, writes, q, cnt[q])
+
+    def dmas(q, sm, pairs, reads, writes):
+        sync(q, reads, writes)
+        for out, in_ in pairs:
+            queues[q].dma_start(out, in_).then_inc(T.sem[sm], 16)
+            cnt[sm] = cnt.get(sm, 0) + 16
+        note(q, reads, writes, sm, cnt[sm])
+
+    V, S, E = g.vector, g.scalar, g.tensor
+
+    def pa(x):
+        return x[3] if len(x) > 3 else T[x[0]][:, x[1]:x[2]]
+
+    def ks(*xs):
+        return [x[:3] for x in xs if isinstance(x, tuple)] + [x[4] for x in xs if isinstance(x, tuple) and len(x) > 4]
+
+    def v_tt(o, a, b, f):
+        op("v", lambda: V.tensor_tensor(pa(o), pa(a), pa(b), f), ks(a, b), ks(o))
+
+    def v_ts(o, a, x, f, y=None, f2=None):
+        x1 = pa(x) if isinstance(x, tuple) else x
+        if f2 is None:
+            op("v", lambda: V.tensor_scalar(pa(o), pa(a), x1, None, f), ks(a, x), ks(o))
+        else:
+            op("v", lambda: V.tensor_scalar(pa(o), pa(a), x1, y, f, f2), ks(a, x), ks(o))
+
+    def v_cp(o, a):
+        op("v", lambda: V.tensor_copy(pa(o), pa(a)), ks(a), ks(o))
+
+    def v_scan(o, d0, d1, init, f, f2):
+        op("v", lambda: V.tensor_tensor_scan(pa(o), pa(d0), pa(d1), init, f, f2), ks(d0, d1), ks(o))
+
+    def v_ms(o, c):
+        op("v", lambda: V.memset(pa(o), c), [], ks(o))
+
+    def s_act(o, a, f):
+        op("s", lambda: S.activation(pa(o), pa(a), f), ks(a), ks(o))
+
+    def s_mul(o, a, c):
+        op("s", lambda: S.activation(pa(o), pa(a), F.Copy, scale=c), ks(a), ks(o))
+
+    def mm(o, l, r, start, stop):
+        op("t", lambda: E.matmul(pa(o), pa(l), pa(r), start, stop), ks(l, r), ks(o))
+
+    def iota(o, pattern, base, cm):
+        flag = {} if o[0] in ("ia", "ib", "ic", "idd", "LI") else {"allow_small_or_imprecise_dtypes": True}
+        op("p", lambda: g.iota(pa(o), pattern, base, cm, **flag), [], ks(o))
+
+    def ind(w, lo, hi, u, c0, c1):
+        return (w, lo, hi, T[w][:, lo:hi].indirect(T[u][:, c0:c1]), (u, c0, c1))
+
+    def st(b, lo, hi, step):
+        return (b, lo, hi, T[b][:, lo:hi:step])
+
+    def rev(b, lo, hi):
+        return (b, lo, hi, T[b][:, hi - 1:lo - 1:-1] if lo else T[b][:, hi - 1::-1])
+
+    def full(b):
+        return SMALL[b] if b in SMALL else (b, 0, int(SCRATCH[b][1][-1]))
+
+    def h8(b, h):
+        x = full(b)
+        return (x[0], x[1] + h * 8, x[1] + h * 8 + 8)
+
+    def half(b, h):
+        return (b, h * H, h * H + H)
+
+    for t in range(1, R):
+        for n, src in (("K", prv), ("P", nxt)):
+            sm = "%sa%d" % (n, t)
+            cnt[sm] = len(topo.engines(src, core))
+            recs["%sl%d" % (n, t)] = [(0, 256, "r", sm, cnt[sm], True)]
+    dmas("y", "dp", [(T.PI[:], T.ph[:])], [], ["PI"])
+    dmas("y", "dk", [(T.KI[:], T.ka[:])], [], ["KI"])
+    dmas("y", "dx", [(T.X[:, 0:4096], T.x0[:])], [], [("X", 0, 4096)])
+
+    iota(full("ia"), [[1, 256]], 256, -1)
+    iota(full("ib"), [[0, 256]], 0, 1)
+    iota(full("ic"), [[1, 256]], 0, 0)
+    iota(full("J4"), [[0, 8], [4096, 16]], 0, 0)
+    iota(full("CL"), [[16, 16]], 0, 0)
+    iota(("W", 0, 17 * 256), [[0, 17 * 256]], 0, 0)
+    iota(("W", 17 * 256, WW), [[1, 256]], 4096, 0)
+    iota(full("FF"), [[0, FW]], 0, 0)
+    v_ms(("X", 4096, XW), 0.0)
+    v_ms(full("Z"), 0.0)
+    v_ms(full("NB"), -864.0 * 65536)
+    v_ms(full("c15"), 15.0)
+    v_ms(("FD", 0, 1), 0.0)
+    v_ms(full("Af"), 0.0)
+    v_ms(full("thr"), 160.0 * 65536 - 1)
+    v_ms(full("KD"), 0.0)
+    v_ms(full("CF"), 16.0)
+    v_ms(full("CF2"), 17.0)
+    v_ms(full("cb"), -2000.5)
+    v_ms(full("cy"), -127.5)
+    v_ms(full("HH"), 0.5)
+    v_cp(full("Pl0"), full("PI"))
+    v_cp(full("Kl0"), full("KI"))
+    dmas("y", "dkd", [(T.kd[:, 0:1, :], T.KD[0:8, 0:256])], ["KD"], ["kd0"])
+    v_ts(full("If"), ("ia", 0, 128), 256.0, A.is_equal)
+    s_act(full("Ib"), full("If"), F.Copy)
+    s_mul(full("In"), full("If"), -1.0)
+    s_mul(full("Hb"), full("If"), 0.5)
+    v_ts(full("idd"), full("ia"), 15, A.bitwise_and)
+    v_ts(full("mf"), ("idd", 0, 128), 0.0, A.is_equal)
+    s_act(full("mb"), full("mf"), F.Copy)
+    v_ts(full("OD"), full("idd"), 0.0, A.not_equal, OFF, A.mult)
+    v_ts(full("ia"), full("ib"), 4, A.arith_shift_right)
+    v_tt(full("B8f"), ("ia", 0, 8), ("ic", 0, 8), A.is_equal)
+    s_act(full("B8"), full("B8f"), F.Copy)
+    s_mul(full("WN"), full("B8f"), -65536.0)
+    s_mul(full("WP"), full("B8f"), 65536.0)
+    s_mul(full("WR"), full("B8f"), 131072.0)
+    s_mul(full("B8n"), full("B8f"), -1.0)
+    s_mul(full("B82"), full("B8f"), 2.0)
+    v_ts(full("idd"), full("ic"), 4, A.arith_shift_right)
+    v_tt(full("BKf"), ("ia", 0, 128), ("idd", 0, 128), A.is_equal)
+    s_mul(full("BK8"), full("BKf"), 8192.0)
+    v_ts(full("ic"), full("ic"), 15, A.bitwise_and)
+    v_ts(full("ib"), full("ib"), 15, A.bitwise_and)
+    v_ts(full("RS"), full("ic"), 0.0, A.is_equal, BIG, A.mult)
+    v_ts(full("RB"), ("ic", 0, 128), 0.0, A.is_equal, 1024.0, A.mult)
+    v_ts(full("RN"), full("RB"), -1.0, A.add)
+    v_ts(full("L0"), ("ic", 0, 128), 4.0 * NB1, A.is_ge, -1.0, A.mult)
+    v_tt(full("BKn"), full("L0"), full("BKf"), A.mult)
+    v_ts(full("L0"), ("ib", 0, 128), 0.0, A.is_equal)
+    v_tt(full("L0"), full("L0"), full("BKf"), A.mult)
+    v_ts(full("L15"), ("ib", 0, 128), 15.0, A.is_equal)
+    v_tt(full("L15"), full("L15"), full("BKf"), A.mult)
+    v_tt(full("LD"), full("If"), full("L15"), A.subtract)
+    v_ts(full("If"), ("ic", 0, 128), 0.0, A.not_equal)
+    v_tt(full("L15"), full("L15"), full("If"), A.mult)
+    v_tt(full("CL"), full("CL"), ("ib", 0, 16), A.add)
+    v_ts(full("C16"), full("CL"), 16.0, A.mult)
+    v_ts(h8("C16", 1), h8("C16", 1), -2048.0, A.add)
+    v_ts(full("CW"), full("CL"), 4096.0, A.add)
+    v_ts(full("CK"), full("CL"), 17 * 256.0, A.add)
+    v_ts(full("CU"), full("CL"), 256.0, A.add)
+
+    hb = ("b0", "b1")
+    KEY = [(hb[h], 0, 128) for h in range(2)]
+    ND = [(hb[h], 128, 256) for h in range(2)]
+    QT = [(hb[h], 264, 272) for h in range(2)]
+    KILL = [("b2", 0, 128), ("b2", 128, 256)]
+    XP = ("b2", 256, 384)
+    QL = [("b2", 384, 392), ("b2", 392, 400)]
+    VP, VE, ME = ("b3", 0, 256), ("b4", 0, 256), ("b5", 0, 256)
+    NEAR = ("b4", "b5", "b6", "b7")
+
+    def strip(k, j):
+        return (k[0], k[1], k[2], T[k[0]][:, k[1] + j:k[2]:16])
+
+    def group(k, src, w, stop=False, step=16, js=range(LO)):
+        for j in js:
+            x = st(src, j, 2048, 16) if step == 16 else (src, j * 128, j * 128 + 128)
+            mm(strip(k, j), x, full(w), False, stop and j == js[-1])
+
+    def bias(h):
+        mm(KEY[h], full("Ib"), full("NB"), True, False)
+        mm(KEY[h], full("Ib"), full("J4"), False, False)
+
+    def best(h):
+        v_scan(half("KM", h), ("RS", 0, 128), KEY[h], BIG, A.add, A.min)
+        v_scan(rev("KC", h * H, h * H + H), ("RS", 0, 128), rev("KM", h * H, h * H + H), BIG, A.add, A.min)
+        v_tt(half("QM", h), half("KC", h), full("mf"), A.mult)
+        op("s", lambda: S.activation(pa(half("KB", h)), pa(half("KC", h)), F.Sign, bias=T.cb[:], scale=-1.0), [half("KC", h), full("cb")], [half("KB", h)])
+
+    def best_t(h):
+        mm(QL[h], half("QM", h), full("B8f"), True, True)
+        mm(KILL[h], half("KB", h), full("Hb"), True, False)
+        mm(KILL[h], full("Ib"), full("HH"), False, True)
+
+    def pick(h):
+        q, r, sg, a, s2, a1, dl, fs, f, o1 = [h8(n, h) for n in ("q", "r", "sg", "a", "s2", "a1", "dl", "fs", "f", "o1")]
+        v_ts(q, QL[h], 2047.0, A.add)
+        v_ts(sg, q, 11, A.arith_shift_right, 1, A.bitwise_and)
+        v_ts(a, q, 16, A.arith_shift_right, 3, A.bitwise_and)
+        v_ts(s2, sg, 2.0, A.mult, -1.0, A.add)
+        v_ts(a1, a, 1.0, A.add)
+        v_ts(r, q, 12, A.arith_shift_right)
+        v_tt(dl, s2, a1, A.mult)
+        v_tt(fs, r, dl, A.add)
+        v_ts(f, fs, 15, A.bitwise_and)
+        v_tt(o1, f, h8("C16", h), A.add)
+        v_cp(full("uf%d" % h), o1)
+
+    def near_open(b):
+        mm((NEAR[b], 0, 512), full("Ib"), full("Z"), True, False)
+
+    def near_load(b, srcs):
+        for i, src in enumerate(srcs):
+            for j in range(4):
+                mm((NEAR[b], j * 128, j * 128 + 128), full("Ib"), st(src, 4 * b + j, 2048, 16), False, False)
+
+    def near_diff(b, xn, out):
+        for j in range(4):
+            mm((NEAR[b], j * 128, j * 128 + 128), full("In"), full(xn), False, j == 3)
+        s_act((out, b * 512, b * 512 + 512), (NEAR[b], 0, 512), F.Abs)
+
+    def penalty(h):
+        v_ts(half("pen", h), ND[h], 1024.0, A.is_ge, 16.0, A.mult)
+        v_scan(half("ts", h), full("RN"), half("pen", h), 1024.0, A.add, A.min)
+        v_scan(rev("tb", h * H, h * H + H), full("RB"), rev("ts", h * H, h * H + H), 1024.0, A.add, A.min)
+        v_tt(half("tm", h), half("tb", h), full("mb"), A.mult)
+        mm(QT[h], full("Ib"), full("c15"), True, False)
+        mm(QT[h], half("tm", h), full("B8"), False, True)
+
+    def send(n, t, dst):
+        b, l, sm = "%so%d" % (n, t), "%sl%d" % (n, t + 1), "%sa%d" % (n, t + 1)
+        rid, pid, _ = topo.addr(dst)
+        sync("p", [full(b)], [])
+        g.remote_dma(T[l][:], T[b][:], T.sem[sm], T.sem.ls, pid, rid, topo.mask(core, dst))
+        cnt["ls"] = cnt.get("ls", 0) + len(topo.engines(core, dst))
+
+    def thresh(t):
+        if t:
+            v_tt(full("Af"), full("Af"), full("cnt"), A.add)
+            v_cp(full("Ai"), full("Af"))
+            v_ts(full("Am"), full("Ai"), 15, A.bitwise_and)
+            v_ts(full("thr"), full("Am"), 262144.0, A.mult, 160.0 * 65536 - 1, A.add)
+
+    FK = ["F%d" % j for j in range(1, 15)] + ["F17"]
+    recs.update({k: list(recs["FF"]) for k in FK})
+    recs.update({"W0": list(recs["W"]), "W16": list(recs["W"])})
+    WK = ["W0", "W16", "W"]
+
+    for t in range(R):
+        Kl, Pl = "Kl%d" % t, "Pl%d" % t
+        last = t == R - 1
+
+        def own_names():
+            mm(VP, full("L0"), full("VG"), True, True)
+
+        def own_marks():
+            for x in (VE, ME):
+                mm(x, full("L0"), full("VG"), True, False)
+                mm(x, full("Ib"), full("OD"), False, x is VE)
+
+        def near_max():
+            for j in range(4 * NB1, LO):
+                v_tt(("M1", j * 128, j * 128 + 128), st("S1", j, 2048, 16), XP, A.max)
+                mm(strip(ND[1], j), ("M1", j * 128, j * 128 + 128), full("B82"), False, j == LO - 1)
+
+        def write_table():
+            v_scan(full("RU"), full("RS"), VE, BIG, A.add, A.min)
+            v_cp(full("Vu"), VP)
+            v_tt(("FD", 1, 256), ("b3", 1, 256), ("RU", 0, 255), A.is_equal)
+            mm(ME, full("BK8"), full("FD"), False, False)
+            for c in range(15):
+                lo = 16 * c + 16
+                v_ts(("EQ", c * 256 + lo, c * 256 + 256), ("Vu", lo, 256), ("RU", 16 * c + 15, 16 * c + 16), A.is_equal)
+                mm(("b5", lo, 256), full("BK8"), ("EQ", c * 256 + lo, c * 256 + 256), False, c == 14)
+            s_act(("YK", 0, 128), ind("Y0", 0, 2048, "uk", 0, 8), F.Copy)
+            s_act(("AD", 0, 128), ind("D0", 0, 2048, "uk", 0, 8), F.Abs)
+            s_act(full("SK1"), ind("S1", 0, 2048, "uk", 8, 16), F.Copy)
+            s_act(("AD", 128, 256), ind("D1", 0, 2048, "uk", 8, 16), F.Abs)
+            op("s", lambda: S.activation(T.KJ[:], T.b2[:, 0:256], F.Copy, accum_out=pa(full("cnt"))), [("b2", 0, 256)], [full("KJ"), full("cnt")])
+            v_tt(("YK", 128, 256), ind("D1", 0, 2048, "uk", 8, 16), full("SK1"), A.add)
+            v_ts(full("w2"), full("AD"), 32.0, A.is_le, -128.0, A.mult)
+            op("s", lambda: S.activation(T.b6[:, 0:256], T.YK[:], F.Sign, bias=T.cy[:]), [full("YK"), full("cy")], [("b6", 0, 256)])
+            v_tt(full("wg"), full("w2"), ("b6", 0, 256), A.mult)
+            v_scan(full("SE"), full("RS"), ME, BIG, A.add, A.min)
+            v_tt(full("ow"), st("SE", 15, 256, 16), full("CW"), A.min)
+            v_cp(full("uX"), full("ow"))
+            xs = T.X[:, 0:XW].indirect(T.uX[:, 0:16])
+            op("v", lambda: V.tensor_tensor(xs, T.YK[:], T.wg[:], A.add), [full("uX"), full("YK"), full("wg")], ["X"])
+
+        v_cp(full("PF"), full("PI") if t == 0 else full(Pl))
+        dmas("y", "dw", [(T.W[0::16, 0:4096], T.PF[:])], ["PF"], ["W0"])
+        n, l = 2048 // CH, 128 // CH
+        for c in range(CH):
+            s_act(("Y0", c * n, c * n + n), ind("X", 0, 4096, Pl, c * l, c * l + l), F.Copy)
+        v_cp(full("KF"), full("KI") if t == 0 else full(Kl))
+        bias(0)
+        mm(("b3", 0, 256), full("LD"), full("KF"), True, True)
+        bias(1)
+        mm(("b3", 256, 512), full("L15"), full("KF"), True, True)
+        for b in range(4):
+            near_open(b)
+        for c in range(CH):
+            v_tt(("D0", c * n, c * n + n), ind("X", 0, 4096, Kl, c * l, c * l + l), ("Y0", c * n, c * n + n), A.subtract)
+        s_act(full("KD"), ("b3", 0, 256), F.Copy)
+        for c in range(2):
+            s_act(("S1", c * 1024, c * 1024 + 1024), ind("X", 0, 4096, Kl, 128 + c * 64, 192 + c * 64), F.Copy)
+        s_act(full("K15"), ("b3", 256, 512), F.Copy)
+        dmas("y", "dkd", [(T.kd[:, 1:17, :], T.KD[:])], ["KD"], ["kd"])
+        dmas("y", "dw2", [(T.W[0::16, 4096:4352], T.KF[0::16, :])], ["KF"], ["W16"])
+        dmas("y", "df", [(T.FF[j::16, 256:(16 - j) * 256], T.kd[:, j + 1:16, :]) for j in range(1, 15)] + [(T.FF[:, 17 * 256:18 * 256], T.kd[:, 0:16, :])], ["kd", "kd0"], FK)
+        group(KEY[0], "D0", "WN")
+        v_ts(full("R0"), full("D0"), 0.0, A.max)
+        group(KEY[0], "R0", "WR")
+        group(KEY[0], "D0", "B8", stop=True)
+        for c in range(2):
+            v_tt(("D1", c * 1024, c * 1024 + 1024), ind("X", 0, 4096, Pl, 128 + c * 64, 192 + c * 64), ("S1", c * 1024, c * 1024 + 1024), A.subtract)
+        for c in range(2):
+            s_act(("R1", c * 1024, c * 1024 + 1024), ("D1", c * 1024, c * 1024 + 1024), F.Abs)
+        near_load(0, ("D0", "Y0"))
+        near_load(1, ("D0", "Y0"))
+        best(0)
+        best_t(0)
+        v_tt(full("kp"), full("KF"), full("PF"), A.mult)
+        group(KEY[1], "R1", "WP")
+        group(KEY[1], "D1", "B8n", stop=True)
+        pick(0)
+        s_act(full("XN0"), ind("Y0", 0, 2048, "uf0", 0, 8), F.Copy)
+        best(1)
+        near_diff(0, "XN0", "A0")
+        best_t(1)
+        v_ts(full("kq"), full("kp"), 5, A.arith_shift_right)
+        thresh(t)
+        pick(1)
+        near_diff(1, "XN0", "A0")
+        s_act(full("SF1"), ind("S1", 0, 2048, "uf1", 0, 8), F.Copy)
+        for b in range(2, 4):
+            near_load(b, ("D0", "Y0"))
+            near_diff(b, "XN0", "A0")
+        v_tt(full("p1"), full("kq"), ("b2", 0, 256), A.mult)
+        v_tt(full("XN1"), ind("D1", 0, 2048, "uf1", 0, 8), full("SF1"), A.add)
+        mm(XP, full("Ib"), full("XN1"), True, True)
+        mm(ND[1], full("XN1"), full("BKn"), True, False)
+        for b in range(NB1):
+            near_open(b)
+            near_load(b, ("S1",))
+            near_diff(b, "XN1", "A1")
+        group(ND[1], "S1", "B8n", js=range(4 * NB1, LO))
+        mm(ND[0], full("Ib"), ("Z", 0, 128), True, False)
+        v_tt(full("p2"), full("p1"), full("PF"), A.add)
+        v_ts(full("p3"), full("p2"), 4095, A.bitwise_and)
+        if not last:
+            v_cp(full("Po%d" % t), full("p3"))
+            send("P", t, prv)
+        v_ts(full("nk"), full("q"), 47.0, A.is_ge)
+        v_ts(full("lt"), full("q"), full("thr"), A.is_lt, 256.0, A.mult)
+        v_ts(full("k"), full("r"), 15, A.bitwise_and)
+        v_tt(full("pr"), full("nk"), full("lt"), A.mult)
+        v_tt(full("prb"), full("nk"), full("lt"), A.mult)
+        v_tt(full("fxx"), full("fk"), full("CFF"), A.subtract)
+        v_tt(full("o2"), full("k"), full("C16"), A.add)
+        v_tt(full("fmm"), full("fxx"), full("pp"), A.mult)
+        v_cp(full("uk"), full("o2"))
+        v_tt(full("foo"), full("fmm"), full("CWK"), A.add)
+        v_cp(full("uWV"), full("foo"))
+        vw = ind("W", 0, WW, "uWV", 16, 32)
+        op("s", lambda: S.activation(T.VG[:], vw[3], F.Copy), WK + [full("uWV")], ["VG"])
+        if last:
+            own_names()
+            own_marks()
+        group(ND[0], "A0", "B8", stop=True, step=1)
+        group(ND[1], "A1", "B8", step=1, js=range(4 * NB1))
+        near_max()
+        if last:
+            write_table()
+            dmas("y", "dy3", [(T.yx[:], T.X[:, 0:4096])], ["X"], ["yx"])
+        penalty(0)
+        if not last:
+            own_names()
+        bw = ind("W", 0, WW, "uWV", 0, 16)
+        op("v", lambda: V.tensor_tensor(T.BA[:], bw[3], T.K15[:], A.add), WK + [full("uWV"), full("K15")], ["BA"])
+        penalty(1)
+        if not last:
+            own_marks()
+        for h in range(2):
+            v_tt(h8("uy", h), QT[h], h8("pr", h), A.mult)
+            v_tt(h8("uz", h), h8("uy", h), h8("CU", h), A.add)
+        v_cp(full("uu"), full("uz"))
+        fw = ind("FF", 0, FW, "uu", 0, 16)
+        op("v", lambda: V.tensor_tensor(T.KN[:], fw[3], T.BA[:], A.add), FK + ["FF", full("uu"), full("BA")], [full("KN")])
+        if not last:
+            v_cp(full("Ko%d" % t), full("KN"))
+            send("K", t, nxt)
+            write_table()
+        else:
+            dmas("y", "dy1", [(T.yk[:], T.KN[:])], ["KN"], ["yk"])
+            v_cp(full("PF"), full("p3"))
+            dmas("y", "dy2", [(T.yp[:], T.PF[:])], ["PF"], ["yp"])
+    for sm, val in sorted(cnt.items()):
+        g.wait_ge(T.sem[sm], val)

@@ -2,60 +2,55 @@ import numpy as np
 from concourse.mybir import AluOpType as A, ActivationFunctionType as F
 
 R, H, LO = 4, 128, 16
-NB1 = 0
-CH = 4
 BIG = float(2 ** 30)
 OFF = 65536.0
-FW, WW, XW = 18 * 256, 18 * 256, 4352
+FW, WW, XW = 17 * 256, 17 * 256 + 16, 4096 + 256
+SC = 4
+NG = 5
+KZ = 16
+ABS = (0, 0, 0, 0, 1, 1, 0, 0)
+PIECE = (4, 4, 4, 4, 2, 2, 2, 2)
+WAKE, FAR, FIT = 150, 2000, {"v": 250, "s": 350, "t": 100, "p": 0, "y": 0}
 
 SCRATCH = {
     "X": ("sbuf", [128, XW], "bfloat16"),
     "KI": ("sbuf", [128, 256], "int32"), "PI": ("sbuf", [128, 256], "int32"),
-    "KF": ("sbuf", [128, 256], "float32"), "PF": ("sbuf", [128, 256], "float32"),
-    "Y0": ("sbuf", [128, 2048], "bfloat16"), "D0": ("sbuf", [128, 2048], "bfloat16"), "R0": ("sbuf", [128, 2048], "bfloat16"),
-    "S1": ("sbuf", [128, 2048], "bfloat16"), "D1": ("sbuf", [128, 2048], "bfloat16"), "R1": ("sbuf", [128, 2048], "bfloat16"),
-    "A0": ("sbuf", [128, 2048], "bfloat16"), "A1": ("sbuf", [128, 2048], "bfloat16"), "M1": ("sbuf", [128, 2048], "bfloat16"),
-    "KM": ("sbuf", [128, 256], "float32"), "KC": ("sbuf", [128, 256], "float32"), "QM": ("sbuf", [128, 256], "float32"),
-    "KB": ("sbuf", [128, 256], "bfloat16"),
-    "LI": ("sbuf", [128, 256], "int32"), "LF": ("sbuf", [128, 336], "float32"),
-    "uf0": ("sbuf", [128, 8], "uint16"), "uf1": ("sbuf", [128, 8], "uint16"), "uk": ("sbuf", [128, 16], "uint16"),
-    "uu": ("sbuf", [128, 16], "uint16"), "uWV": ("sbuf", [128, 32], "uint16"), "uX": ("sbuf", [128, 16], "uint16"),
-    "XN0": ("sbuf", [128, 128], "bfloat16"), "XN1": ("sbuf", [128, 128], "bfloat16"), "SF1": ("sbuf", [128, 128], "bfloat16"),
-    "SK1": ("sbuf", [128, 128], "bfloat16"), "YK": ("sbuf", [128, 256], "bfloat16"), "AD": ("sbuf", [128, 256], "bfloat16"),
+    "Ku": ("sbuf", [128, 256], "uint16"), "Pu": ("sbuf", [128, 256], "uint16"),
+    "S": ("sbuf", [128, 4096], "bfloat16"), "D": ("sbuf", [128, 4096], "bfloat16"),
+    "RA": ("sbuf", [128, 4096], "bfloat16"), "NA": ("sbuf", [128, 4096], "bfloat16"),
+    "KM": ("sbuf", [128, 256], "float32"),
+    "LI": ("sbuf", [128, 256], "int32"), "LF": ("sbuf", [128, 256], "float32"), "LB": ("sbuf", [128, 128], "bfloat16"), "LU": ("sbuf", [128, 160], "uint16"),
+    "SF": ("sbuf", [128, 256], "bfloat16"), "DF": ("sbuf", [128, 256], "bfloat16"), "XT": ("sbuf", [128, 256], "bfloat16"),
+    "YK": ("sbuf", [128, 256], "bfloat16"), "AD": ("sbuf", [128, 256], "bfloat16"),
     "w2": ("sbuf", [128, 256], "bfloat16"), "wg": ("sbuf", [128, 256], "bfloat16"),
-    "pen": ("sbuf", [128, 256], "bfloat16"), "ts": ("sbuf", [128, 256], "bfloat16"), "tb": ("sbuf", [128, 256], "bfloat16"), "tm": ("sbuf", [128, 256], "bfloat16"),
-    "kp": ("sbuf", [128, 256], "int32"), "kq": ("sbuf", [128, 256], "int32"), "p1": ("sbuf", [128, 256], "int32"), "p2": ("sbuf", [128, 256], "int32"), "p3": ("sbuf", [128, 256], "int32"),
-    "KD": ("sbuf", [128, 256], "float32"), "K15": ("sbuf", [128, 256], "float32"), "BA": ("sbuf", [128, 256], "float32"), "KN": ("sbuf", [128, 256], "float32"),
+    "pen": ("sbuf", [128, 256], "bfloat16"), "ts": ("sbuf", [128, 256], "bfloat16"),
+    "kp": ("sbuf", [128, 256], "float32"), "p1": ("sbuf", [128, 256], "int32"), "p2": ("sbuf", [128, 256], "int32"),
+    "KD": ("sbuf", [128, 256], "float32"), "N0": ("sbuf", [128, 256], "float32"), "BA": ("sbuf", [128, 256], "float32"),
     "W": ("sbuf", [128, WW], "float32"), "FF": ("sbuf", [128, FW], "float32"), "kd": ("dram", [8, 17, 256], "float32"),
-    "VG": ("sbuf", [128, 256], "float32"), "RU": ("sbuf", [128, 256], "float32"), "Vu": ("sbuf", [128, 256], "uint16"),
-    "FD": ("sbuf", [128, 256], "bfloat16"), "EQ": ("sbuf", [128, 15 * 256], "bfloat16"), "SE": ("sbuf", [128, 256], "float32"),
-    "KJ": ("sbuf", [128, 256], "bfloat16"),
-    "ia": ("sbuf", [128, 256], "int32"), "ib": ("sbuf", [128, 256], "int32"), "ic": ("sbuf", [128, 256], "int32"), "idd": ("sbuf", [128, 256], "int32"),
-    "If": ("sbuf", [128, 128], "float32"), "Ib": ("sbuf", [128, 128], "bfloat16"), "In": ("sbuf", [128, 128], "bfloat16"),
-    "mf": ("sbuf", [128, 128], "float32"), "mb": ("sbuf", [128, 128], "bfloat16"), "OD": ("sbuf", [128, 256], "bfloat16"),
-    "B8f": ("sbuf", [128, 8], "float32"), "B8": ("sbuf", [128, 8], "bfloat16"), "B8n": ("sbuf", [128, 8], "bfloat16"), "B82": ("sbuf", [128, 8], "bfloat16"),
-    "WN": ("sbuf", [128, 8], "bfloat16"), "WR": ("sbuf", [128, 8], "bfloat16"), "WP": ("sbuf", [128, 8], "bfloat16"),
-    "BKf": ("sbuf", [128, 128], "float32"), "BKn": ("sbuf", [128, 128], "bfloat16"), "BK8": ("sbuf", [128, 128], "bfloat16"),
-    "L0": ("sbuf", [128, 128], "float32"), "L15": ("sbuf", [128, 128], "float32"), "LD": ("sbuf", [128, 128], "float32"),
-    "RS": ("sbuf", [128, 256], "float32"), "RN": ("sbuf", [128, 128], "bfloat16"), "RB": ("sbuf", [128, 128], "bfloat16"),
-    "NB": ("sbuf", [128, 128], "bfloat16"), "J4": ("sbuf", [128, 128], "bfloat16"), "Z": ("sbuf", [128, 512], "bfloat16"), "c15": ("sbuf", [128, 8], "bfloat16"),
-    "cb": ("sbuf", [128, 1], "float32"), "cy": ("sbuf", [128, 1], "float32"), "Hb": ("sbuf", [128, 128], "bfloat16"), "HH": ("sbuf", [128, 128], "bfloat16"),
-    "b0": ("psum", [128, 512], "float32"), "b1": ("psum", [128, 512], "float32"), "b2": ("psum", [128, 512], "float32"), "b3": ("psum", [128, 512], "float32"),
-    "b4": ("psum", [128, 512], "float32"), "b5": ("psum", [128, 512], "float32"), "b6": ("psum", [128, 512], "float32"), "b7": ("psum", [128, 512], "float32"),
+    "VG": ("sbuf", [128, 256], "float32"), "RU": ("sbuf", [128, 256], "float32"), "FD": ("sbuf", [128, 256], "bfloat16"),
+    "EQ": ("sbuf", [128, 2048], "bfloat16"), "SE": ("sbuf", [128, 256], "float32"),
+    "If": ("sbuf", [128, 128], "float32"), "I32": ("sbuf", [128, 128], "float32"), "Ib": ("sbuf", [128, 128], "bfloat16"), "I256": ("sbuf", [128, 128], "bfloat16"),
+    "ZF": ("sbuf", [128, 256], "float32"), "ZB": ("sbuf", [128, 256], "bfloat16"),
+    "OD": ("sbuf", [128, 256], "bfloat16"), "NL": ("sbuf", [128, 128], "bfloat16"), "EX": ("sbuf", [128, 2048], "bfloat16"),
+    "Q": ("sbuf", [128, 576], "bfloat16"), "BK": ("sbuf", [128, 128], "bfloat16"),
+    "L0": ("sbuf", [128, 128], "float32"), "L15": ("sbuf", [128, 128], "float32"), "L16": ("sbuf", [128, 128], "float32"), "LD": ("sbuf", [128, 128], "float32"),
+    "RS": ("sbuf", [128, 128], "float32"), "RC": ("sbuf", [128, 256], "float32"), "RN": ("sbuf", [128, 128], "bfloat16"),
+    "NB": ("sbuf", [128, 128], "bfloat16"), "J4": ("sbuf", [128, 128], "bfloat16"), "N23": ("sbuf", [128, 256], "bfloat16"),
 }
+for _i in range(8):
+    SCRATCH["b%d" % _i] = ("psum", [128, 512], "float32")
 SMALL = {}
-for _b, _l in (("LI", "q r sg a s2 a1 dl fs f k o1 o2 CL C16 Ai Am"), ("LF", "lt nk pr prb fx fx2 fm fm2 fo fo2 uy uz ow CW CK CU CF CF2 cnt Af thr")):
+for _b, _l in (("LI", "q r sg a s2 a1 dl fs f k o1 o2 C16 CK Ai Am"), ("LF", "klc av oV oN oM uy CL CW CU cnt thr cn cy junk"),
+               ("LB", "kl0 kl1 kl2 kl3 g1"), ("LU", "uf uk uu uV uN uK uY uP uX")):
     for _i, _n in enumerate(_l.split()):
-        SMALL[_n] = (_b, 16 * _i, 16 * _i + (1 if _n in ("Ai", "Am", "cnt", "Af", "thr") else 16))
-for _n, _a, _z in (("fk", "f", "k"), ("pp", "pr", "prb"), ("fxx", "fx", "fx2"), ("fmm", "fm", "fm2"), ("foo", "fo", "fo2"), ("CWK", "CW", "CK"), ("CFF", "CF", "CF2")):
-    SMALL[_n] = (SMALL[_a][0], SMALL[_a][1], SMALL[_z][2])
-for _n in ("K", "P"):
-    for _t in range(R):
-        SCRATCH["%sl%d" % (_n, _t)] = ("sbuf", [128, 256], "uint16")
-        if _t < R - 1:
-            SCRATCH["%so%d" % (_n, _t)] = ("sbuf", [128, 256], "uint16")
+        SMALL[_n] = (_b, 16 * _i, 16 * _i + (1 if _n in ("Ai", "Am", "cnt", "thr", "cn", "cy") else 16))
+for _t in range(R):
+    SCRATCH["Kl%d" % _t] = ("sbuf", [128, KZ + 256], "float32")
+    for _n in ("Pl", "Ko", "Po"):
+        SCRATCH["%s%d" % (_n, _t)] = ("sbuf", [128, 256], "float32")
 
-SEMAPHORES = ["v", "s", "t", "p", "ls", "dx", "dk", "dp", "dw", "dw2", "dkd", "df", "dy1", "dy2", "dy3"] + ["%sa%d" % (n, t) for n in "KP" for t in range(1, R)]
+SEMAPHORES = (["v", "s", "t", "p", "ls", "dx", "dk", "dp", "dz", "dw", "dw2", "dkd", "df", "dg", "dy0", "dy1", "dy2", "dy3"]
+              + ["%s%d" % (n, t) for n in ("Ka", "Kb", "Pa") for t in range(1, R)])
 
 
 def rank_program(g, core, T, topo):
@@ -110,67 +105,140 @@ def rank_program(g, core, T, topo):
                 old = [e for e in old if not (e[2] == q and e[3] == sm and e[0] >= lo and e[1] <= hi and (wr or not e[5]))]
                 recs[b] = old + [(lo, hi, q, sm, val, wr)]
 
-    def op(q, call, reads, writes):
-        sync(q, reads, writes)
-        cnt[q] = cnt.get(q, 0) + 1
-        call().then_inc(T.sem[q], 1)
-        note(q, reads, writes, q, cnt[q])
+    calls = []
 
-    def dmas(q, sm, pairs, reads, writes):
-        sync(q, reads, writes)
-        for out, in_ in pairs:
-            queues[q].dma_start(out, in_).then_inc(T.sem[sm], 16)
-            cnt[sm] = cnt.get(sm, 0) + 16
-        note(q, reads, writes, sm, cnt[sm])
+    def op(q, call, reads, writes, ns, kind=None):
+        def issue():
+            sync(q, reads, writes)
+            cnt[q] = cnt.get(q, 0) + 1
+            call().then_inc(T.sem[q], 1)
+            note(q, reads, writes, q, cnt[q])
+        calls.append((q, issue, reads, writes, ns, ns, kind))
+
+    def dmas(q, sm, pairs, reads, writes, kib):
+        def issue():
+            sync(q, reads, writes)
+            for out, in_ in pairs:
+                queues[q].dma_start(out, in_).then_inc(T.sem[sm], 16)
+                cnt[sm] = cnt.get(sm, 0) + 16
+            note(q, reads, writes, sm, cnt[sm])
+        ns = len(pairs) * (1000 if q == "p" else 300)
+        calls.append((q, issue, reads, writes, ns, ns + 1500 + 4 * kib, None))
+
+    def schedule():
+        n = len(calls)
+        pred, seen, closed, group = [set() for _ in range(n)], {}, {}, {}
+        for i, (q, _, reads, writes, _, _, kind) in enumerate(calls):
+            for accs, wr in ((reads, False), (writes, True)):
+                for x in accs:
+                    b, lo, hi = key(x)
+                    pred[i].update(j for l2, h2, w2, j in seen.get(b, ()) if (wr or w2) and l2 < hi and lo < h2 and j != i)
+                    if wr:
+                        seen[b] = [e for e in seen.get(b, ()) if not (lo <= e[0] and e[1] <= hi)]
+                        if kind and kind[0] and b in closed:
+                            pred[i].add(closed[b])
+                        if kind:
+                            group[b] = ([] if kind[0] else group[b]) + [i]
+                        if kind and kind[1]:
+                            closed[b] = i
+                            pred[i].update(group[b][:-1])
+                    seen.setdefault(b, []).append((lo, hi, wr, i))
+        succ = [[] for _ in range(n)]
+        for i in range(n):
+            for j in pred[i]:
+                succ[j].append(i)
+        banks = [[key(x)[0] for x in c[2] + c[3] if bank(key(x)[0])] for c in calls]
+        left, early, free, held = [len(p) for p in pred], [0.0] * n, {q: 0.0 for q in queues}, {}
+        ready = {q: [i for i in range(n) if calls[i][0] == q and not left[i]] for q in queues}
+
+        def start(i):
+            return max([early[i], free[calls[i][0]]] + [held[b][1] + WAKE for b in banks[i] if b in held and held[b][0] != calls[i][0]])
+        for _ in range(n):
+            best = None
+            for q in queues:
+                if ready[q]:
+                    at = {i: start(i) for i in ready[q]}
+                    i = min(ready[q])
+                    while True:
+                        fit = [j for j in ready[q] if j > i and at[j] < at[i] and at[j] + calls[j][4] <= at[i] + FIT[q]]
+                        if not fit:
+                            break
+                        i = min(fit)
+                    if best is None or at[i] < best[0]:
+                        best = (at[i], i)
+            t0, i = best
+            q = calls[i][0]
+            ready[q].remove(i)
+            free[q] = t0 + calls[i][4]
+            for b in banks[i]:
+                held[b] = (q, t0 + calls[i][5])
+            for j in succ[i]:
+                early[j] = max(early[j], t0 + calls[i][5] + (0 if q == calls[j][0] == "t" else WAKE))
+                left[j] -= 1
+                if not left[j]:
+                    ready[calls[j][0]].append(j)
+            calls[i][1]()
 
     V, S, E = g.vector, g.scalar, g.tensor
 
     def pa(x):
-        return x[3] if len(x) > 3 else T[x[0]][:, x[1]:x[2]]
+        return x[3][0] if len(x) > 3 else T[x[0]][:, x[1]:x[2]]
 
     def ks(*xs):
         return [x[:3] for x in xs if isinstance(x, tuple)] + [x[4] for x in xs if isinstance(x, tuple) and len(x) > 4]
 
-    def v_tt(o, a, b, f):
-        op("v", lambda: V.tensor_tensor(pa(o), pa(a), pa(b), f), ks(a, b), ks(o))
+    def ns(o, rate, *xs):
+        if any(len(x) > 4 for x in xs):
+            rate = 1.56
+        return 55 + 0.83 * rate * (o[3][1] if len(o) > 3 else o[2] - o[1])
+
+    def short(*xs):
+        return 0.5 if all(SCRATCH[x[0]][2] in ("bfloat16", "uint16") for x in xs) else 1
+
+    def v_tt(o, a, b, f, more=()):
+        op("v", lambda: V.tensor_tensor(pa(o), pa(a), pa(b), f), ks(a, b) + list(more), ks(o), ns(o, 1 if bank(a[0]) or bank(b[0]) else 2, a))
 
     def v_ts(o, a, x, f, y=None, f2=None):
         x1 = pa(x) if isinstance(x, tuple) else x
         if f2 is None:
-            op("v", lambda: V.tensor_scalar(pa(o), pa(a), x1, None, f), ks(a, x), ks(o))
+            op("v", lambda: V.tensor_scalar(pa(o), pa(a), x1, None, f), ks(a, x), ks(o), ns(o, short(o, a), a))
         else:
-            op("v", lambda: V.tensor_scalar(pa(o), pa(a), x1, y, f, f2), ks(a, x), ks(o))
+            op("v", lambda: V.tensor_scalar(pa(o), pa(a), x1, y, f, f2), ks(a, x), ks(o), ns(o, short(o, a), a))
 
     def v_cp(o, a):
-        op("v", lambda: V.tensor_copy(pa(o), pa(a)), ks(a), ks(o))
+        op("v", lambda: V.tensor_copy(pa(o), pa(a)), ks(a), ks(o), ns(o, short(o, a), a))
 
     def v_scan(o, d0, d1, init, f, f2):
-        op("v", lambda: V.tensor_tensor_scan(pa(o), pa(d0), pa(d1), init, f, f2), ks(d0, d1), ks(o))
+        op("v", lambda: V.tensor_tensor_scan(pa(o), pa(d0), pa(d1), init, f, f2), ks(d0, d1), ks(o), ns(o, short(o, d0, d1)))
 
     def v_ms(o, c):
-        op("v", lambda: V.memset(pa(o), c), [], ks(o))
+        op("v", lambda: V.memset(pa(o), c), [], ks(o), ns(o, short(o)))
 
-    def s_act(o, a, f):
-        op("s", lambda: S.activation(pa(o), pa(a), f), ks(a), ks(o))
+    def s_act(o, a, f, more=()):
+        op("s", lambda: S.activation(pa(o), pa(a), f), ks(a) + list(more), ks(o), ns(o, 1, a))
 
-    def s_mul(o, a, c):
-        op("s", lambda: S.activation(pa(o), pa(a), F.Copy, scale=c), ks(a), ks(o))
+    def s_sign(o, a, bias, scale):
+        op("s", lambda: S.activation(pa(o), pa(a), F.Sign, bias=pa(bias), scale=scale), ks(a, bias), ks(o), ns(o, 1))
 
     def mm(o, l, r, start, stop):
-        op("t", lambda: E.matmul(pa(o), pa(l), pa(r), start, stop), ks(l, r), ks(o))
+        n = max(64, o[3][1] if len(o) > 3 else o[2] - o[1]) * (4 if SCRATCH[l[0]][2] == "float32" else 1)
+        op("t", lambda: E.matmul(pa(o), pa(l), pa(r), start, stop), ks(l, r), ks(o), 0.42 * n, (start, stop))
 
     def iota(o, pattern, base, cm):
-        flag = {} if o[0] in ("ia", "ib", "ic", "idd", "LI") else {"allow_small_or_imprecise_dtypes": True}
-        op("p", lambda: g.iota(pa(o), pattern, base, cm, **flag), [], ks(o))
+        flag = {} if SCRATCH[o[0]][2] == "int32" else {"allow_small_or_imprecise_dtypes": True}
+        op("p", lambda: g.iota(pa(o), pattern, base, cm, **flag), [], ks(o), ns(o, 2) + 75)
 
-    def ind(w, lo, hi, u, c0, c1):
-        return (w, lo, hi, T[w][:, lo:hi].indirect(T[u][:, c0:c1]), (u, c0, c1))
+    def pick_of(o, src, pattern, how, fill, base_, cm):
+        op("p", lambda: g.affine_select(pa(o), pa(src), pattern, how, fill, base_, cm), ks(src), ks(o), ns(o, 2) + 115)
+
+    def ind(w, u):
+        return (w[0], w[1], w[2], (T[w[0]][:, w[1]:w[2]].indirect(T[u[0]][:, u[1]:u[2]]), 16 * (u[2] - u[1])), u[:3])
 
     def st(b, lo, hi, step):
-        return (b, lo, hi, T[b][:, lo:hi:step])
+        return (b, lo, hi, (T[b][:, lo:hi:step], len(range(lo, hi, step))))
 
     def rev(b, lo, hi):
-        return (b, lo, hi, T[b][:, hi - 1:lo - 1:-1] if lo else T[b][:, hi - 1::-1])
+        return (b, lo, hi, (T[b][:, hi - 1:lo - 1:-1] if lo else T[b][:, hi - 1::-1], hi - lo))
 
     def full(b):
         return SMALL[b] if b in SMALL else (b, 0, int(SCRATCH[b][1][-1]))
@@ -179,317 +247,324 @@ def rank_program(g, core, T, topo):
         x = full(b)
         return (x[0], x[1] + h * 8, x[1] + h * 8 + 8)
 
-    def half(b, h):
-        return (b, h * H, h * H + H)
+    def half(b, h, at=0):
+        return (b, at + h * H, at + h * H + H)
+
+    def wide(b, h, c=0, n=4):
+        return (b, 2048 * h + 512 * c, 2048 * h + 512 * (c + n))
 
     for t in range(1, R):
-        for n, src in (("K", prv), ("P", nxt)):
-            sm = "%sa%d" % (n, t)
-            cnt[sm] = len(topo.engines(src, core))
-            recs["%sl%d" % (n, t)] = [(0, 256, "r", sm, cnt[sm], True)]
-    dmas("y", "dp", [(T.PI[:], T.ph[:])], [], ["PI"])
-    dmas("y", "dk", [(T.KI[:], T.ka[:])], [], ["KI"])
-    dmas("y", "dx", [(T.X[:, 0:4096], T.x0[:])], [], [("X", 0, 4096)])
+        for sm, src, x in (("Ka", prv, half("Kl%d" % t, 0, KZ)), ("Kb", prv, half("Kl%d" % t, 1, KZ)), ("Pa", nxt, full("Pl%d" % t))):
+            cnt[sm + str(t)] = len(topo.engines(src, core))
+            recs.setdefault(x[0], []).append((x[1], x[2], "r", sm + str(t), cnt[sm + str(t)], True))
+    dmas("y", "dk", [(T.KI[:], T.ka[:])], [], ["KI"], 128)
+    dmas("y", "dp", [(T.PI[:], T.ph[:])], [], ["PI"], 256)
+    dmas("y", "dx", [(T.X[:, 0:4096], T.x0[:])], [], [("X", 0, 4096)], 1024)
 
-    iota(full("ia"), [[1, 256]], 256, -1)
-    iota(full("ib"), [[0, 256]], 0, 1)
-    iota(full("ic"), [[1, 256]], 0, 0)
+    ZF, ZB, FQ = ("ZF", 0, 128), ("ZB", 0, 128), FW // 4
+    v_ms(full("ZF"), 0.0)
+    v_ms(("W", 0, FQ), 0.0)
+    v_ms(full("ZB"), 0.0)
+    v_ms(full("Q"), 0.0)
+    iota(full("q"), [[0, 16]], 0, 1)
+    iota(full("o1"), [[128, 2], [2, 8]], 0, 0)
+    pick_of(full("If"), ZF, [[1, 128]], A.not_equal, 1.0, 0, -1)
+    pick_of(full("L16"), ZF, [[16, 8], [0, 16]], A.not_equal, 1.0, 15, -1)
+    pick_of(full("Ib"), ZB, [[1, 128]], A.not_equal, 1.0, 0, -1)
     iota(full("J4"), [[0, 8], [4096, 16]], 0, 0)
-    iota(full("CL"), [[16, 16]], 0, 0)
-    iota(("W", 0, 17 * 256), [[0, 17 * 256]], 0, 0)
-    iota(("W", 17 * 256, WW), [[1, 256]], 4096, 0)
-    iota(full("FF"), [[0, FW]], 0, 0)
-    v_ms(("X", 4096, XW), 0.0)
-    v_ms(full("Z"), 0.0)
+    for n, w in enumerate((-65536.0, 131072.0, -1.0, 65536.0)):
+        x = st("Q", 144 * n + 15, 144 * n + 144, 16)
+        pick_of(x, x, [[16, 9]], A.is_gt, w, 0, -1)
+    x = st("Q", 15, 576, 16)
+    pick_of(x, x, [[0, 4], [16, 9]], A.is_ge, 0.0, 15, -1)
+    iota(full("o2"), [[16, 16]], 0, 0)
+    iota(full("C16"), [[0, 2], [16, 8]], 0, 0)
+    iota(full("CK"), [[2048, 2], [16, 8]], 0, 0)
+    pick_of(full("RS"), ZF, [[0, 8], [1, 16]], A.not_equal, BIG, 0, 0)
+    pick_of(full("I32"), ZF, [[1, 128]], A.not_equal, 32.0, 0, -1)
+    for n in range(4):
+        s_act(("FF", n * FQ, n * FQ + FQ), ("W", 0, FQ), F.Copy)
+    s_act(("W", FQ, 2 * FQ), ("W", 0, FQ), F.Copy, ["FF"])
+    v_ts(full("a"), full("q"), 7, A.bitwise_and)
+    v_ts(full("r"), full("q"), 3, A.arith_shift_right, 1, A.bitwise_and)
+    v_ms(full("EX"), 0.0)
+    v_ts(full("a1"), full("a"), 16.0, A.mult)
+    v_tt(full("s2"), full("r"), full("o1"), A.add)
+    v_ts(full("k"), full("q"), 15, A.bitwise_and)
+    v_tt(full("dl"), full("a1"), full("s2"), A.add)
     v_ms(full("NB"), -864.0 * 65536)
-    v_ms(full("c15"), 15.0)
-    v_ms(("FD", 0, 1), 0.0)
-    v_ms(full("Af"), 0.0)
-    v_ms(full("thr"), 160.0 * 65536 - 1)
-    v_ms(full("KD"), 0.0)
-    v_ms(full("CF"), 16.0)
-    v_ms(full("CF2"), 17.0)
-    v_ms(full("cb"), -2000.5)
-    v_ms(full("cy"), -127.5)
-    v_ms(full("HH"), 0.5)
+    v_cp(full("uP"), full("dl"))
+    for t in range(R):
+        v_ms(("Kl%d" % t, 0, KZ), 0.0)
+    v_cp(full("Ku"), ind(full("KI"), full("uP")))
+    v_cp(full("Pu"), ind(full("PI"), full("uP")))
+    v_cp(("Kl0", KZ, KZ + 256), full("KI"))
+    v_tt(full("LD"), full("If"), full("L16"), A.subtract)
     v_cp(full("Pl0"), full("PI"))
-    v_cp(full("Kl0"), full("KI"))
-    dmas("y", "dkd", [(T.kd[:, 0:1, :], T.KD[0:8, 0:256])], ["KD"], ["kd0"])
-    v_ts(full("If"), ("ia", 0, 128), 256.0, A.is_equal)
-    s_act(full("Ib"), full("If"), F.Copy)
-    s_mul(full("In"), full("If"), -1.0)
-    s_mul(full("Hb"), full("If"), 0.5)
-    v_ts(full("idd"), full("ia"), 15, A.bitwise_and)
-    v_ts(full("mf"), ("idd", 0, 128), 0.0, A.is_equal)
-    s_act(full("mb"), full("mf"), F.Copy)
-    v_ts(full("OD"), full("idd"), 0.0, A.not_equal, OFF, A.mult)
-    v_ts(full("ia"), full("ib"), 4, A.arith_shift_right)
-    v_tt(full("B8f"), ("ia", 0, 8), ("ic", 0, 8), A.is_equal)
-    s_act(full("B8"), full("B8f"), F.Copy)
-    s_mul(full("WN"), full("B8f"), -65536.0)
-    s_mul(full("WP"), full("B8f"), 65536.0)
-    s_mul(full("WR"), full("B8f"), 131072.0)
-    s_mul(full("B8n"), full("B8f"), -1.0)
-    s_mul(full("B82"), full("B8f"), 2.0)
-    v_ts(full("idd"), full("ic"), 4, A.arith_shift_right)
-    v_tt(full("BKf"), ("ia", 0, 128), ("idd", 0, 128), A.is_equal)
-    s_mul(full("BK8"), full("BKf"), 8192.0)
-    v_ts(full("ic"), full("ic"), 15, A.bitwise_and)
-    v_ts(full("ib"), full("ib"), 15, A.bitwise_and)
-    v_ts(full("RS"), full("ic"), 0.0, A.is_equal, BIG, A.mult)
-    v_ts(full("RB"), ("ic", 0, 128), 0.0, A.is_equal, 1024.0, A.mult)
-    v_ts(full("RN"), full("RB"), -1.0, A.add)
-    v_ts(full("L0"), ("ic", 0, 128), 4.0 * NB1, A.is_ge, -1.0, A.mult)
-    v_tt(full("BKn"), full("L0"), full("BKf"), A.mult)
-    v_ts(full("L0"), ("ib", 0, 128), 0.0, A.is_equal)
-    v_tt(full("L0"), full("L0"), full("BKf"), A.mult)
-    v_ts(full("L15"), ("ib", 0, 128), 15.0, A.is_equal)
-    v_tt(full("L15"), full("L15"), full("BKf"), A.mult)
-    v_tt(full("LD"), full("If"), full("L15"), A.subtract)
-    v_ts(full("If"), ("ic", 0, 128), 0.0, A.not_equal)
-    v_tt(full("L15"), full("L15"), full("If"), A.mult)
-    v_tt(full("CL"), full("CL"), ("ib", 0, 16), A.add)
-    v_ts(full("C16"), full("CL"), 16.0, A.mult)
-    v_ts(h8("C16", 1), h8("C16", 1), -2048.0, A.add)
-    v_ts(full("CW"), full("CL"), 4096.0, A.add)
-    v_ts(full("CK"), full("CL"), 17 * 256.0, A.add)
-    v_ts(full("CU"), full("CL"), 256.0, A.add)
+    v_ms(("W", 2 * FQ, FW), 0.0)
+    dmas("y", "dz", [(T.kd[:, 0:1, :], T.ZF[0:8, 0:256])], ["ZF"], ["kz"], 8)
+    pick_of(full("EX"), full("EX"), [[1, 16], [16, 8], [0, 16]], A.not_equal, -1.0, 0, -1)
+    iota(("W", FW, WW), [[0, 16]], 8192, 0)
+    iota(full("N23"), [[0, 256]], -2 ** 23, 0)
+    iota(("X", 4096, XW), [[0, 256]], 0, 0)
+    iota(full("RC"), [[0, 256]], 0, 0)
+    pick_of(full("L0"), ZF, [[16, 8], [0, 16]], A.not_equal, 1.0, 0, -1)
+    pick_of(full("OD"), full("ZB"), [[0, 16], [1, 16]], A.not_equal, OFF, 0, -1)
+    pick_of(full("NL"), ZB, [[0, 8], [1, 16]], A.is_equal, 1.0, 0, -1)
+    pick_of(full("I256"), ZB, [[1, 128]], A.not_equal, 256.0, 0, -1)
+    pick_of(full("L15"), full("L16"), [[0, 8], [1, 16]], A.not_equal, 0.0, 0, 0)
+    pick_of(full("BK"), ZB, [[16, 8], [0, 16]], A.is_gt, 8192.0, 0, -1)
+    pick_of(full("BK"), full("BK"), [[16, 8], [0, 16]], A.is_ge, 0.0, 15, -1)
 
-    hb = ("b0", "b1")
-    KEY = [(hb[h], 0, 128) for h in range(2)]
-    ND = [(hb[h], 128, 256) for h in range(2)]
-    QT = [(hb[h], 264, 272) for h in range(2)]
-    KILL = [("b2", 0, 128), ("b2", 128, 256)]
-    XP = ("b2", 256, 384)
-    QL = [("b2", 384, 392), ("b2", 392, 400)]
-    VP, VE, ME = ("b3", 0, 256), ("b4", 0, 256), ("b5", 0, 256)
-    NEAR = ("b4", "b5", "b6", "b7")
+    def more_constants():
+        v_tt(full("o2"), full("o2"), full("k"), A.add)
+        v_ts(full("a"), full("k"), 128.0, A.mult)
+        v_ms(full("RN"), 0.125)
+        v_ms(("FD", 0, 1), 0.0)
+        v_ms(full("thr"), 160.0 * 65536 - 1)
+        v_tt(full("C16"), full("C16"), full("a"), A.add)
+        v_tt(full("CK"), full("CK"), full("a"), A.add)
+        v_ms(full("cn"), -1023.5)
+        v_ms(full("cy"), -127.5)
+        v_ts(st("RN", 0, 128, 16), ("ZB", 0, 8), 4.0, A.add)
+        v_ts(st("RC", 0, 256, 16), full("o2"), 4096.0, A.add)
+        v_ts(full("CL"), full("o2"), 1.0 / 256, A.mult)
+        v_ts(full("CW"), full("o2"), 1.0 / 256, A.mult, 16.0, A.add)
+        v_ts(full("CU"), full("o2"), 1.0 / 2048, A.mult, 1.0, A.add)
 
-    def strip(k, j):
-        return (k[0], k[1], k[2], T[k[0]][:, k[1] + j:k[2]:16])
+    KEY = [("b0", 0, 128), ("b1", 0, 128)]
+    ND = [("b1", 128, 256), ("b1", 256, 384)]
+    VP, CN = ("b0", 256, 512), ("b0", 128, 144)
+    NEAR = ("b2", "b3", "b4")
+    BP = [("b5", 0, 128), ("b5", 128, 256)]
+    XP = [("b5", 256, 384), ("b5", 384, 512)]
+    P32, ME, VE, SG = ("b6", 0, 256), ("b6", 256, 512), ("b7", 0, 256), ("b7", 256, 512)
 
-    def group(k, src, w, stop=False, step=16, js=range(LO)):
-        for j in js:
-            x = st(src, j, 2048, 16) if step == 16 else (src, j * 128, j * 128 + 128)
-            mm(strip(k, j), x, full(w), False, stop and j == js[-1])
+    def lanes(w, i):
+        n = 144 * ("QN", "QR", "Q1", "QP").index(w)
+        return ("Q", n + 15 - i, n + 143 - i)
+
+    def part(b, h, i):
+        return (b, 2048 * h + 128 * i, 2048 * h + 128 * i + 128)
+
+    def send(x, to, sm, dst):
+        rid, pid, _ = topo.addr(dst)
+
+        def issue():
+            sync("p", [x], [])
+            g.remote_dma(pa(to), pa(x), T.sem[sm], T.sem.ls, pid, rid, topo.mask(core, dst))
+            cnt["ls"] = cnt.get("ls", 0) + len(topo.engines(core, dst))
+        calls.append(("p", issue, [x], [to], 500, FAR + 4 * (x[2] - x[1]), None))
+
+    FK, WK = ["Fy", "Fg"], ["W0", "W16", "W"]
+    nb = [0]
+
+    def s_gather(h, c):
+        s_act(wide("S", h, c, 1), ind(("X", 0, 4096), ("Ku", 128 * h + 32 * c, 128 * h + 32 * c + 32)), F.Copy)
+
+    def d_gather(h, c, a, n):
+        lo = 128 * h + 32 * c + 8 * a
+        v_tt(("D", 16 * lo, 16 * lo + 128 * n), ind(("X", 0, 4096), ("Pu", lo, lo + 8 * n)), ("S", 16 * lo, 16 * lo + 128 * n), A.subtract)
 
     def bias(h):
         mm(KEY[h], full("Ib"), full("NB"), True, False)
         mm(KEY[h], full("Ib"), full("J4"), False, False)
 
-    def best(h):
-        v_scan(half("KM", h), ("RS", 0, 128), KEY[h], BIG, A.add, A.min)
-        v_scan(rev("KC", h * H, h * H + H), ("RS", 0, 128), rev("KM", h * H, h * H + H), BIG, A.add, A.min)
-        v_tt(half("QM", h), half("KC", h), full("mf"), A.mult)
-        op("s", lambda: S.activation(pa(half("KB", h)), pa(half("KC", h)), F.Sign, bias=T.cb[:], scale=-1.0), [half("KC", h), full("cb")], [half("KB", h)])
-
-    def best_t(h):
-        mm(QL[h], half("QM", h), full("B8f"), True, True)
-        mm(KILL[h], half("KB", h), full("Hb"), True, False)
-        mm(KILL[h], full("Ib"), full("HH"), False, True)
+    def keys(h, c, n, scalar):
+        if scalar:
+            s_act(wide("RA", h, c, n), wide("D", h, c, n), F.Abs)
+        else:
+            for i in range(4 * c, 4 * (c + n)):
+                mm(KEY[h], lanes("QN", i), part("D", h, i), False, False)
+            v_ts(wide("RA", h, c, n), wide("D", h, c, n), 0.0, A.max)
+        for i in range(4 * c, 4 * (c + n)):
+            mm(KEY[h], lanes("QP" if scalar else "QR", i), part("RA", h, i), False, False)
+            mm(KEY[h], lanes("Q1", i), part("D", h, i), False, i == LO - 1)
 
     def pick(h):
         q, r, sg, a, s2, a1, dl, fs, f, o1 = [h8(n, h) for n in ("q", "r", "sg", "a", "s2", "a1", "dl", "fs", "f", "o1")]
-        v_ts(q, QL[h], 2047.0, A.add)
-        v_ts(sg, q, 11, A.arith_shift_right, 1, A.bitwise_and)
-        v_ts(a, q, 16, A.arith_shift_right, 3, A.bitwise_and)
-        v_ts(s2, sg, 2.0, A.mult, -1.0, A.add)
-        v_ts(a1, a, 1.0, A.add)
-        v_ts(r, q, 12, A.arith_shift_right)
-        v_tt(dl, s2, a1, A.mult)
-        v_tt(fs, r, dl, A.add)
-        v_ts(f, fs, 15, A.bitwise_and)
-        v_tt(o1, f, h8("C16", h), A.add)
-        v_cp(full("uf%d" % h), o1)
+        return [[lambda: v_scan(half("KM", h), ("RS", 0, 128), KEY[h], BIG, A.add, A.min)],
+                [lambda: v_ts(q, st("KM", h * H + 15, h * H + H, 16), 2047.0, A.add)],
+                [lambda: v_ts(sg, q, 10, A.arith_shift_right, 2, A.bitwise_and), lambda: v_ts(a, q, 16, A.arith_shift_right, 3, A.bitwise_and),
+                 lambda: v_ts(r, q, 12, A.arith_shift_right)],
+                [lambda: v_ts(s2, sg, -1.0, A.add), lambda: v_ts(a1, a, 1.0, A.add)],
+                [lambda: v_tt(dl, s2, a1, A.mult)], [lambda: v_tt(fs, r, dl, A.add)], [lambda: v_ts(f, fs, 15, A.bitwise_and)],
+                [lambda: v_tt(o1, f, h8("C16", h), A.add)], [lambda: v_cp(h8("uf", h), o1)]]
 
-    def near_open(b):
-        mm((NEAR[b], 0, 512), full("Ib"), full("Z"), True, False)
+    def run(*steps):
+        for s_ in steps:
+            for c in s_:
+                c()
 
-    def near_load(b, srcs):
-        for i, src in enumerate(srcs):
-            for j in range(4):
-                mm((NEAR[b], j * 128, j * 128 + 128), full("Ib"), st(src, 4 * b + j, 2048, 16), False, False)
+    def x_n(h):
+        s_act(half("SF", h), ind(wide("S", h), h8("uf", h)), F.Copy)
+        s_act(half("DF", h), ind(wide("D", h), h8("uf", h)), F.Copy)
+        mm(XP[h], half("SF", h), full("Ib"), True, False)
+        mm(XP[h], half("DF", h), full("Ib"), False, True)
 
-    def near_diff(b, xn, out):
-        for j in range(4):
-            mm((NEAR[b], j * 128, j * 128 + 128), full("In"), full(xn), False, j == 3)
-        s_act((out, b * 512, b * 512 + 512), (NEAR[b], 0, 512), F.Abs)
+    def near(h):
+        s_act(half("XT", h), XP[h], F.Copy)
+        for c in range(4):
+            b = (NEAR[nb[0] % 3], 0, 512)
+            nb[0] += 1
+            mm(b, full("Ib"), wide("S", h, c, 1), True, False)
+            mm(b, half("XT", h), ("EX", 512 * c, 512 * c + 512), False, True)
+            s_act(wide("NA", h, c, 1), b, F.Abs)
+            for i in range(4 * c, 4 * c + 4):
+                mm(ND[h], lanes("Q1", i), part("NA", h, i), i == 0, False)
 
-    def penalty(h):
-        v_ts(half("pen", h), ND[h], 1024.0, A.is_ge, 16.0, A.mult)
-        v_scan(half("ts", h), full("RN"), half("pen", h), 1024.0, A.add, A.min)
-        v_scan(rev("tb", h * H, h * H + H), full("RB"), rev("ts", h * H, h * H + H), 1024.0, A.add, A.min)
-        v_tt(half("tm", h), half("tb", h), full("mb"), A.mult)
-        mm(QT[h], full("Ib"), full("c15"), True, False)
-        mm(QT[h], half("tm", h), full("B8"), False, True)
+    def new_arrays(t, h):
+        x = st(ND[h][0], ND[h][1], ND[h][2], 16)
+        mm(x, full("I256"), h8("kl%d" % t, h), False, False)
+        mm(x, full("I256"), h8("g1", h), False, True)
+        s_sign(half("pen", h), ND[h], full("cn"), -1.0)
+        mm(BP[h], full("L15"), half("Kl%d" % t, h, KZ), True, False)
+        mm(BP[h], full("If"), half("N0", h), False, True)
+        s_act(half("BA", h), BP[h], F.Copy)
+        ko = half("Ko%d" % t, h)
+        v_scan(rev("ts", h * H, h * H + H), full("RN"), rev("pen", h * H, h * H + H), 4.0, A.add, A.min)
+        v_tt(h8("uy", h), st("ts", h * H, h * H + H, 16), h8("CU", h), A.add)
+        v_ts(h8("uu", h), h8("uy", h), 2048.0, A.mult)
+        v_tt(ko, ind(full("FF"), h8("uu", h)), half("BA", h), A.add, FK)
+        if t < R - 1:
+            send(ko, half("Kl%d" % (t + 1), h, KZ), ("Ka", "Kb")[h] + str(t + 1), nxt)
+        else:
+            dmas("y", "dy%d" % h, [(T.yk[:, h * H:h * H + H], pa(ko))], [ko], ["yk%d" % h], 64)
 
-    def send(n, t, dst):
-        b, l, sm = "%so%d" % (n, t), "%sl%d" % (n, t + 1), "%sa%d" % (n, t + 1)
-        rid, pid, _ = topo.addr(dst)
-        sync("p", [full(b)], [])
-        g.remote_dma(T[l][:], T[b][:], T.sem[sm], T.sem.ls, pid, rid, topo.mask(core, dst))
-        cnt["ls"] = cnt.get("ls", 0) + len(topo.engines(core, dst))
+    def window(t):
+        kl = ("Kl%d" % t, KZ, KZ + 256)
+        mm(("b5", 0, 256), full("LD"), kl, True, True)
+        s_act(full("KD"), ("b5", 0, 256), F.Copy)
+        dmas("y", "dkd", [(T.kd[:, 1:17, :], T.KD[:])], ["KD"], ["kd"], 128)
+        dmas("y", "dw2", [(T.W[0::16, 4096:FW], T[kl[0]][0::16, kl[1]:kl[2]])], [kl, "W"], ["W16"], 8)
+        runs = [(T.FF[j::16, 0:(15 - j) * 256], T.kd[:, j + 1:16, :]) for j in range(1, 15)] + [(T.FF[:, 16 * 256:FW], T.kd[:, 0:16, :])]
+        dmas("y", "df", runs[NG:], ["kd", "kz", "FF"], ["Fy"], 500)
+        dmas("p", "dg", runs[:NG], ["kd", "FF"], ["Fg"], 500)
+
+    def names(t):
+        dmas("y", "dw", [(T.W[0::16, 0:4096], T["Pl%d" % t][:])], ["Pl%d" % t, "W"], ["W0"], 128)
+        mm(P32, full("I32"), full("Pl%d" % t), True, False)
+        mm(P32, full("Ib"), full("N23"), False, True)
+
+    def k_list(t, h):
+        v_cp(half("Ku", h), ind(half("Kl%d" % t, h, KZ), h8("uP", 0)))
+
+    def p_list(t):
+        v_cp(full("Pu"), ind(full("Pl%d" % t), full("uP")))
+
+    def phages(t):
+        po = full("Po%d" % t)
+
+        def out():
+            v_cp(po, full("p2"))
+            if t < R - 1:
+                send(po, full("Pl%d" % (t + 1)), "Pa%d" % (t + 1), prv)
+            else:
+                dmas("y", "dy2", [(T.yp[:], pa(po))], [po], ["yp"], 128)
+        return [[lambda: v_tt(full("kp"), ind(full("Kl%d" % t), full("uK")), full("Pl%d" % t), A.mult)],
+                [lambda: v_tt(full("p1"), full("kp"), P32, A.add)],
+                [lambda: v_ts(full("p2"), full("p1"), 5, A.arith_shift_right, 4095, A.bitwise_and)], [out]]
 
     def thresh(t):
-        if t:
-            v_tt(full("Af"), full("Af"), full("cnt"), A.add)
-            v_cp(full("Ai"), full("Af"))
-            v_ts(full("Am"), full("Ai"), 15, A.bitwise_and)
-            v_ts(full("thr"), full("Am"), 262144.0, A.mult, 160.0 * 65536 - 1, A.add)
+        for u in range(t):
+            mm(CN, full("BK"), full("kl%d" % u), u == 0, u == t - 1)
+        op("s", lambda: S.activation(pa(full("junk")), pa(CN), F.Copy, accum_out=pa(full("cnt"))), [CN], [full("junk"), full("cnt")], 200)
+        v_cp(full("Ai"), full("cnt"))
+        v_ts(full("Am"), full("Ai"), 15 << 18, A.bitwise_and)
+        v_ts(full("thr"), full("Am"), 160.0 * 65536 - 1, A.add)
 
-    FK = ["F%d" % j for j in range(1, 15)] + ["F17"]
-    recs.update({k: list(recs["FF"]) for k in FK})
-    recs.update({"W0": list(recs["W"]), "W16": list(recs["W"])})
-    WK = ["W0", "W16", "W"]
+    def w_gather(o, u):
+        s_act(full(o), ind(full("W"), full(u)), F.Copy, WK)
+
+    def scatter(c):
+        u, x = full("uX")[1] + SC * c, (16 * SC * c, 16 * SC * (c + 1))
+        xs = T.X[:, 0:XW].indirect(T.LU[:, u:u + SC])
+        op("v", lambda: V.tensor_tensor(xs, pa(("YK",) + x), pa(("wg",) + x), A.add), [("LU", u, u + SC), ("YK",) + x, ("wg",) + x], ["X"], 55 + 50 * SC)
+
+    def equals():
+        todo, at = [c for c in range(LO) if c % SC < SC - 1], 0
+        for c in todo:
+            lo, hi = 16 * c + 16, 16 * SC * (c // SC + 1)
+            v_ts(("EQ", at, at + hi - lo), (VP[0], VP[1] + lo, VP[1] + hi), ("RU", 16 * c + 15, 16 * c + 16), A.is_equal)
+            mm((ME[0], ME[1] + lo, ME[1] + hi), full("BK"), ("EQ", at, at + hi - lo), False, c == todo[-1])
+            at += hi - lo
+
+    def marked(x, stop):
+        mm(x, full("NL"), full("OD"), True, False)
+        mm(x, full("L0"), full("VG"), False, stop)
 
     for t in range(R):
-        Kl, Pl = "Kl%d" % t, "Pl%d" % t
-        last = t == R - 1
-
-        def own_names():
-            mm(VP, full("L0"), full("VG"), True, True)
-
-        def own_marks():
-            for x in (VE, ME):
-                mm(x, full("L0"), full("VG"), True, False)
-                mm(x, full("Ib"), full("OD"), False, x is VE)
-
-        def near_max():
-            for j in range(4 * NB1, LO):
-                v_tt(("M1", j * 128, j * 128 + 128), st("S1", j, 2048, 16), XP, A.max)
-                mm(strip(ND[1], j), ("M1", j * 128, j * 128 + 128), full("B82"), False, j == LO - 1)
-
-        def write_table():
-            v_scan(full("RU"), full("RS"), VE, BIG, A.add, A.min)
-            v_cp(full("Vu"), VP)
-            v_tt(("FD", 1, 256), ("b3", 1, 256), ("RU", 0, 255), A.is_equal)
-            mm(ME, full("BK8"), full("FD"), False, False)
-            for c in range(15):
-                lo = 16 * c + 16
-                v_ts(("EQ", c * 256 + lo, c * 256 + 256), ("Vu", lo, 256), ("RU", 16 * c + 15, 16 * c + 16), A.is_equal)
-                mm(("b5", lo, 256), full("BK8"), ("EQ", c * 256 + lo, c * 256 + 256), False, c == 14)
-            s_act(("YK", 0, 128), ind("Y0", 0, 2048, "uk", 0, 8), F.Copy)
-            s_act(("AD", 0, 128), ind("D0", 0, 2048, "uk", 0, 8), F.Abs)
-            s_act(full("SK1"), ind("S1", 0, 2048, "uk", 8, 16), F.Copy)
-            s_act(("AD", 128, 256), ind("D1", 0, 2048, "uk", 8, 16), F.Abs)
-            op("s", lambda: S.activation(T.KJ[:], T.b2[:, 0:256], F.Copy, accum_out=pa(full("cnt"))), [("b2", 0, 256)], [full("KJ"), full("cnt")])
-            v_tt(("YK", 128, 256), ind("D1", 0, 2048, "uk", 8, 16), full("SK1"), A.add)
-            v_ts(full("w2"), full("AD"), 32.0, A.is_le, -128.0, A.mult)
-            op("s", lambda: S.activation(T.b6[:, 0:256], T.YK[:], F.Sign, bias=T.cy[:]), [full("YK"), full("cy")], [("b6", 0, 256)])
-            v_tt(full("wg"), full("w2"), ("b6", 0, 256), A.mult)
-            v_scan(full("SE"), full("RS"), ME, BIG, A.add, A.min)
-            v_tt(full("ow"), st("SE", 15, 256, 16), full("CW"), A.min)
-            v_cp(full("uX"), full("ow"))
-            xs = T.X[:, 0:XW].indirect(T.uX[:, 0:16])
-            op("v", lambda: V.tensor_tensor(xs, T.YK[:], T.wg[:], A.add), [full("uX"), full("YK"), full("wg")], ["X"])
-
-        v_cp(full("PF"), full("PI") if t == 0 else full(Pl))
-        dmas("y", "dw", [(T.W[0::16, 0:4096], T.PF[:])], ["PF"], ["W0"])
-        n, l = 2048 // CH, 128 // CH
-        for c in range(CH):
-            s_act(("Y0", c * n, c * n + n), ind("X", 0, 4096, Pl, c * l, c * l + l), F.Copy)
-        v_cp(full("KF"), full("KI") if t == 0 else full(Kl))
-        bias(0)
-        mm(("b3", 0, 256), full("LD"), full("KF"), True, True)
-        bias(1)
-        mm(("b3", 256, 512), full("L15"), full("KF"), True, True)
-        for b in range(4):
-            near_open(b)
-        for c in range(CH):
-            v_tt(("D0", c * n, c * n + n), ind("X", 0, 4096, Kl, c * l, c * l + l), ("Y0", c * n, c * n + n), A.subtract)
-        s_act(full("KD"), ("b3", 0, 256), F.Copy)
-        for c in range(2):
-            s_act(("S1", c * 1024, c * 1024 + 1024), ind("X", 0, 4096, Kl, 128 + c * 64, 192 + c * 64), F.Copy)
-        s_act(full("K15"), ("b3", 256, 512), F.Copy)
-        dmas("y", "dkd", [(T.kd[:, 1:17, :], T.KD[:])], ["KD"], ["kd"])
-        dmas("y", "dw2", [(T.W[0::16, 4096:4352], T.KF[0::16, :])], ["KF"], ["W16"])
-        dmas("y", "df", [(T.FF[j::16, 256:(16 - j) * 256], T.kd[:, j + 1:16, :]) for j in range(1, 15)] + [(T.FF[:, 17 * 256:18 * 256], T.kd[:, 0:16, :])], ["kd", "kd0"], FK)
-        group(KEY[0], "D0", "WN")
-        v_ts(full("R0"), full("D0"), 0.0, A.max)
-        group(KEY[0], "R0", "WR")
-        group(KEY[0], "D0", "B8", stop=True)
-        for c in range(2):
-            v_tt(("D1", c * 1024, c * 1024 + 1024), ind("X", 0, 4096, Pl, 128 + c * 64, 192 + c * 64), ("S1", c * 1024, c * 1024 + 1024), A.subtract)
-        for c in range(2):
-            s_act(("R1", c * 1024, c * 1024 + 1024), ("D1", c * 1024, c * 1024 + 1024), F.Abs)
-        near_load(0, ("D0", "Y0"))
-        near_load(1, ("D0", "Y0"))
-        best(0)
-        best_t(0)
-        v_tt(full("kp"), full("KF"), full("PF"), A.mult)
-        group(KEY[1], "R1", "WP")
-        group(KEY[1], "D1", "B8n", stop=True)
-        pick(0)
-        s_act(full("XN0"), ind("Y0", 0, 2048, "uf0", 0, 8), F.Copy)
-        best(1)
-        near_diff(0, "XN0", "A0")
-        best_t(1)
-        v_ts(full("kq"), full("kp"), 5, A.arith_shift_right)
-        thresh(t)
-        pick(1)
-        near_diff(1, "XN0", "A0")
-        s_act(full("SF1"), ind("S1", 0, 2048, "uf1", 0, 8), F.Copy)
-        for b in range(2, 4):
-            near_load(b, ("D0", "Y0"))
-            near_diff(b, "XN0", "A0")
-        v_tt(full("p1"), full("kq"), ("b2", 0, 256), A.mult)
-        v_tt(full("XN1"), ind("D1", 0, 2048, "uf1", 0, 8), full("SF1"), A.add)
-        mm(XP, full("Ib"), full("XN1"), True, True)
-        mm(ND[1], full("XN1"), full("BKn"), True, False)
-        for b in range(NB1):
-            near_open(b)
-            near_load(b, ("S1",))
-            near_diff(b, "XN1", "A1")
-        group(ND[1], "S1", "B8n", js=range(4 * NB1, LO))
-        mm(ND[0], full("Ib"), ("Z", 0, 128), True, False)
-        v_tt(full("p2"), full("p1"), full("PF"), A.add)
-        v_ts(full("p3"), full("p2"), 4095, A.bitwise_and)
-        if not last:
-            v_cp(full("Po%d" % t), full("p3"))
-            send("P", t, prv)
-        v_ts(full("nk"), full("q"), 47.0, A.is_ge)
-        v_ts(full("lt"), full("q"), full("thr"), A.is_lt, 256.0, A.mult)
-        v_ts(full("k"), full("r"), 15, A.bitwise_and)
-        v_tt(full("pr"), full("nk"), full("lt"), A.mult)
-        v_tt(full("prb"), full("nk"), full("lt"), A.mult)
-        v_tt(full("fxx"), full("fk"), full("CFF"), A.subtract)
-        v_tt(full("o2"), full("k"), full("C16"), A.add)
-        v_tt(full("fmm"), full("fxx"), full("pp"), A.mult)
-        v_cp(full("uk"), full("o2"))
-        v_tt(full("foo"), full("fmm"), full("CWK"), A.add)
-        v_cp(full("uWV"), full("foo"))
-        vw = ind("W", 0, WW, "uWV", 16, 32)
-        op("s", lambda: S.activation(T.VG[:], vw[3], F.Copy), WK + [full("uWV")], ["VG"])
-        if last:
-            own_names()
-            own_marks()
-        group(ND[0], "A0", "B8", stop=True, step=1)
-        group(ND[1], "A1", "B8", step=1, js=range(4 * NB1))
-        near_max()
-        if last:
-            write_table()
-            dmas("y", "dy3", [(T.yx[:], T.X[:, 0:4096])], ["X"], ["yx"])
-        penalty(0)
-        if not last:
-            own_names()
-        bw = ind("W", 0, WW, "uWV", 0, 16)
-        op("v", lambda: V.tensor_tensor(T.BA[:], bw[3], T.K15[:], A.add), WK + [full("uWV"), full("K15")], ["BA"])
-        penalty(1)
-        if not last:
-            own_marks()
+        kl, last = full("kl%d" % t), t == R - 1
+        p0, p1, ph = pick(0), pick(1), phages(t)
+        if t:
+            k_list(t, 0)
+            p_list(t)
+            k_list(t, 1)
         for h in range(2):
-            v_tt(h8("uy", h), QT[h], h8("pr", h), A.mult)
-            v_tt(h8("uz", h), h8("uy", h), h8("CU", h), A.add)
-        v_cp(full("uu"), full("uz"))
-        fw = ind("FF", 0, FW, "uu", 0, 16)
-        op("v", lambda: V.tensor_tensor(T.KN[:], fw[3], T.BA[:], A.add), FK + ["FF", full("uu"), full("BA")], [full("KN")])
+            bias(h)
+            for c in range(4):
+                s_gather(h, c)
+                for a in range(0, 4, PIECE[4 * h + c]):
+                    d_gather(h, c, a, PIECE[4 * h + c])
+                keys(h, c, 1, ABS[4 * h + c])
+            if h == 0:
+                window(t)
+                if t == 0:
+                    more_constants()
+                run(*p0)
+                x_n(0)
+                near(0)
+                if t:
+                    thresh(t)
+                names(t)
+        run(*p1[:3])
+        v_ts(kl, full("q"), 0.0, A.is_lt, 32.0, A.mult)
+        v_ts(full("g1"), full("q"), full("thr"), A.is_ge, 32.0, A.mult)
+        v_tt(full("klc"), kl, full("CL"), A.add)
+        v_ts(full("k"), full("r"), 15, A.bitwise_and)
+        v_tt(full("av"), full("klc"), full("g1"), A.add)
+        v_tt(full("oV"), full("k"), full("av"), A.add)
+        v_ts(full("uV"), full("oV"), 17.0, A.min, 256.0, A.mult)
+        w_gather("VG", "uV")
+        marked(VE, True)
+        mm(VP, full("L0"), full("VG"), True, True)
+        v_scan(full("RU"), full("RC"), VE, 0.0, A.max, A.min)
+        v_cp(full("uY"), st("RU", 15, 256, 16))
+        run(*p1[3:])
+        v_tt(full("oN"), full("f"), full("av"), A.add)
+        v_tt(full("oM"), full("oN"), full("CW"), A.min)
+        v_ts(full("uN"), full("oM"), 256.0, A.mult)
         if not last:
-            v_cp(full("Ko%d" % t), full("KN"))
-            send("K", t, nxt)
-            write_table()
-        else:
-            dmas("y", "dy1", [(T.yk[:], T.KN[:])], ["KN"], ["yk"])
-            v_cp(full("PF"), full("p3"))
-            dmas("y", "dy2", [(T.yp[:], T.PF[:])], ["PF"], ["yp"])
+            w_gather("N0", "uN")
+            new_arrays(t, 0)
+            x_n(1)
+        v_tt(full("o2"), full("k"), full("CK"), A.add)
+        v_cp(full("uk"), full("o2"))
+        v_ts(full("uK"), full("klc"), KZ / 256.0 - 32.0, A.add, 256.0, A.mult)
+        run(ph[0], ph[1])
+        marked(ME, False)
+        v_tt(("FD", 1, 256), (VP[0], VP[1] + 1, VP[2]), ("RU", 0, 255), A.is_equal)
+        mm(ME, full("BK"), full("FD"), False, False)
+        if not last:
+            run(ph[2], ph[3])
+        equals()
+        s_act(full("YK"), ind(full("X"), full("uY")), F.Copy)
+        s_sign(SG, full("YK"), full("cy"), 1.0)
+        s_act(full("AD"), ind(full("D"), full("uk")), F.Abs)
+        v_scan(full("SE"), full("RC"), ME, 0.0, A.max, A.min)
+        v_cp(full("uX"), st("SE", 15, 256, 16))
+        v_ts(full("w2"), full("AD"), 32.0, A.is_le, -128.0, A.mult)
+        v_tt(full("wg"), full("w2"), SG, A.mult)
+        for c in range(LO // SC - 1, -1, -1):
+            scatter(c)
+        if last:
+            dmas("y", "dy3", [(T.yx[:], T.X[:, 0:4096])], ["X"], ["yx"], 1024)
+            w_gather("N0", "uN")
+            x_n(1)
+            new_arrays(t, 0)
+            run(ph[2], ph[3])
+        near(1)
+        new_arrays(t, 1)
+    schedule()
     for sm, val in sorted(cnt.items()):
         g.wait_ge(T.sem[sm], val)

@@ -8,9 +8,11 @@ FW, WW, XW = 17 * 256, 17 * 256 + 16, 4096 + 256
 SC = 4
 NG = 5
 KZ = 16
-ABS = (0, 0, 0, 0, 1, 1, 0, 0)
+ABS = (0, 0, 0, 0, 1, 1, 1, 0)
 PIECE = (4, 4, 4, 4, 2, 2, 2, 2)
-WAKE, FAR, FIT = 150, 2000, {"v": 250, "s": 350, "t": 100, "p": 0, "y": 0}
+NE = 2
+WAKE, FAR, FIT = 175, 2000, {"v": 250, "s": 200, "t": 200, "p": 0, "y": 0}
+DY, DG, DL = 150, 1000, 1200
 
 SCRATCH = {
     "X": ("sbuf", [128, XW], "bfloat16"),
@@ -25,14 +27,14 @@ SCRATCH = {
     "w2": ("sbuf", [128, 256], "bfloat16"), "wg": ("sbuf", [128, 256], "bfloat16"),
     "pen": ("sbuf", [128, 256], "bfloat16"), "ts": ("sbuf", [128, 256], "bfloat16"),
     "kp": ("sbuf", [128, 256], "float32"), "p1": ("sbuf", [128, 256], "int32"), "p2": ("sbuf", [128, 256], "int32"),
-    "KD": ("sbuf", [128, 256], "float32"), "N0": ("sbuf", [128, 256], "float32"), "BA": ("sbuf", [128, 256], "float32"),
+    "KD": ("sbuf", [128, 256], "float32"), "K15": ("sbuf", [128, 256], "float32"), "BA": ("sbuf", [128, 256], "float32"),
     "W": ("sbuf", [128, WW], "float32"), "FF": ("sbuf", [128, FW], "float32"), "kd": ("dram", [8, 17, 256], "float32"),
-    "VG": ("sbuf", [128, 256], "float32"), "RU": ("sbuf", [128, 256], "float32"), "FD": ("sbuf", [128, 256], "bfloat16"),
+    "VG": ("sbuf", [128, 256], "float16"), "L0h": ("sbuf", [128, 128], "float16"), "RU": ("sbuf", [128, 256], "float32"), "FD": ("sbuf", [128, 256], "bfloat16"),
     "EQ": ("sbuf", [128, 2048], "bfloat16"), "SE": ("sbuf", [128, 256], "float32"),
     "If": ("sbuf", [128, 128], "float32"), "I32": ("sbuf", [128, 128], "float32"), "Ib": ("sbuf", [128, 128], "bfloat16"), "I256": ("sbuf", [128, 128], "bfloat16"),
     "ZF": ("sbuf", [128, 256], "float32"), "ZB": ("sbuf", [128, 256], "bfloat16"),
     "OD": ("sbuf", [128, 256], "bfloat16"), "NL": ("sbuf", [128, 128], "bfloat16"), "EX": ("sbuf", [128, 2048], "bfloat16"),
-    "Q": ("sbuf", [128, 576], "bfloat16"), "BK": ("sbuf", [128, 128], "bfloat16"),
+    "Q": ("sbuf", [128, 720], "bfloat16"), "BK": ("sbuf", [128, 128], "bfloat16"),
     "L0": ("sbuf", [128, 128], "float32"), "L15": ("sbuf", [128, 128], "float32"), "L16": ("sbuf", [128, 128], "float32"), "LD": ("sbuf", [128, 128], "float32"),
     "RS": ("sbuf", [128, 128], "float32"), "RC": ("sbuf", [128, 256], "float32"), "RN": ("sbuf", [128, 128], "bfloat16"),
     "NB": ("sbuf", [128, 128], "bfloat16"), "J4": ("sbuf", [128, 128], "bfloat16"), "N23": ("sbuf", [128, 256], "bfloat16"),
@@ -40,17 +42,17 @@ SCRATCH = {
 for _i in range(8):
     SCRATCH["b%d" % _i] = ("psum", [128, 512], "float32")
 SMALL = {}
-for _b, _l in (("LI", "q r sg a s2 a1 dl fs f k o1 o2 C16 CK Ai Am"), ("LF", "klc av oV oN oM uy CL CW CU cnt thr cn cy junk"),
+for _b, _l in (("LI", "q r sg a s2 a1 dl fs f k o1 o2 C16 CK Ai Am"), ("LF", "klc av oV oN oM uy CL CW CU cnt thr cn cy junk k2"),
                ("LB", "kl0 kl1 kl2 kl3 g1"), ("LU", "uf uk uu uV uN uK uY uP uX")):
     for _i, _n in enumerate(_l.split()):
         SMALL[_n] = (_b, 16 * _i, 16 * _i + (1 if _n in ("Ai", "Am", "cnt", "thr", "cn", "cy") else 16))
 for _t in range(R):
-    SCRATCH["Kl%d" % _t] = ("sbuf", [128, KZ + 256], "float32")
+    SCRATCH["Kl%d" % _t] = ("sbuf", [128, 2 * KZ + 256], "float32")
     for _n in ("Pl", "Ko", "Po"):
         SCRATCH["%s%d" % (_n, _t)] = ("sbuf", [128, 256], "float32")
 
 SEMAPHORES = (["v", "s", "t", "p", "ls", "dx", "dk", "dp", "dz", "dw", "dw2", "dkd", "df", "dg", "dy0", "dy1", "dy2", "dy3"]
-              + ["%s%d" % (n, t) for n in ("Ka", "Kb", "Pa") for t in range(1, R)])
+              + ["%s%d" % (n, t) for n in ("Ka", "Kb", "Pa", "Pb") for t in range(1, R)])
 
 
 def rank_program(g, core, T, topo):
@@ -122,8 +124,8 @@ def rank_program(g, core, T, topo):
                 queues[q].dma_start(out, in_).then_inc(T.sem[sm], 16)
                 cnt[sm] = cnt.get(sm, 0) + 16
             note(q, reads, writes, sm, cnt[sm])
-        ns = len(pairs) * (1000 if q == "p" else 300)
-        calls.append((q, issue, reads, writes, ns, ns + 1500 + 4 * kib, None))
+        ns = len(pairs) * (DG if q == "p" else DY)
+        calls.append((q, issue, reads, writes, ns, ns + DL + 3 * kib, None))
 
     def schedule():
         n = len(calls)
@@ -189,8 +191,8 @@ def rank_program(g, core, T, topo):
 
     def ns(o, rate, *xs):
         if any(len(x) > 4 for x in xs):
-            rate = 1.56
-        return 55 + 0.83 * rate * (o[3][1] if len(o) > 3 else o[2] - o[1])
+            return 55 + 0.83 * 1.56 * (o[2] - o[1])
+        return 0.83 * max(64, rate * (o[3][1] if len(o) > 3 else o[2] - o[1]))
 
     def short(*xs):
         return 0.5 if all(SCRATCH[x[0]][2] in ("bfloat16", "uint16") for x in xs) else 1
@@ -215,10 +217,10 @@ def rank_program(g, core, T, topo):
         op("v", lambda: V.memset(pa(o), c), [], ks(o), ns(o, short(o)))
 
     def s_act(o, a, f, more=()):
-        op("s", lambda: S.activation(pa(o), pa(a), f), ks(a) + list(more), ks(o), ns(o, 1, a))
+        op("s", lambda: S.activation(pa(o), pa(a), f), ks(a) + list(more), ks(o), ns(o, 1, a) + (10 if len(a) > 4 else 60))
 
     def s_sign(o, a, bias, scale):
-        op("s", lambda: S.activation(pa(o), pa(a), F.Sign, bias=pa(bias), scale=scale), ks(a, bias), ks(o), ns(o, 1))
+        op("s", lambda: S.activation(pa(o), pa(a), F.Sign, bias=pa(bias), scale=scale), ks(a, bias), ks(o), ns(o, 1) + 60)
 
     def mm(o, l, r, start, stop):
         n = max(64, o[3][1] if len(o) > 3 else o[2] - o[1]) * (4 if SCRATCH[l[0]][2] == "float32" else 1)
@@ -254,7 +256,8 @@ def rank_program(g, core, T, topo):
         return (b, 2048 * h + 512 * c, 2048 * h + 512 * (c + n))
 
     for t in range(1, R):
-        for sm, src, x in (("Ka", prv, half("Kl%d" % t, 0, KZ)), ("Kb", prv, half("Kl%d" % t, 1, KZ)), ("Pa", nxt, full("Pl%d" % t))):
+        for sm, src, x in (("Ka", prv, half("Kl%d" % t, 0, KZ)), ("Kb", prv, half("Kl%d" % t, 1, 2 * KZ)),
+                           ("Pa", nxt, half("Pl%d" % t, 0)), ("Pb", nxt, half("Pl%d" % t, 1))):
             cnt[sm + str(t)] = len(topo.engines(src, core))
             recs.setdefault(x[0], []).append((x[1], x[2], "r", sm + str(t), cnt[sm + str(t)], True))
     dmas("y", "dk", [(T.KI[:], T.ka[:])], [], ["KI"], 128)
@@ -272,11 +275,11 @@ def rank_program(g, core, T, topo):
     pick_of(full("L16"), ZF, [[16, 8], [0, 16]], A.not_equal, 1.0, 15, -1)
     pick_of(full("Ib"), ZB, [[1, 128]], A.not_equal, 1.0, 0, -1)
     iota(full("J4"), [[0, 8], [4096, 16]], 0, 0)
-    for n, w in enumerate((-65536.0, 131072.0, -1.0, 65536.0)):
+    for n, w in enumerate((-65536.0, 131072.0, -1.0, 65536.0, 1.0)):
         x = st("Q", 144 * n + 15, 144 * n + 144, 16)
         pick_of(x, x, [[16, 9]], A.is_gt, w, 0, -1)
-    x = st("Q", 15, 576, 16)
-    pick_of(x, x, [[0, 4], [16, 9]], A.is_ge, 0.0, 15, -1)
+    x = st("Q", 15, 720, 16)
+    pick_of(x, x, [[0, 5], [16, 9]], A.is_ge, 0.0, 15, -1)
     iota(full("o2"), [[16, 16]], 0, 0)
     iota(full("C16"), [[0, 2], [16, 8]], 0, 0)
     iota(full("CK"), [[2048, 2], [16, 8]], 0, 0)
@@ -296,9 +299,11 @@ def rank_program(g, core, T, topo):
     v_cp(full("uP"), full("dl"))
     for t in range(R):
         v_ms(("Kl%d" % t, 0, KZ), 0.0)
+        v_ms(("Kl%d" % t, KZ + H, 2 * KZ + H), 0.0)
     v_cp(full("Ku"), ind(full("KI"), full("uP")))
     v_cp(full("Pu"), ind(full("PI"), full("uP")))
-    v_cp(("Kl0", KZ, KZ + 256), full("KI"))
+    v_cp(half("Kl0", 0, KZ), half("KI", 0))
+    v_cp(half("Kl0", 1, 2 * KZ), half("KI", 1))
     v_tt(full("LD"), full("If"), full("L16"), A.subtract)
     v_cp(full("Pl0"), full("PI"))
     v_ms(("W", 2 * FQ, FW), 0.0)
@@ -307,7 +312,7 @@ def rank_program(g, core, T, topo):
     iota(("W", FW, WW), [[0, 16]], 8192, 0)
     iota(full("N23"), [[0, 256]], -2 ** 23, 0)
     iota(("X", 4096, XW), [[0, 256]], 0, 0)
-    iota(full("RC"), [[0, 256]], 0, 0)
+    iota(full("RC"), [[0, 256]], -4096, 0)
     pick_of(full("L0"), ZF, [[16, 8], [0, 16]], A.not_equal, 1.0, 0, -1)
     pick_of(full("OD"), full("ZB"), [[0, 16], [1, 16]], A.not_equal, OFF, 0, -1)
     pick_of(full("NL"), ZB, [[0, 8], [1, 16]], A.is_equal, 1.0, 0, -1)
@@ -327,7 +332,8 @@ def rank_program(g, core, T, topo):
         v_ms(full("cn"), -1023.5)
         v_ms(full("cy"), -127.5)
         v_ts(st("RN", 0, 128, 16), ("ZB", 0, 8), 4.0, A.add)
-        v_ts(st("RC", 0, 256, 16), full("o2"), 4096.0, A.add)
+        v_ts(st("RC", 0, 256, 16), full("o2"), 2048.0, A.add)
+        v_cp(full("L0h"), full("L0"))
         v_ts(full("CL"), full("o2"), 1.0 / 256, A.mult)
         v_ts(full("CW"), full("o2"), 1.0 / 256, A.mult, 16.0, A.add)
         v_ts(full("CU"), full("o2"), 1.0 / 2048, A.mult, 1.0, A.add)
@@ -335,13 +341,13 @@ def rank_program(g, core, T, topo):
     KEY = [("b0", 0, 128), ("b1", 0, 128)]
     ND = [("b1", 128, 256), ("b1", 256, 384)]
     VP, CN = ("b0", 256, 512), ("b0", 128, 144)
-    NEAR = ("b2", "b3", "b4")
-    BP = [("b5", 0, 128), ("b5", 128, 256)]
+    NEAR = ("b2", "b3", "b4", "b6")
+    LP = [("b5", 0, 128), ("b5", 128, 256)]
     XP = [("b5", 256, 384), ("b5", 384, 512)]
-    P32, ME, VE, SG = ("b6", 0, 256), ("b6", 256, 512), ("b7", 0, 256), ("b7", 256, 512)
+    P32, ME, VE, SG = ("b5", 0, 256), ("b7", 256, 512), ("b7", 0, 256), ("b5", 0, 256)
 
     def lanes(w, i):
-        n = 144 * ("QN", "QR", "Q1", "QP").index(w)
+        n = 144 * ("QN", "QR", "Q1", "QP", "Q2").index(w)
         return ("Q", n + 15 - i, n + 143 - i)
 
     def part(b, h, i):
@@ -360,26 +366,27 @@ def rank_program(g, core, T, topo):
     nb = [0]
 
     def s_gather(h, c):
-        s_act(wide("S", h, c, 1), ind(("X", 0, 4096), ("Ku", 128 * h + 32 * c, 128 * h + 32 * c + 32)), F.Copy)
+        s_act(wide("S", h, c, 1), ind(("X", 0, 4096), (("Ku", "Pu")[h], 128 * h + 32 * c, 128 * h + 32 * c + 32)), F.Copy)
 
     def d_gather(h, c, a, n):
         lo = 128 * h + 32 * c + 8 * a
-        v_tt(("D", 16 * lo, 16 * lo + 128 * n), ind(("X", 0, 4096), ("Pu", lo, lo + 8 * n)), ("S", 16 * lo, 16 * lo + 128 * n), A.subtract)
+        v_tt(("D", 16 * lo, 16 * lo + 128 * n), ind(("X", 0, 4096), (("Pu", "Ku")[h], lo, lo + 8 * n)), ("S", 16 * lo, 16 * lo + 128 * n), A.subtract)
 
     def bias(h):
         mm(KEY[h], full("Ib"), full("NB"), True, False)
         mm(KEY[h], full("Ib"), full("J4"), False, False)
 
-    def keys(h, c, n, scalar):
+    def keys(h, i0, n, scalar):
+        d, ra = [(b, 2048 * h + 128 * i0, 2048 * h + 128 * (i0 + n)) for b in ("D", "RA")]
         if scalar:
-            s_act(wide("RA", h, c, n), wide("D", h, c, n), F.Abs)
+            s_act(ra, d, F.Abs)
         else:
-            for i in range(4 * c, 4 * (c + n)):
+            for i in range(i0, i0 + n):
                 mm(KEY[h], lanes("QN", i), part("D", h, i), False, False)
-            v_ts(wide("RA", h, c, n), wide("D", h, c, n), 0.0, A.max)
-        for i in range(4 * c, 4 * (c + n)):
+            v_ts(ra, d, 0.0, A.max)
+        for i in range(i0, i0 + n):
             mm(KEY[h], lanes("QP" if scalar else "QR", i), part("RA", h, i), False, False)
-            mm(KEY[h], lanes("Q1", i), part("D", h, i), False, i == LO - 1)
+            mm(KEY[h], lanes(("Q1", "Q2")[h], i), part("D", h, i), False, i == LO - 1)
 
     def pick(h):
         q, r, sg, a, s2, a1, dl, fs, f, o1 = [h8(n, h) for n in ("q", "r", "sg", "a", "s2", "a1", "dl", "fs", "f", "o1")]
@@ -398,16 +405,19 @@ def rank_program(g, core, T, topo):
 
     def x_n(h):
         s_act(half("SF", h), ind(wide("S", h), h8("uf", h)), F.Copy)
-        s_act(half("DF", h), ind(wide("D", h), h8("uf", h)), F.Copy)
-        mm(XP[h], half("SF", h), full("Ib"), True, False)
-        mm(XP[h], half("DF", h), full("Ib"), False, True)
-
-    def near(h):
+        mm(XP[h], half("SF", h), full("Ib"), True, h == 1)
+        if h == 0:
+            s_act(half("DF", h), ind(wide("D", h), h8("uf", h)), F.Copy)
+            mm(XP[h], half("DF", h), full("Ib"), False, True)
         s_act(half("XT", h), XP[h], F.Copy)
-        for c in range(4):
-            b = (NEAR[nb[0] % 3], 0, 512)
+
+    def near(h, cs):
+        for c in cs:
+            b = (NEAR[nb[0] % 4], 0, 512)
             nb[0] += 1
             mm(b, full("Ib"), wide("S", h, c, 1), True, False)
+            if h:
+                mm(b, full("Ib"), wide("D", h, c, 1), False, False)
             mm(b, half("XT", h), ("EX", 512 * c, 512 * c + 512), False, True)
             s_act(wide("NA", h, c, 1), b, F.Abs)
             for i in range(4 * c, 4 * c + 4):
@@ -418,52 +428,59 @@ def rank_program(g, core, T, topo):
         mm(x, full("I256"), h8("kl%d" % t, h), False, False)
         mm(x, full("I256"), h8("g1", h), False, True)
         s_sign(half("pen", h), ND[h], full("cn"), -1.0)
-        mm(BP[h], full("L15"), half("Kl%d" % t, h, KZ), True, False)
-        mm(BP[h], full("If"), half("N0", h), False, True)
-        s_act(half("BA", h), BP[h], F.Copy)
         ko = half("Ko%d" % t, h)
         v_scan(rev("ts", h * H, h * H + H), full("RN"), rev("pen", h * H, h * H + H), 4.0, A.add, A.min)
         v_tt(h8("uy", h), st("ts", h * H, h * H + H, 16), h8("CU", h), A.add)
         v_ts(h8("uu", h), h8("uy", h), 2048.0, A.mult)
         v_tt(ko, ind(full("FF"), h8("uu", h)), half("BA", h), A.add, FK)
         if t < R - 1:
-            send(ko, half("Kl%d" % (t + 1), h, KZ), ("Ka", "Kb")[h] + str(t + 1), nxt)
+            send(ko, kh(t + 1, h), ("Ka", "Kb")[h] + str(t + 1), nxt)
         else:
             dmas("y", "dy%d" % h, [(T.yk[:, h * H:h * H + H], pa(ko))], [ko], ["yk%d" % h], 64)
 
     def window(t):
-        kl = ("Kl%d" % t, KZ, KZ + 256)
-        mm(("b5", 0, 256), full("LD"), kl, True, True)
+        for h in range(2):
+            mm(LP[h], full("LD"), kh(t, h), True, True)
         s_act(full("KD"), ("b5", 0, 256), F.Copy)
+        for h in range(2):
+            mm(XP[h], full("L15"), kh(t, h), True, True)
+        s_act(full("K15"), ("b5", 256, 512), F.Copy)
         dmas("y", "dkd", [(T.kd[:, 1:17, :], T.KD[:])], ["KD"], ["kd"], 128)
-        dmas("y", "dw2", [(T.W[0::16, 4096:FW], T[kl[0]][0::16, kl[1]:kl[2]])], [kl, "W"], ["W16"], 8)
+        dmas("y", "dw2", [(T.W[0::16, 4096 + h * H:4096 + h * H + H], T[kh(t, h)[0]][0::16, kh(t, h)[1]:kh(t, h)[2]]) for h in range(2)], ["Kl%d" % t, "W"], ["W16"], 8)
         runs = [(T.FF[j::16, 0:(15 - j) * 256], T.kd[:, j + 1:16, :]) for j in range(1, 15)] + [(T.FF[:, 16 * 256:FW], T.kd[:, 0:16, :])]
         dmas("y", "df", runs[NG:], ["kd", "kz", "FF"], ["Fy"], 500)
         dmas("p", "dg", runs[:NG], ["kd", "FF"], ["Fg"], 500)
 
-    def names(t):
-        dmas("y", "dw", [(T.W[0::16, 0:4096], T["Pl%d" % t][:])], ["Pl%d" % t, "W"], ["W0"], 128)
-        mm(P32, full("I32"), full("Pl%d" % t), True, False)
-        mm(P32, full("Ib"), full("N23"), False, True)
+    def names(t, h):
+        x = half(P32[0], h, P32[1])
+        mm(x, full("I32"), half("Pl%d" % t, h), True, False)
+        mm(x, full("Ib"), half("N23", 0), False, True)
+        if h:
+            dmas("y", "dw", [(T.W[0::16, 0:4096], T["Pl%d" % t][:])], ["Pl%d" % t, "W"], ["W0"], 128)
+
+    def kh(t, h):
+        return ("Kl%d" % t, KZ + (KZ + H) * h, (KZ + H) * (h + 1))
 
     def k_list(t, h):
-        v_cp(half("Ku", h), ind(half("Kl%d" % t, h, KZ), h8("uP", 0)))
+        v_cp(half("Ku", h), ind(kh(t, h), h8("uP", 0)))
 
-    def p_list(t):
-        v_cp(full("Pu"), ind(full("Pl%d" % t), full("uP")))
+    def p_list(t, h):
+        v_cp(half("Pu", h), ind(half("Pl%d" % t, h), h8("uP", 0)))
 
-    def phages(t):
-        po = full("Po%d" % t)
-
-        def out():
-            v_cp(po, full("p2"))
-            if t < R - 1:
-                send(po, full("Pl%d" % (t + 1)), "Pa%d" % (t + 1), prv)
-            else:
-                dmas("y", "dy2", [(T.yp[:], pa(po))], [po], ["yp"], 128)
-        return [[lambda: v_tt(full("kp"), ind(full("Kl%d" % t), full("uK")), full("Pl%d" % t), A.mult)],
-                [lambda: v_tt(full("p1"), full("kp"), P32, A.add)],
-                [lambda: v_ts(full("p2"), full("p1"), 5, A.arith_shift_right, 4095, A.bitwise_and)], [out]]
+    def phages(t, h):
+        kl, po = h8("kl%d" % t, h), half("Po%d" % t, h)
+        v_ts(kl, h8("q", h), 0.0, A.is_lt, 32.0, A.mult)
+        v_tt(h8("klc", h), kl, h8("CL", h), A.add)
+        v_ts(h8("uK", h), h8("klc", h), KZ / 256.0 - 32.0 - h / 2.0, A.add, 256.0, A.mult)
+        kw = ("Kl%d" % t, (KZ + H) * h, (KZ + H) * (h + 1))
+        v_tt(half("kp", h), ind(kw, h8("uK", h)), half("Pl%d" % t, h), A.mult)
+        v_tt(half("p1", h), half("kp", h), half(P32[0], h, P32[1]), A.add)
+        v_ts(half("p2", h), half("p1", h), 5, A.arith_shift_right, 4095, A.bitwise_and)
+        v_cp(po, half("p2", h))
+        if t < R - 1:
+            send(po, half("Pl%d" % (t + 1), h), ("Pa", "Pb")[h] + str(t + 1), prv)
+        elif h:
+            dmas("y", "dy2", [(T.yp[:], T["Po%d" % t][:])], ["Po%d" % t], ["yp"], 128)
 
     def thresh(t):
         for u in range(t):
@@ -473,8 +490,12 @@ def rank_program(g, core, T, topo):
         v_ts(full("Am"), full("Ai"), 15 << 18, A.bitwise_and)
         v_ts(full("thr"), full("Am"), 160.0 * 65536 - 1, A.add)
 
-    def w_gather(o, u):
-        s_act(full(o), ind(full("W"), full(u)), F.Copy, WK)
+    def own_names():
+        x = ind(full("W"), full("uV"))
+        op("v", lambda: V.tensor_scalar(T.VG[:], pa(x), -2048.0, None, A.add), WK + [full("uV")], ["VG"], ns(full("VG"), 1, x))
+
+    def base():
+        v_tt(full("BA"), ind(full("W"), full("uN")), full("K15"), A.add, WK)
 
     def scatter(c):
         u, x = full("uX")[1] + SC * c, (16 * SC * c, 16 * SC * (c + 1))
@@ -491,79 +512,87 @@ def rank_program(g, core, T, topo):
 
     def marked(x, stop):
         mm(x, full("NL"), full("OD"), True, False)
-        mm(x, full("L0"), full("VG"), False, stop)
+        mm(x, full("L0h"), full("VG"), False, stop)
+
+    def gathers(h):
+        bias(h)
+        todo = None
+        for c in range(4):
+            s_gather(h, c)
+            n = PIECE[4 * h + c]
+            for a in range(0, 4, n):
+                d_gather(h, c, a, n)
+                if todo:
+                    keys(h, *todo)
+                todo = (4 * c + a, n, ABS[4 * h + c]) if c == 3 else (4 * c, 4, ABS[4 * h + c]) if a + n == 4 else None
+        keys(h, *todo)
 
     for t in range(R):
-        kl, last = full("kl%d" % t), t == R - 1
-        p0, p1, ph = pick(0), pick(1), phages(t)
+        last = t == R - 1
+        p0, p1 = pick(0), pick(1)
         if t:
             k_list(t, 0)
-            p_list(t)
+            p_list(t, 0)
+            p_list(t, 1)
+        gathers(0)
+        if t:
             k_list(t, 1)
-        for h in range(2):
-            bias(h)
-            for c in range(4):
-                s_gather(h, c)
-                for a in range(0, 4, PIECE[4 * h + c]):
-                    d_gather(h, c, a, PIECE[4 * h + c])
-                keys(h, c, 1, ABS[4 * h + c])
-            if h == 0:
-                window(t)
-                if t == 0:
-                    more_constants()
-                run(*p0)
-                x_n(0)
-                near(0)
-                if t:
-                    thresh(t)
-                names(t)
-        run(*p1[:3])
-        v_ts(kl, full("q"), 0.0, A.is_lt, 32.0, A.mult)
+        window(t)
+        if t == 0:
+            more_constants()
+        names(t, 0)
+        names(t, 1)
+        run(*p0)
+        x_n(0)
+        if t:
+            thresh(t)
+        gathers(1)
+        phages(t, 0)
+        run(*p1[:2])
         v_ts(full("g1"), full("q"), full("thr"), A.is_ge, 32.0, A.mult)
-        v_tt(full("klc"), kl, full("CL"), A.add)
-        v_ts(full("k"), full("r"), 15, A.bitwise_and)
-        v_tt(full("av"), full("klc"), full("g1"), A.add)
-        v_tt(full("oV"), full("k"), full("av"), A.add)
+        v_ts(full("k"), full("q"), 12, A.arith_shift_right, 15, A.bitwise_and)
+        v_ts(full("k2"), full("q"), 0.0, A.is_lt, 32.0, A.mult)
+        v_tt(full("oM"), full("g1"), full("CL"), A.add)
+        v_tt(full("oN"), full("k"), full("k2"), A.add)
+        v_tt(full("oV"), full("oM"), full("oN"), A.add)
         v_ts(full("uV"), full("oV"), 17.0, A.min, 256.0, A.mult)
-        w_gather("VG", "uV")
+        run(*p1[2:])
+        own_names()
+        x_n(1)
         marked(VE, True)
-        mm(VP, full("L0"), full("VG"), True, True)
-        v_scan(full("RU"), full("RC"), VE, 0.0, A.max, A.min)
-        v_cp(full("uY"), st("RU", 15, 256, 16))
-        run(*p1[3:])
+        mm(VP, full("L0h"), full("VG"), True, True)
+        v_scan(full("RU"), full("RC"), VE, -4096.0, A.max, A.min)
+        v_ts(full("uY"), st("RU", 15, 256, 16), 2048.0, A.add)
+        near(0, range(4))
+        phages(t, 1)
+        v_tt(full("av"), full("oM"), full("k2"), A.add)
         v_tt(full("oN"), full("f"), full("av"), A.add)
         v_tt(full("oM"), full("oN"), full("CW"), A.min)
         v_ts(full("uN"), full("oM"), 256.0, A.mult)
         if not last:
-            w_gather("N0", "uN")
+            base()
             new_arrays(t, 0)
-            x_n(1)
+            near(1, range(NE))
         v_tt(full("o2"), full("k"), full("CK"), A.add)
         v_cp(full("uk"), full("o2"))
-        v_ts(full("uK"), full("klc"), KZ / 256.0 - 32.0, A.add, 256.0, A.mult)
-        run(ph[0], ph[1])
         marked(ME, False)
         v_tt(("FD", 1, 256), (VP[0], VP[1] + 1, VP[2]), ("RU", 0, 255), A.is_equal)
         mm(ME, full("BK"), full("FD"), False, False)
-        if not last:
-            run(ph[2], ph[3])
         equals()
         s_act(full("YK"), ind(full("X"), full("uY")), F.Copy)
         s_sign(SG, full("YK"), full("cy"), 1.0)
         s_act(full("AD"), ind(full("D"), full("uk")), F.Abs)
-        v_scan(full("SE"), full("RC"), ME, 0.0, A.max, A.min)
-        v_cp(full("uX"), st("SE", 15, 256, 16))
+        v_scan(full("SE"), full("RC"), ME, -4096.0, A.max, A.min)
+        v_ts(full("uX"), st("SE", 15, 256, 16), 2048.0, A.add)
         v_ts(full("w2"), full("AD"), 32.0, A.is_le, -128.0, A.mult)
         v_tt(full("wg"), full("w2"), SG, A.mult)
         for c in range(LO // SC - 1, -1, -1):
             scatter(c)
         if last:
             dmas("y", "dy3", [(T.yx[:], T.X[:, 0:4096])], ["X"], ["yx"], 1024)
-            w_gather("N0", "uN")
-            x_n(1)
+            base()
             new_arrays(t, 0)
-            run(ph[2], ph[3])
-        near(1)
+        near(1, range(0 if last else NE, 4))
         new_arrays(t, 1)
     schedule()
     for sm, val in sorted(cnt.items()):

@@ -8,42 +8,51 @@ FW, WW, XW = 17 * 256, 17 * 256 + 16, 4096 + 256
 SC = 4
 NG = 5
 KZ = 16
-ABS = (0, 0, 0, 0, 1, 1, 1, 0)
-PIECE = (4, 4, 4, 4, 2, 2, 2, 2)
-NE = 2
-WAKE, FAR, FIT = 175, 2000, {"v": 250, "s": 200, "t": 200, "p": 0, "y": 0}
+YP, DP, KP = ((2, 2, 4, 4, 4), (4, 4, 4, 4)), ((2, 2, 4, 4, 4), (4, 2, 2, 2, 2, 2, 2)), ((4, 4, 4, 4), (-4, -4, -2, -2, -2, 2))
+LIST = {
+    "v": ("D D D RA RA D D RA Ku Ai RA D D KM D q D sg a D a1 s2 kl k L0h dl D fs D f klc RA o1 uK Am uf kp "
+          "KM p1 q thr a sg kl k a1 g1 p2 klc s2 uK dl av RC oN fs kp oV f uV o1 oN p1 VG o2 uf oM Po uN "
+          "RU p2 EQ EQ EQ uk EQ EQ EQ EQ FD ts EQ Po uy BA uu EQ EQ EQ EQ Ko w2 SE wg uX X X X Pu+ X Pu+ ts uy uu Ku+ Ko",
+          "D D D Ai RA D RA D Am Ku RA thr RA D D KM q D a sg k kl a1 s2 D dl D fs D f D klc o1 RA uf uK kp "
+          "KM q p1 a k kl sg a1 g1 o2 s2 p2 oN dl klc oV Po fs uV av uk f VG o1 uf "
+          "RU w2 EQ EQ EQ EQ uK oN FD EQ oM EQ EQ EQ wg uN EQ EQ EQ EQ SE uX X X X X kp ts p1 BA uy ts uu uy p2 uu Ko Po Ko"),
+    "s": ("Y Y Y Y Y Y Y junk KD Y Y K15 RA RA RA RA RA SF XT NA NA NA NA SF pen YK XT b5 AD NA NA NA NA pen",
+          "Y Y Y junk Y Y Y Y KD Y Y RA K15 RA RA RA RA SF XT NA NA YK AD NA b7 SF XT NA NA NA pen NA NA pen"),
+}
+WAKE, FAR, FIT = 175, 2300, {"v": 0, "s": 0, "t": 200, "p": 2000, "y": 0}
 DY, DG, DL = 150, 1000, 1200
 
 SCRATCH = {
     "X": ("sbuf", [128, XW], "bfloat16"),
     "KI": ("sbuf", [128, 256], "int32"), "PI": ("sbuf", [128, 256], "int32"),
     "Ku": ("sbuf", [128, 256], "uint16"), "Pu": ("sbuf", [128, 256], "uint16"),
-    "S": ("sbuf", [128, 4096], "bfloat16"), "D": ("sbuf", [128, 4096], "bfloat16"),
+    "Y": ("sbuf", [128, 4096], "bfloat16"), "D": ("sbuf", [128, 4096], "bfloat16"),
     "RA": ("sbuf", [128, 4096], "bfloat16"), "NA": ("sbuf", [128, 4096], "bfloat16"),
     "KM": ("sbuf", [128, 256], "float32"),
     "LI": ("sbuf", [128, 256], "int32"), "LF": ("sbuf", [128, 256], "float32"), "LB": ("sbuf", [128, 128], "bfloat16"), "LU": ("sbuf", [128, 160], "uint16"),
-    "SF": ("sbuf", [128, 256], "bfloat16"), "DF": ("sbuf", [128, 256], "bfloat16"), "XT": ("sbuf", [128, 256], "bfloat16"),
+    "SF": ("sbuf", [128, 256], "bfloat16"), "XT": ("sbuf", [128, 256], "bfloat16"),
     "YK": ("sbuf", [128, 256], "bfloat16"), "AD": ("sbuf", [128, 256], "bfloat16"),
     "w2": ("sbuf", [128, 256], "bfloat16"), "wg": ("sbuf", [128, 256], "bfloat16"),
     "pen": ("sbuf", [128, 256], "bfloat16"), "ts": ("sbuf", [128, 256], "bfloat16"),
     "kp": ("sbuf", [128, 256], "float32"), "p1": ("sbuf", [128, 256], "int32"), "p2": ("sbuf", [128, 256], "int32"),
     "KD": ("sbuf", [128, 256], "float32"), "K15": ("sbuf", [128, 256], "float32"), "BA": ("sbuf", [128, 256], "float32"),
     "W": ("sbuf", [128, WW], "float32"), "FF": ("sbuf", [128, FW], "float32"), "kd": ("dram", [8, 17, 256], "float32"),
-    "VG": ("sbuf", [128, 256], "float16"), "L0h": ("sbuf", [128, 128], "float16"), "RU": ("sbuf", [128, 256], "float32"), "FD": ("sbuf", [128, 256], "bfloat16"),
+    "VG": ("sbuf", [128, 256], "float16"), "RU": ("sbuf", [128, 256], "float32"), "FD": ("sbuf", [128, 256], "bfloat16"),
     "EQ": ("sbuf", [128, 2048], "bfloat16"), "SE": ("sbuf", [128, 256], "float32"),
     "If": ("sbuf", [128, 128], "float32"), "I32": ("sbuf", [128, 128], "float32"), "Ib": ("sbuf", [128, 128], "bfloat16"), "I256": ("sbuf", [128, 128], "bfloat16"),
     "ZF": ("sbuf", [128, 256], "float32"), "ZB": ("sbuf", [128, 256], "bfloat16"),
     "OD": ("sbuf", [128, 256], "bfloat16"), "NL": ("sbuf", [128, 128], "bfloat16"), "EX": ("sbuf", [128, 2048], "bfloat16"),
-    "Q": ("sbuf", [128, 720], "bfloat16"), "BK": ("sbuf", [128, 128], "bfloat16"),
-    "L0": ("sbuf", [128, 128], "float32"), "L15": ("sbuf", [128, 128], "float32"), "L16": ("sbuf", [128, 128], "float32"), "LD": ("sbuf", [128, 128], "float32"),
+    "Q": ("sbuf", [128, 576], "bfloat16"), "BK": ("sbuf", [128, 128], "bfloat16"),
+    "L0": ("sbuf", [128, 128], "float32"), "L0h": ("sbuf", [128, 128], "float16"),
+    "L15": ("sbuf", [128, 128], "float32"), "L16": ("sbuf", [128, 128], "float32"), "LD": ("sbuf", [128, 128], "float32"),
     "RS": ("sbuf", [128, 128], "float32"), "RC": ("sbuf", [128, 256], "float32"), "RN": ("sbuf", [128, 128], "bfloat16"),
-    "NB": ("sbuf", [128, 128], "bfloat16"), "J4": ("sbuf", [128, 128], "bfloat16"), "N23": ("sbuf", [128, 256], "bfloat16"),
+    "NB": ("sbuf", [128, 128], "bfloat16"), "J4": ("sbuf", [128, 128], "bfloat16"), "N23": ("sbuf", [128, 128], "bfloat16"),
 }
 for _i in range(8):
     SCRATCH["b%d" % _i] = ("psum", [128, 512], "float32")
 SMALL = {}
-for _b, _l in (("LI", "q r sg a s2 a1 dl fs f k o1 o2 C16 CK Ai Am"), ("LF", "klc av oV oN oM uy CL CW CU cnt thr cn cy junk k2"),
-               ("LB", "kl0 kl1 kl2 kl3 g1"), ("LU", "uf uk uu uV uN uK uY uP uX")):
+for _b, _l in (("LI", "q sg a s2 a1 dl fs f k o1 o2 C16 CK Ai Am"), ("LF", "klc av oV oN oM uy CL CW CU cnt thr cn cy junk"),
+               ("LB", "kl0 kl1 kl2 kl3 g1"), ("LU", "uf uk uu uV uN uK uP uX")):
     for _i, _n in enumerate(_l.split()):
         SMALL[_n] = (_b, 16 * _i, 16 * _i + (1 if _n in ("Ai", "Am", "cnt", "thr", "cn", "cy") else 16))
 for _t in range(R):
@@ -51,7 +60,7 @@ for _t in range(R):
     for _n in ("Pl", "Ko", "Po"):
         SCRATCH["%s%d" % (_n, _t)] = ("sbuf", [128, 256], "float32")
 
-SEMAPHORES = (["v", "s", "t", "p", "ls", "dx", "dk", "dp", "dz", "dw", "dw2", "dkd", "df", "dg", "dy0", "dy1", "dy2", "dy3"]
+SEMAPHORES = (["v", "s", "t", "p", "ls", "dx", "dk", "dp", "dz", "dz2", "dw", "dw2", "dkd", "df", "dg", "dy0", "dy1", "dy2", "dy3"]
               + ["%s%d" % (n, t) for n in ("Ka", "Kb", "Pa", "Pb") for t in range(1, R)])
 
 
@@ -108,6 +117,7 @@ def rank_program(g, core, T, topo):
                 recs[b] = old + [(lo, hi, q, sm, val, wr)]
 
     calls = []
+    now = [-1]
 
     def op(q, call, reads, writes, ns, kind=None):
         def issue():
@@ -115,7 +125,7 @@ def rank_program(g, core, T, topo):
             cnt[q] = cnt.get(q, 0) + 1
             call().then_inc(T.sem[q], 1)
             note(q, reads, writes, q, cnt[q])
-        calls.append((q, issue, reads, writes, ns, ns, kind))
+        calls.append((q, issue, reads, writes, ns, ns, kind, now[0]))
 
     def dmas(q, sm, pairs, reads, writes, kib):
         def issue():
@@ -125,12 +135,12 @@ def rank_program(g, core, T, topo):
                 cnt[sm] = cnt.get(sm, 0) + 16
             note(q, reads, writes, sm, cnt[sm])
         ns = len(pairs) * (DG if q == "p" else DY)
-        calls.append((q, issue, reads, writes, ns, ns + DL + 3 * kib, None))
+        calls.append((q, issue, reads, writes, ns, ns + DL + 3 * kib, None, now[0]))
 
     def schedule():
         n = len(calls)
-        pred, seen, closed, group = [set() for _ in range(n)], {}, {}, {}
-        for i, (q, _, reads, writes, _, _, kind) in enumerate(calls):
+        pred, seen, closed, group, users = [set() for _ in range(n)], {}, {}, {}, {}
+        for i, (q, _, reads, writes, _, _, kind, _) in enumerate(calls):
             for accs, wr in ((reads, False), (writes, True)):
                 for x in accs:
                     b, lo, hi = key(x)
@@ -139,12 +149,34 @@ def rank_program(g, core, T, topo):
                         seen[b] = [e for e in seen.get(b, ()) if not (lo <= e[0] and e[1] <= hi)]
                         if kind and kind[0] and b in closed:
                             pred[i].add(closed[b])
+                            pred[i].update(users.pop(b, ()))
                         if kind:
                             group[b] = ([] if kind[0] else group[b]) + [i]
                         if kind and kind[1]:
                             closed[b] = i
                             pred[i].update(group[b][:-1])
                     seen.setdefault(b, []).append((lo, hi, wr, i))
+                    if bank(b) and q != "t":
+                        users.setdefault(b, []).append(i)
+        small, inline = {x[:2]: nm for nm, x in SMALL.items()}, set()
+        for q in LIST:
+            todo = {}
+            for i, c in enumerate(calls):
+                if c[0] == q:
+                    b, lo, _ = key(c[3][0])
+                    nm = small.get((b, lo - lo % 16), b)
+                    todo.setdefault((c[7], nm[:2] if nm[:2] in ("kl", "Ko", "Po") and nm[2:].isdigit() else nm), []).append(i)
+            line = sorted(i for (t, _), x in todo.items() if t < 0 for i in x)
+            for t in range(R):
+                for w in LIST[q][t == R - 1].split():
+                    x = todo.get((t + w.count("+"), w.rstrip("+")))
+                    if x:
+                        line.append(x.pop(0))
+            assert len(line) == sum(c[0] == q for c in calls)
+            for i, j in zip(line, line[1:]):
+                if i not in pred[j]:
+                    pred[j].add(i)
+                    inline.add((i, j))
         succ = [[] for _ in range(n)]
         for i in range(n):
             for j in pred[i]:
@@ -175,7 +207,7 @@ def rank_program(g, core, T, topo):
             for b in banks[i]:
                 held[b] = (q, t0 + calls[i][5])
             for j in succ[i]:
-                early[j] = max(early[j], t0 + calls[i][5] + (0 if q == calls[j][0] == "t" else WAKE))
+                early[j] = max(early[j], t0 + calls[i][5] + (0 if q == calls[j][0] == "t" or (i, j) in inline else WAKE))
                 left[j] -= 1
                 if not left[j]:
                     ready[calls[j][0]].append(j)
@@ -200,10 +232,10 @@ def rank_program(g, core, T, topo):
     def v_tt(o, a, b, f, more=()):
         op("v", lambda: V.tensor_tensor(pa(o), pa(a), pa(b), f), ks(a, b) + list(more), ks(o), ns(o, 1 if bank(a[0]) or bank(b[0]) else 2, a))
 
-    def v_ts(o, a, x, f, y=None, f2=None):
+    def v_ts(o, a, x, f, y=None, f2=None, more=()):
         x1 = pa(x) if isinstance(x, tuple) else x
         if f2 is None:
-            op("v", lambda: V.tensor_scalar(pa(o), pa(a), x1, None, f), ks(a, x), ks(o), ns(o, short(o, a), a))
+            op("v", lambda: V.tensor_scalar(pa(o), pa(a), x1, None, f), ks(a, x) + list(more), ks(o), ns(o, short(o, a), a))
         else:
             op("v", lambda: V.tensor_scalar(pa(o), pa(a), x1, y, f, f2), ks(a, x), ks(o), ns(o, short(o, a), a))
 
@@ -216,11 +248,11 @@ def rank_program(g, core, T, topo):
     def v_ms(o, c):
         op("v", lambda: V.memset(pa(o), c), [], ks(o), ns(o, short(o)))
 
-    def s_act(o, a, f, more=()):
-        op("s", lambda: S.activation(pa(o), pa(a), f), ks(a) + list(more), ks(o), ns(o, 1, a) + (10 if len(a) > 4 else 60))
+    def s_act(o, a, f):
+        op("s", lambda: S.activation(pa(o), pa(a), f), ks(a), ks(o), ns(o, 1, a) + (10 if len(a) > 4 else 60))
 
-    def s_sign(o, a, bias, scale):
-        op("s", lambda: S.activation(pa(o), pa(a), F.Sign, bias=pa(bias), scale=scale), ks(a, bias), ks(o), ns(o, 1) + 60)
+    def s_sign(o, a, bias):
+        op("s", lambda: S.activation(pa(o), pa(a), F.Sign, bias=pa(bias)), ks(a, bias), ks(o), ns(o, 1) + 60)
 
     def mm(o, l, r, start, stop):
         n = max(64, o[3][1] if len(o) > 3 else o[2] - o[1]) * (4 if SCRATCH[l[0]][2] == "float32" else 1)
@@ -228,10 +260,10 @@ def rank_program(g, core, T, topo):
 
     def iota(o, pattern, base, cm):
         flag = {} if SCRATCH[o[0]][2] == "int32" else {"allow_small_or_imprecise_dtypes": True}
-        op("p", lambda: g.iota(pa(o), pattern, base, cm, **flag), [], ks(o), ns(o, 2) + 75)
+        op("p", lambda: g.iota(pa(o), pattern, base, cm, **flag), [], ks(o), ns(o, 2) + 130)
 
     def pick_of(o, src, pattern, how, fill, base_, cm):
-        op("p", lambda: g.affine_select(pa(o), pa(src), pattern, how, fill, base_, cm), ks(src), ks(o), ns(o, 2) + 115)
+        op("p", lambda: g.affine_select(pa(o), pa(src), pattern, how, fill, base_, cm), ks(src), ks(o), ns(o, 2) + 170)
 
     def ind(w, u):
         return (w[0], w[1], w[2], (T[w[0]][:, w[1]:w[2]].indirect(T[u[0]][:, u[1]:u[2]]), 16 * (u[2] - u[1])), u[:3])
@@ -252,21 +284,23 @@ def rank_program(g, core, T, topo):
     def half(b, h, at=0):
         return (b, at + h * H, at + h * H + H)
 
-    def wide(b, h, c=0, n=4):
-        return (b, 2048 * h + 512 * c, 2048 * h + 512 * (c + n))
+    def part(b, h, i=0, n=LO):
+        return (b, 2048 * h + 128 * i, 2048 * h + 128 * (i + n))
+
+    def kh(t, h):
+        return ("Kl%d" % t, KZ + (KZ + H) * h, (KZ + H) * (h + 1))
 
     for t in range(1, R):
-        for sm, src, x in (("Ka", prv, half("Kl%d" % t, 0, KZ)), ("Kb", prv, half("Kl%d" % t, 1, 2 * KZ)),
-                           ("Pa", nxt, half("Pl%d" % t, 0)), ("Pb", nxt, half("Pl%d" % t, 1))):
+        for sm, src, x in (("Ka", prv, kh(t, 0)), ("Kb", prv, kh(t, 1)), ("Pa", nxt, half("Pl%d" % t, 0)), ("Pb", nxt, half("Pl%d" % t, 1))):
             cnt[sm + str(t)] = len(topo.engines(src, core))
             recs.setdefault(x[0], []).append((x[1], x[2], "r", sm + str(t), cnt[sm + str(t)], True))
-    dmas("y", "dk", [(T.KI[:], T.ka[:])], [], ["KI"], 128)
-    dmas("y", "dp", [(T.PI[:], T.ph[:])], [], ["PI"], 256)
+    dmas("y", "dp", [(T.PI[:], T.ph[:])], [], ["PI"], 128)
+    dmas("y", "dk", [(T.KI[:], T.ka[:])], [], ["KI"], 256)
     dmas("y", "dx", [(T.X[:, 0:4096], T.x0[:])], [], [("X", 0, 4096)], 1024)
 
     ZF, ZB, FQ = ("ZF", 0, 128), ("ZB", 0, 128), FW // 4
-    v_ms(full("ZF"), 0.0)
     v_ms(("W", 0, FQ), 0.0)
+    v_ms(full("ZF"), 0.0)
     v_ms(full("ZB"), 0.0)
     v_ms(full("Q"), 0.0)
     iota(full("q"), [[0, 16]], 0, 1)
@@ -275,83 +309,77 @@ def rank_program(g, core, T, topo):
     pick_of(full("L16"), ZF, [[16, 8], [0, 16]], A.not_equal, 1.0, 15, -1)
     pick_of(full("Ib"), ZB, [[1, 128]], A.not_equal, 1.0, 0, -1)
     iota(full("J4"), [[0, 8], [4096, 16]], 0, 0)
-    for n, w in enumerate((-65536.0, 131072.0, -1.0, 65536.0, 1.0)):
+    for n, w in enumerate((-65536.0, 131072.0, 1.0, 65536.0)):
         x = st("Q", 144 * n + 15, 144 * n + 144, 16)
         pick_of(x, x, [[16, 9]], A.is_gt, w, 0, -1)
-    x = st("Q", 15, 720, 16)
-    pick_of(x, x, [[0, 5], [16, 9]], A.is_ge, 0.0, 15, -1)
+    x = st("Q", 15, 576, 16)
+    pick_of(x, x, [[0, 4], [16, 9]], A.is_ge, 0.0, 15, -1)
     iota(full("o2"), [[16, 16]], 0, 0)
     iota(full("C16"), [[0, 2], [16, 8]], 0, 0)
     iota(full("CK"), [[2048, 2], [16, 8]], 0, 0)
     pick_of(full("RS"), ZF, [[0, 8], [1, 16]], A.not_equal, BIG, 0, 0)
+    pick_of(full("L15"), full("L16"), [[0, 8], [1, 16]], A.not_equal, 0.0, 0, 0)
     pick_of(full("I32"), ZF, [[1, 128]], A.not_equal, 32.0, 0, -1)
-    for n in range(4):
-        s_act(("FF", n * FQ, n * FQ + FQ), ("W", 0, FQ), F.Copy)
-    s_act(("W", FQ, 2 * FQ), ("W", 0, FQ), F.Copy, ["FF"])
+    for n in range(1, 4):
+        s_act(("W", n * FQ, n * FQ + FQ), ("W", 0, FQ), F.Copy)
+    dmas("y", "dz2", [(T.FF[:], T.W[:, 0:FW])], [("W", 0, FW), ("X", 0, 4096)], ["FF", "Wz"], 2176)
     v_ts(full("a"), full("q"), 7, A.bitwise_and)
-    v_ts(full("r"), full("q"), 3, A.arith_shift_right, 1, A.bitwise_and)
-    v_ms(full("EX"), 0.0)
-    v_ts(full("a1"), full("a"), 16.0, A.mult)
-    v_tt(full("s2"), full("r"), full("o1"), A.add)
+    v_ts(full("sg"), full("q"), 3, A.arith_shift_right, 1, A.bitwise_and)
     v_ts(full("k"), full("q"), 15, A.bitwise_and)
-    v_tt(full("dl"), full("a1"), full("s2"), A.add)
+    v_ts(full("a1"), full("a"), 16.0, A.mult)
+    v_tt(full("s2"), full("sg"), full("o1"), A.add)
     v_ms(full("NB"), -864.0 * 65536)
-    v_cp(full("uP"), full("dl"))
     for t in range(R):
         v_ms(("Kl%d" % t, 0, KZ), 0.0)
+        if t == 0:
+            v_tt(full("dl"), full("a1"), full("s2"), A.add)
         v_ms(("Kl%d" % t, KZ + H, 2 * KZ + H), 0.0)
-    v_cp(full("Ku"), ind(full("KI"), full("uP")))
+        if t == 1:
+            v_cp(full("uP"), full("dl"))
     v_cp(full("Pu"), ind(full("PI"), full("uP")))
-    v_cp(half("Kl0", 0, KZ), half("KI", 0))
-    v_cp(half("Kl0", 1, 2 * KZ), half("KI", 1))
+    v_cp(full("Ku"), ind(full("KI"), full("uP")))
+    v_cp(kh(0, 0), half("KI", 0))
+    v_cp(kh(0, 1), half("KI", 1))
     v_tt(full("LD"), full("If"), full("L16"), A.subtract)
     v_cp(full("Pl0"), full("PI"))
-    v_ms(("W", 2 * FQ, FW), 0.0)
     dmas("y", "dz", [(T.kd[:, 0:1, :], T.ZF[0:8, 0:256])], ["ZF"], ["kz"], 8)
-    pick_of(full("EX"), full("EX"), [[1, 16], [16, 8], [0, 16]], A.not_equal, -1.0, 0, -1)
+    iota(full("N23"), [[0, 128]], -2 ** 23, 0)
+    for n in range(8):
+        pick_of(("EX", 256 * n, 256 * n + 256), full("ZB"), [[1, 2], [16, 8], [0, 16]], A.not_equal, -1.0, 2 * n, -1)
     iota(("W", FW, WW), [[0, 16]], 8192, 0)
-    iota(full("N23"), [[0, 256]], -2 ** 23, 0)
-    iota(("X", 4096, XW), [[0, 256]], 0, 0)
     iota(full("RC"), [[0, 256]], -4096, 0)
     pick_of(full("L0"), ZF, [[16, 8], [0, 16]], A.not_equal, 1.0, 0, -1)
     pick_of(full("OD"), full("ZB"), [[0, 16], [1, 16]], A.not_equal, OFF, 0, -1)
     pick_of(full("NL"), ZB, [[0, 8], [1, 16]], A.is_equal, 1.0, 0, -1)
-    pick_of(full("I256"), ZB, [[1, 128]], A.not_equal, 256.0, 0, -1)
-    pick_of(full("L15"), full("L16"), [[0, 8], [1, 16]], A.not_equal, 0.0, 0, 0)
+    pick_of(full("I256"), ZB, [[1, 128]], A.not_equal, -256.0, 0, -1)
     pick_of(full("BK"), ZB, [[16, 8], [0, 16]], A.is_gt, 8192.0, 0, -1)
     pick_of(full("BK"), full("BK"), [[16, 8], [0, 16]], A.is_ge, 0.0, 15, -1)
-
-    def more_constants():
-        v_tt(full("o2"), full("o2"), full("k"), A.add)
-        v_ts(full("a"), full("k"), 128.0, A.mult)
-        v_ms(full("RN"), 0.125)
-        v_ms(("FD", 0, 1), 0.0)
-        v_ms(full("thr"), 160.0 * 65536 - 1)
-        v_tt(full("C16"), full("C16"), full("a"), A.add)
-        v_tt(full("CK"), full("CK"), full("a"), A.add)
-        v_ms(full("cn"), -1023.5)
-        v_ms(full("cy"), -127.5)
-        v_ts(st("RN", 0, 128, 16), ("ZB", 0, 8), 4.0, A.add)
-        v_ts(st("RC", 0, 256, 16), full("o2"), 2048.0, A.add)
-        v_cp(full("L0h"), full("L0"))
-        v_ts(full("CL"), full("o2"), 1.0 / 256, A.mult)
-        v_ts(full("CW"), full("o2"), 1.0 / 256, A.mult, 16.0, A.add)
-        v_ts(full("CU"), full("o2"), 1.0 / 2048, A.mult, 1.0, A.add)
+    iota(("X", 4096, XW), [[0, 256]], 0, 0)
+    v_tt(full("o2"), full("o2"), full("k"), A.add)
+    v_ts(full("a"), full("k"), 128.0, A.mult)
+    v_ms(full("RN"), 0.125)
+    v_ms(("FD", 0, 1), 0.0)
+    v_ms(full("thr"), 160.0 * 65536 - 1)
+    v_tt(full("C16"), full("C16"), full("a"), A.add)
+    v_tt(full("CK"), full("CK"), full("a"), A.add)
+    v_ms(full("cn"), -1023.5)
+    v_ms(full("cy"), -127.5)
+    v_ts(st("RN", 0, 128, 16), ("ZB", 0, 8), 4.0, A.add)
+    v_ts(full("CL"), full("o2"), 1.0 / 256, A.mult)
+    v_ts(full("CW"), full("o2"), 1.0 / 256, A.mult, 16.0, A.add)
+    v_ts(full("CU"), full("o2"), 1.0 / 2048, A.mult, 1.0, A.add)
 
     KEY = [("b0", 0, 128), ("b1", 0, 128)]
     ND = [("b1", 128, 256), ("b1", 256, 384)]
-    VP, CN = ("b0", 256, 512), ("b0", 128, 144)
+    XP = [("b0", 128, 256), ("b5", 384, 512)]
+    VP, CN = ("b0", 256, 512), ("b1", 384, 400)
     NEAR = ("b2", "b3", "b4", "b6")
-    LP = [("b5", 0, 128), ("b5", 128, 256)]
-    XP = [("b5", 256, 384), ("b5", 384, 512)]
-    P32, ME, VE, SG = ("b5", 0, 256), ("b7", 256, 512), ("b7", 0, 256), ("b5", 0, 256)
+    LP, LQ, P32 = ("b5", 0, 256), ("b5", 256, 512), ("b5", 0, 256)
+    VE, ME = ("b7", 0, 256), ("b7", 256, 512)
 
     def lanes(w, i):
-        n = 144 * ("QN", "QR", "Q1", "QP", "Q2").index(w)
+        n = 144 * ("QN", "QR", "Q1", "QP").index(w)
         return ("Q", n + 15 - i, n + 143 - i)
-
-    def part(b, h, i):
-        return (b, 2048 * h + 128 * i, 2048 * h + 128 * i + 128)
 
     def send(x, to, sm, dst):
         rid, pid, _ = topo.addr(dst)
@@ -360,74 +388,76 @@ def rank_program(g, core, T, topo):
             sync("p", [x], [])
             g.remote_dma(pa(to), pa(x), T.sem[sm], T.sem.ls, pid, rid, topo.mask(core, dst))
             cnt["ls"] = cnt.get("ls", 0) + len(topo.engines(core, dst))
-        calls.append(("p", issue, [x], [to], 500, FAR + 4 * (x[2] - x[1]), None))
+        calls.append(("p", issue, [x], [to], 500, FAR + 4 * (x[2] - x[1]), None, now[0]))
 
     FK, WK = ["Fy", "Fg"], ["W0", "W16", "W"]
     nb = [0]
 
-    def s_gather(h, c):
-        s_act(wide("S", h, c, 1), ind(("X", 0, 4096), (("Ku", "Pu")[h], 128 * h + 32 * c, 128 * h + 32 * c + 32)), F.Copy)
-
-    def d_gather(h, c, a, n):
-        lo = 128 * h + 32 * c + 8 * a
-        v_tt(("D", 16 * lo, 16 * lo + 128 * n), ind(("X", 0, 4096), (("Pu", "Ku")[h], lo, lo + 8 * n)), ("S", 16 * lo, 16 * lo + 128 * n), A.subtract)
-
-    def bias(h):
-        mm(KEY[h], full("Ib"), full("NB"), True, False)
-        mm(KEY[h], full("Ib"), full("J4"), False, False)
-
     def keys(h, i0, n, scalar):
-        d, ra = [(b, 2048 * h + 128 * i0, 2048 * h + 128 * (i0 + n)) for b in ("D", "RA")]
         if scalar:
-            s_act(ra, d, F.Abs)
+            s_act(part("RA", h, i0, n), part("D", h, i0, n), F.Abs)
         else:
             for i in range(i0, i0 + n):
-                mm(KEY[h], lanes("QN", i), part("D", h, i), False, False)
-            v_ts(ra, d, 0.0, A.max)
+                mm(KEY[h], lanes("QN", i), part("D", h, i, 1), False, False)
+            v_ts(part("RA", h, i0, n), part("D", h, i0, n), 0.0, A.max)
         for i in range(i0, i0 + n):
-            mm(KEY[h], lanes("QP" if scalar else "QR", i), part("RA", h, i), False, False)
-            mm(KEY[h], lanes(("Q1", "Q2")[h], i), part("D", h, i), False, i == LO - 1)
+            mm(KEY[h], lanes("QP" if scalar else "QR", i), part("RA", h, i, 1), False, False)
+            mm(KEY[h], lanes("Q1", i), part("D", h, i, 1), False, i == LO - 1)
 
-    def pick(h):
-        q, r, sg, a, s2, a1, dl, fs, f, o1 = [h8(n, h) for n in ("q", "r", "sg", "a", "s2", "a1", "dl", "fs", "f", "o1")]
-        return [[lambda: v_scan(half("KM", h), ("RS", 0, 128), KEY[h], BIG, A.add, A.min)],
-                [lambda: v_ts(q, st("KM", h * H + 15, h * H + H, 16), 2047.0, A.add)],
-                [lambda: v_ts(sg, q, 10, A.arith_shift_right, 2, A.bitwise_and), lambda: v_ts(a, q, 16, A.arith_shift_right, 3, A.bitwise_and),
-                 lambda: v_ts(r, q, 12, A.arith_shift_right)],
-                [lambda: v_ts(s2, sg, -1.0, A.add), lambda: v_ts(a1, a, 1.0, A.add)],
-                [lambda: v_tt(dl, s2, a1, A.mult)], [lambda: v_tt(fs, r, dl, A.add)], [lambda: v_ts(f, fs, 15, A.bitwise_and)],
-                [lambda: v_tt(o1, f, h8("C16", h), A.add)], [lambda: v_cp(h8("uf", h), o1)]]
+    def gathers(h):
+        mm(KEY[h], full("Ib"), full("NB"), True, False)
+        mm(KEY[h], full("Ib"), full("J4"), False, False)
+        a = 0
+        for n in YP[h]:
+            s_act(part("Y", h, a, n), ind(("X", 0, 4096), ("Pu", H * h + 8 * a, H * h + 8 * (a + n))), F.Copy)
+            a += n
+        a, b, todo = 0, 0, list(KP[h])
+        for n in DP[h] + (0,):
+            if n:
+                v_tt(part("D", h, a, n), ind(("X", 0, 4096), ("Ku", H * h + 8 * a, H * h + 8 * (a + n))), part("Y", h, a, n), A.subtract)
+            while todo and b + abs(todo[0]) <= a:
+                keys(h, b, abs(todo[0]), todo[0] < 0)
+                b += abs(todo.pop(0))
+            a += n
 
-    def run(*steps):
-        for s_ in steps:
-            for c in s_:
-                c()
+    def pick(t, h):
+        q, k, sg, a, s2, a1, dl, fs, f, o1 = [h8(n, h) for n in ("q", "k", "sg", "a", "s2", "a1", "dl", "fs", "f", "o1")]
+        v_scan(half("KM", h), full("RS"), KEY[h], BIG, A.add, A.min)
+        v_ts(q, st("KM", h * H + 15, h * H + H, 16), 2047.0, A.add)
+        v_ts(sg, q, 10, A.arith_shift_right, 2, A.bitwise_and)
+        v_ts(a, q, 16, A.arith_shift_right, 3, A.bitwise_and)
+        v_ts(k, q, 12, A.arith_shift_right, 15, A.bitwise_and)
+        v_ts(h8("kl%d" % t, h), q, 0.0, A.is_lt, 32.0, A.mult)
+        v_tt(h8("klc", h), h8("kl%d" % t, h), h8("CL", h), A.add)
+        v_ts(s2, sg, -1.0, A.add)
+        v_ts(a1, a, 1.0, A.add)
+        v_tt(dl, s2, a1, A.mult)
+        v_tt(fs, k, dl, A.add)
+        v_ts(f, fs, 15, A.bitwise_and)
+        v_tt(o1, f, h8("C16", h), A.add)
+        v_cp(h8("uf", h), o1)
 
     def x_n(h):
-        s_act(half("SF", h), ind(wide("S", h), h8("uf", h)), F.Copy)
-        mm(XP[h], half("SF", h), full("Ib"), True, h == 1)
-        if h == 0:
-            s_act(half("DF", h), ind(wide("D", h), h8("uf", h)), F.Copy)
-            mm(XP[h], half("DF", h), full("Ib"), False, True)
+        s_act(half("SF", h), ind(part("Y", h), h8("uf", h)), F.Copy)
+        mm(XP[h], half("SF", h), full("Ib"), True, True)
         s_act(half("XT", h), XP[h], F.Copy)
 
-    def near(h, cs):
-        for c in cs:
+    def near(h):
+        for c in range(4):
             b = (NEAR[nb[0] % 4], 0, 512)
             nb[0] += 1
-            mm(b, full("Ib"), wide("S", h, c, 1), True, False)
-            if h:
-                mm(b, full("Ib"), wide("D", h, c, 1), False, False)
+            mm(b, full("Ib"), part("Y", h, 4 * c, 4), True, False)
+            mm(b, full("Ib"), part("D", h, 4 * c, 4), False, False)
             mm(b, half("XT", h), ("EX", 512 * c, 512 * c + 512), False, True)
-            s_act(wide("NA", h, c, 1), b, F.Abs)
+            s_act(part("NA", h, 4 * c, 4), b, F.Abs)
             for i in range(4 * c, 4 * c + 4):
-                mm(ND[h], lanes("Q1", i), part("NA", h, i), i == 0, False)
+                mm(ND[h], lanes("Q1", i), part("NA", h, i, 1), i == 0, False)
 
     def new_arrays(t, h):
         x = st(ND[h][0], ND[h][1], ND[h][2], 16)
         mm(x, full("I256"), h8("kl%d" % t, h), False, False)
         mm(x, full("I256"), h8("g1", h), False, True)
-        s_sign(half("pen", h), ND[h], full("cn"), -1.0)
+        s_sign(half("pen", h), ND[h], full("cn"))
         ko = half("Ko%d" % t, h)
         v_scan(rev("ts", h * H, h * H + H), full("RN"), rev("pen", h * H, h * H + H), 4.0, A.add, A.min)
         v_tt(h8("uy", h), st("ts", h * H, h * H + H, 16), h8("CU", h), A.add)
@@ -438,28 +468,23 @@ def rank_program(g, core, T, topo):
         else:
             dmas("y", "dy%d" % h, [(T.yk[:, h * H:h * H + H], pa(ko))], [ko], ["yk%d" % h], 64)
 
-    def window(t):
+    def windows(t):
+        dmas("y", "dw", [(T.W[0::16, 0:4096], T["Pl%d" % t][:])], ["Pl%d" % t, "Wz"], ["W0"], 128)
         for h in range(2):
-            mm(LP[h], full("LD"), kh(t, h), True, True)
-        s_act(full("KD"), ("b5", 0, 256), F.Copy)
+            mm(half(LP[0], h, LP[1]), full("LD"), kh(t, h), True, True)
+        s_act(full("KD"), LP, F.Copy)
         for h in range(2):
-            mm(XP[h], full("L15"), kh(t, h), True, True)
-        s_act(full("K15"), ("b5", 256, 512), F.Copy)
+            mm(half(LQ[0], h, LQ[1]), full("L15"), kh(t, h), True, True)
+        s_act(full("K15"), LQ, F.Copy)
         dmas("y", "dkd", [(T.kd[:, 1:17, :], T.KD[:])], ["KD"], ["kd"], 128)
-        dmas("y", "dw2", [(T.W[0::16, 4096 + h * H:4096 + h * H + H], T[kh(t, h)[0]][0::16, kh(t, h)[1]:kh(t, h)[2]]) for h in range(2)], ["Kl%d" % t, "W"], ["W16"], 8)
+        dmas("y", "dw2", [(T.W[0::16, 4096 + h * H:4096 + h * H + H], T[kh(t, h)[0]][0::16, kh(t, h)[1]:kh(t, h)[2]]) for h in range(2)],
+             ["Kl%d" % t, "Wz"], ["W16"], 8)
         runs = [(T.FF[j::16, 0:(15 - j) * 256], T.kd[:, j + 1:16, :]) for j in range(1, 15)] + [(T.FF[:, 16 * 256:FW], T.kd[:, 0:16, :])]
         dmas("y", "df", runs[NG:], ["kd", "kz", "FF"], ["Fy"], 500)
         dmas("p", "dg", runs[:NG], ["kd", "FF"], ["Fg"], 500)
-
-    def names(t, h):
-        x = half(P32[0], h, P32[1])
-        mm(x, full("I32"), half("Pl%d" % t, h), True, False)
-        mm(x, full("Ib"), half("N23", 0), False, True)
-        if h:
-            dmas("y", "dw", [(T.W[0::16, 0:4096], T["Pl%d" % t][:])], ["Pl%d" % t, "W"], ["W0"], 128)
-
-    def kh(t, h):
-        return ("Kl%d" % t, KZ + (KZ + H) * h, (KZ + H) * (h + 1))
+        for h in range(2):
+            mm(half(P32[0], h, P32[1]), full("I32"), half("Pl%d" % t, h), True, False)
+            mm(half(P32[0], h, P32[1]), full("Ib"), full("N23"), False, True)
 
     def k_list(t, h):
         v_cp(half("Ku", h), ind(kh(t, h), h8("uP", 0)))
@@ -468,12 +493,9 @@ def rank_program(g, core, T, topo):
         v_cp(half("Pu", h), ind(half("Pl%d" % t, h), h8("uP", 0)))
 
     def phages(t, h):
-        kl, po = h8("kl%d" % t, h), half("Po%d" % t, h)
-        v_ts(kl, h8("q", h), 0.0, A.is_lt, 32.0, A.mult)
-        v_tt(h8("klc", h), kl, h8("CL", h), A.add)
+        po = half("Po%d" % t, h)
         v_ts(h8("uK", h), h8("klc", h), KZ / 256.0 - 32.0 - h / 2.0, A.add, 256.0, A.mult)
-        kw = ("Kl%d" % t, (KZ + H) * h, (KZ + H) * (h + 1))
-        v_tt(half("kp", h), ind(kw, h8("uK", h)), half("Pl%d" % t, h), A.mult)
+        v_tt(half("kp", h), ind(("Kl%d" % t, (KZ + H) * h, (KZ + H) * (h + 1)), h8("uK", h)), half("Pl%d" % t, h), A.mult)
         v_tt(half("p1", h), half("kp", h), half(P32[0], h, P32[1]), A.add)
         v_ts(half("p2", h), half("p1", h), 5, A.arith_shift_right, 4095, A.bitwise_and)
         v_cp(po, half("p2", h))
@@ -490,17 +512,16 @@ def rank_program(g, core, T, topo):
         v_ts(full("Am"), full("Ai"), 15 << 18, A.bitwise_and)
         v_ts(full("thr"), full("Am"), 160.0 * 65536 - 1, A.add)
 
-    def own_names():
-        x = ind(full("W"), full("uV"))
-        op("v", lambda: V.tensor_scalar(T.VG[:], pa(x), -2048.0, None, A.add), WK + [full("uV")], ["VG"], ns(full("VG"), 1, x))
-
     def base():
+        v_tt(full("av"), full("klc"), full("g1"), A.add)
+        v_tt(full("oN"), full("f"), full("av"), A.add)
+        v_tt(full("oM"), full("oN"), full("CW"), A.min)
+        v_ts(full("uN"), full("oM"), 256.0, A.mult)
         v_tt(full("BA"), ind(full("W"), full("uN")), full("K15"), A.add, WK)
 
-    def scatter(c):
-        u, x = full("uX")[1] + SC * c, (16 * SC * c, 16 * SC * (c + 1))
-        xs = T.X[:, 0:XW].indirect(T.LU[:, u:u + SC])
-        op("v", lambda: V.tensor_tensor(xs, pa(("YK",) + x), pa(("wg",) + x), A.add), [("LU", u, u + SC), ("YK",) + x, ("wg",) + x], ["X"], 55 + 50 * SC)
+    def marked(x, stop):
+        mm(x, full("NL"), full("OD"), True, False)
+        mm(x, full("L0h"), full("VG"), False, stop)
 
     def equals():
         todo, at = [c for c in range(LO) if c % SC < SC - 1], 0
@@ -510,89 +531,67 @@ def rank_program(g, core, T, topo):
             mm((ME[0], ME[1] + lo, ME[1] + hi), full("BK"), ("EQ", at, at + hi - lo), False, c == todo[-1])
             at += hi - lo
 
-    def marked(x, stop):
-        mm(x, full("NL"), full("OD"), True, False)
-        mm(x, full("L0h"), full("VG"), False, stop)
-
-    def gathers(h):
-        bias(h)
-        todo = None
-        for c in range(4):
-            s_gather(h, c)
-            n = PIECE[4 * h + c]
-            for a in range(0, 4, n):
-                d_gather(h, c, a, n)
-                if todo:
-                    keys(h, *todo)
-                todo = (4 * c + a, n, ABS[4 * h + c]) if c == 3 else (4 * c, 4, ABS[4 * h + c]) if a + n == 4 else None
-        keys(h, *todo)
+    def scatter(c):
+        u, x = full("uX")[1] + SC * c, (16 * SC * c, 16 * SC * (c + 1))
+        xs = T.X[:, 0:XW].indirect(T.LU[:, u:u + SC])
+        op("v", lambda: V.tensor_tensor(xs, pa(("YK",) + x), pa(("wg",) + x), A.add), [("LU", u, u + SC), ("YK",) + x, ("wg",) + x], ["X"], 55 + 50 * SC)
 
     for t in range(R):
+        now[0] = t
         last = t == R - 1
-        p0, p1 = pick(0), pick(1)
         if t:
-            k_list(t, 0)
             p_list(t, 0)
+            k_list(t, 0)
             p_list(t, 1)
+            thresh(t)
         gathers(0)
         if t:
             k_list(t, 1)
-        window(t)
-        if t == 0:
-            more_constants()
-        names(t, 0)
-        names(t, 1)
-        run(*p0)
+        windows(t)
+        pick(t, 0)
         x_n(0)
-        if t:
-            thresh(t)
+        if t == 0:
+            v_ts(st("RC", 0, 256, 16), full("CW"), 256.0, A.mult, -2048.0, A.add)
+            v_cp(full("L0h"), full("L0"))
         gathers(1)
         phages(t, 0)
-        run(*p1[:2])
+        pick(t, 1)
         v_ts(full("g1"), full("q"), full("thr"), A.is_ge, 32.0, A.mult)
-        v_ts(full("k"), full("q"), 12, A.arith_shift_right, 15, A.bitwise_and)
-        v_ts(full("k2"), full("q"), 0.0, A.is_lt, 32.0, A.mult)
-        v_tt(full("oM"), full("g1"), full("CL"), A.add)
-        v_tt(full("oN"), full("k"), full("k2"), A.add)
-        v_tt(full("oV"), full("oM"), full("oN"), A.add)
+        v_tt(full("oN"), full("k"), full("g1"), A.add)
+        v_tt(full("oV"), full("oN"), full("klc"), A.add)
         v_ts(full("uV"), full("oV"), 17.0, A.min, 256.0, A.mult)
-        run(*p1[2:])
-        own_names()
+        v_ts(full("VG"), ind(full("W"), full("uV")), -2048.0, A.add, more=WK)
         x_n(1)
         marked(VE, True)
         mm(VP, full("L0h"), full("VG"), True, True)
         v_scan(full("RU"), full("RC"), VE, -4096.0, A.max, A.min)
-        v_ts(full("uY"), st("RU", 15, 256, 16), 2048.0, A.add)
-        near(0, range(4))
-        phages(t, 1)
-        v_tt(full("av"), full("oM"), full("k2"), A.add)
-        v_tt(full("oN"), full("f"), full("av"), A.add)
-        v_tt(full("oM"), full("oN"), full("CW"), A.min)
-        v_ts(full("uN"), full("oM"), 256.0, A.mult)
+        near(0)
         if not last:
+            phages(t, 1)
             base()
             new_arrays(t, 0)
-            near(1, range(NE))
         v_tt(full("o2"), full("k"), full("CK"), A.add)
         v_cp(full("uk"), full("o2"))
         marked(ME, False)
         v_tt(("FD", 1, 256), (VP[0], VP[1] + 1, VP[2]), ("RU", 0, 255), A.is_equal)
         mm(ME, full("BK"), full("FD"), False, False)
         equals()
-        s_act(full("YK"), ind(full("X"), full("uY")), F.Copy)
-        s_sign(SG, full("YK"), full("cy"), 1.0)
+        sign = VE if last else P32
+        s_act(full("YK"), ind(full("Y"), full("uk")), F.Copy)
+        s_sign(sign, full("YK"), full("cy"))
         s_act(full("AD"), ind(full("D"), full("uk")), F.Abs)
         v_scan(full("SE"), full("RC"), ME, -4096.0, A.max, A.min)
         v_ts(full("uX"), st("SE", 15, 256, 16), 2048.0, A.add)
         v_ts(full("w2"), full("AD"), 32.0, A.is_le, -128.0, A.mult)
-        v_tt(full("wg"), full("w2"), SG, A.mult)
+        v_tt(full("wg"), full("w2"), sign, A.mult)
         for c in range(LO // SC - 1, -1, -1):
             scatter(c)
         if last:
             dmas("y", "dy3", [(T.yx[:], T.X[:, 0:4096])], ["X"], ["yx"], 1024)
+            phages(t, 1)
             base()
             new_arrays(t, 0)
-        near(1, range(0 if last else NE, 4))
+        near(1)
         new_arrays(t, 1)
     schedule()
     for sm, val in sorted(cnt.items()):

import numpy as np
from concourse.mybir import AluOpType as A, ActivationFunctionType as F

R, H, LO = 4, 128, 16
BIG = float(2 ** 30)
OFF = 65536.0
FW, WW, XW = 17 * 256, 17 * 256 + 16, 4096 + 256
SC = 4
NG = 5
KZ = 16
YP, DP, KP = ((2, 2, 4, 4, 4), (4, 4, 4, 4)), ((2, 2, 4, 4, 4), (4, 2, 2, 2, 2, 2, 2)), ((4, 4, 4, 4), (-4, -4, -2, -2, -2, 2))
LIST = {
    "v": ("D D D RA RA D D RA Ku Ai RA D D KM D q D sg a D a1 s2 kl k L0h dl D fs D f klc RA o1 uK Am uf kp "
          "KM p1 q thr a sg kl k a1 g1 p2 klc s2 uK dl av RC oN fs kp oV f uV o1 oN p1 VG o2 uf oM Po uN "
          "RU p2 EQ EQ EQ uk EQ EQ EQ EQ FD ts EQ Po uy BA uu EQ EQ EQ EQ Ko w2 SE wg uX X X X Pu+ X Pu+ ts uy uu Ku+ Ko",
          "D D D Ai RA D RA D Am Ku RA thr RA D D KM q D a sg k kl a1 s2 D dl D fs D f D klc o1 RA uf uK kp "
          "KM q p1 a k kl sg a1 g1 o2 s2 p2 oN dl klc oV Po fs uV av uk f VG o1 uf "
          "RU w2 EQ EQ EQ EQ uK oN FD EQ oM EQ EQ EQ wg uN EQ EQ EQ EQ SE uX X X X X kp ts p1 BA uy ts uu uy p2 uu Ko Po Ko"),
    "s": ("Y Y Y Y Y Y Y junk KD Y Y K15 RA RA RA RA RA SF XT NA NA NA NA SF pen YK XT b5 AD NA NA NA NA pen",
          "Y Y Y junk Y Y Y Y KD Y Y RA K15 RA RA RA RA SF XT NA NA YK AD NA b7 SF XT NA NA NA pen NA NA pen"),
}
WAKE, FAR, FIT = 175, 2300, {"v": 0, "s": 0, "t": 200, "p": 2000, "y": 0}
DY, DG, DL = 150, 1000, 1200

SCRATCH = {
    "X": ("sbuf", [128, XW], "bfloat16"),
    "KI": ("sbuf", [128, 256], "int32"), "PI": ("sbuf", [128, 256], "int32"),
    "Ku": ("sbuf", [128, 256], "uint16"), "Pu": ("sbuf", [128, 256], "uint16"),
    "Y": ("sbuf", [128, 4096], "bfloat16"), "D": ("sbuf", [128, 4096], "bfloat16"),
    "RA": ("sbuf", [128, 4096], "bfloat16"), "NA": ("sbuf", [128, 4096], "bfloat16"),
    "KM": ("sbuf", [128, 256], "float32"),
    "LI": ("sbuf", [128, 256], "int32"), "LF": ("sbuf", [128, 256], "float32"), "LB": ("sbuf", [128, 128], "bfloat16"), "LU": ("sbuf", [128, 160], "uint16"),
    "SF": ("sbuf", [128, 256], "bfloat16"), "XT": ("sbuf", [128, 256], "bfloat16"),
    "YK": ("sbuf", [128, 256], "bfloat16"), "AD": ("sbuf", [128, 256], "bfloat16"),
    "w2": ("sbuf", [128, 256], "bfloat16"), "wg": ("sbuf", [128, 256], "bfloat16"),
    "pen": ("sbuf", [128, 256], "bfloat16"), "ts": ("sbuf", [128, 256], "bfloat16"),
    "kp": ("sbuf", [128, 256], "float32"), "p1": ("sbuf", [128, 256], "int32"), "p2": ("sbuf", [128, 256], "int32"),
    "KD": ("sbuf", [128, 256], "float32"), "K15": ("sbuf", [128, 256], "float32"), "BA": ("sbuf", [128, 256], "float32"),
    "W": ("sbuf", [128, WW], "float32"), "FF": ("sbuf", [128, FW], "float32"), "kd": ("dram", [8, 17, 256], "float32"),
    "VG": ("sbuf", [128, 256], "float16"), "RU": ("sbuf", [128, 256], "float32"), "FD": ("sbuf", [128, 256], "bfloat16"),
    "EQ": ("sbuf", [128, 2048], "bfloat16"), "SE": ("sbuf", [128, 256], "float32"),
    "If": ("sbuf", [128, 128], "float32"), "I32": ("sbuf", [128, 128], "float32"), "Ib": ("sbuf", [128, 128], "bfloat16"), "I256": ("sbuf", [128, 128], "bfloat16"),
    "ZF": ("sbuf", [128, 256], "float32"), "ZB": ("sbuf", [128, 256], "bfloat16"),
    "OD": ("sbuf", [128, 256], "bfloat16"), "NL": ("sbuf", [128, 128], "bfloat16"), "EX": ("sbuf", [128, 2048], "bfloat16"),
    "Q": ("sbuf", [128, 576], "bfloat16"), "BK": ("sbuf", [128, 128], "bfloat16"),
    "L0": ("sbuf", [128, 128], "float32"), "L0h": ("sbuf", [128, 128], "float16"),
    "L15": ("sbuf", [128, 128], "float32"), "L16": ("sbuf", [128, 128], "float32"), "LD": ("sbuf", [128, 128], "float32"),
    "RS": ("sbuf", [128, 128], "float32"), "RC": ("sbuf", [128, 256], "float32"), "RN": ("sbuf", [128, 128], "bfloat16"),
    "NB": ("sbuf", [128, 128], "bfloat16"), "J4": ("sbuf", [128, 128], "bfloat16"), "N23": ("sbuf", [128, 128], "bfloat16"),
}
for _i in range(8):
    SCRATCH["b%d" % _i] = ("psum", [128, 512], "float32")
SMALL = {}
for _b, _l in (("LI", "q sg a s2 a1 dl fs f k o1 o2 C16 CK Ai Am"), ("LF", "klc av oV oN oM uy CL CW CU cnt thr cn cy junk"),
               ("LB", "kl0 kl1 kl2 kl3 g1"), ("LU", "uf uk uu uV uN uK uP uX")):
    for _i, _n in enumerate(_l.split()):
        SMALL[_n] = (_b, 16 * _i, 16 * _i + (1 if _n in ("Ai", "Am", "cnt", "thr", "cn", "cy") else 16))
for _t in range(R):
    SCRATCH["Kl%d" % _t] = ("sbuf", [128, 2 * KZ + 256], "float32")
    for _n in ("Pl", "Ko", "Po"):
        SCRATCH["%s%d" % (_n, _t)] = ("sbuf", [128, 256], "float32")

SEMAPHORES = (["v", "s", "t", "p", "ls", "dx", "dk", "dp", "dz", "dz2", "dw", "dw2", "dkd", "df", "dg", "dy0", "dy1", "dy2", "dy3"]
              + ["%s%d" % (n, t) for n in ("Ka", "Kb", "Pa", "Pb") for t in range(1, R)])


def rank_program(g, core, T, topo):
    rank = T.rank_of(core)
    if rank is None:
        return
    nxt, prv = T.cores[(rank + 1) % 4], T.cores[(rank + 3) % 4]
    queues = {"v": g.vector, "s": g.scalar, "t": g.tensor, "p": g, "y": g.sync}
    cnt = {}
    known = {q: {} for q in queues}
    snaps = {}
    recs = {}

    def bank(b):
        return len(b) == 2 and b[0] == "b" and b[1].isdigit()

    def key(x):
        return x if isinstance(x, tuple) else (x, 0, 1 << 30)

    def sync(q, reads, writes):
        need = {}
        for accs, wr in ((reads, False), (writes, True)):
            for x in accs:
                b, lo, hi = key(x)
                for (l2, h2, q2, sm, val, w2) in recs.get(b, ()):
                    if bank(b):
                        hit = q2 != q or (q != "t" and (wr or w2) and l2 < hi and lo < h2)
                    else:
                        hit = (wr or w2) and l2 < hi and lo < h2 and not q2 == q == "t"
                    if hit and val > known[q].get(sm, 0):
                        need[sm] = max(need.get(sm, 0), val)
        kn = known[q]
        for sm in sorted(need):
            if any(o != sm and snaps.get((o, need[o]), {}).get(sm, 0) >= need[sm] for o in need):
                continue
            queues[q].wait_ge(T.sem[sm], need[sm])
        for sm, val in need.items():
            for o, x in snaps.get((sm, val), {}).items():
                kn[o] = max(kn.get(o, 0), x)
            kn[sm] = max(kn.get(sm, 0), val)

    def note(q, reads, writes, sm, val):
        snap = dict(known[q])
        snap[sm] = max(snap.get(sm, 0), val)
        snaps[(sm, val)] = snap
        for accs, wr in ((reads, False), (writes, True)):
            for x in accs:
                b, lo, hi = key(x)
                old = recs.get(b, [])
                if wr and not bank(b):
                    old = [e for e in old if not (lo <= e[0] and e[1] <= hi)]
                old = [e for e in old if not (e[2] == q and e[3] == sm and e[0] >= lo and e[1] <= hi and (wr or not e[5]))]
                recs[b] = old + [(lo, hi, q, sm, val, wr)]

    calls = []
    now = [-1]

    def op(q, call, reads, writes, ns, kind=None):
        def issue():
            sync(q, reads, writes)
            cnt[q] = cnt.get(q, 0) + 1
            call().then_inc(T.sem[q], 1)
            note(q, reads, writes, q, cnt[q])
        calls.append((q, issue, reads, writes, ns, ns, kind, now[0]))

    def dmas(q, sm, pairs, reads, writes, kib):
        def issue():
            sync(q, reads, writes)
            for out, in_ in pairs:
                queues[q].dma_start(out, in_).then_inc(T.sem[sm], 16)
                cnt[sm] = cnt.get(sm, 0) + 16
            note(q, reads, writes, sm, cnt[sm])
        ns = len(pairs) * (DG if q == "p" else DY)
        calls.append((q, issue, reads, writes, ns, ns + DL + 3 * kib, None, now[0]))

    def schedule():
        n = len(calls)
        pred, seen, closed, group, users = [set() for _ in range(n)], {}, {}, {}, {}
        for i, (q, _, reads, writes, _, _, kind, _) in enumerate(calls):
            for accs, wr in ((reads, False), (writes, True)):
                for x in accs:
                    b, lo, hi = key(x)
                    pred[i].update(j for l2, h2, w2, j in seen.get(b, ()) if (wr or w2) and l2 < hi and lo < h2 and j != i)
                    if wr:
                        seen[b] = [e for e in seen.get(b, ()) if not (lo <= e[0] and e[1] <= hi)]
                        if kind and kind[0] and b in closed:
                            pred[i].add(closed[b])
                            pred[i].update(users.pop(b, ()))
                        if kind:
                            group[b] = ([] if kind[0] else group[b]) + [i]
                        if kind and kind[1]:
                            closed[b] = i
                            pred[i].update(group[b][:-1])
                    seen.setdefault(b, []).append((lo, hi, wr, i))
                    if bank(b) and q != "t":
                        users.setdefault(b, []).append(i)
        small, inline = {x[:2]: nm for nm, x in SMALL.items()}, set()
        for q in LIST:
            todo = {}
            for i, c in enumerate(calls):
                if c[0] == q:
                    b, lo, _ = key(c[3][0])
                    nm = small.get((b, lo - lo % 16), b)
                    todo.setdefault((c[7], nm[:2] if nm[:2] in ("kl", "Ko", "Po") and nm[2:].isdigit() else nm), []).append(i)
            line = sorted(i for (t, _), x in todo.items() if t < 0 for i in x)
            for t in range(R):
                for w in LIST[q][t == R - 1].split():
                    x = todo.get((t + w.count("+"), w.rstrip("+")))
                    if x:
                        line.append(x.pop(0))
            assert len(line) == sum(c[0] == q for c in calls)
            for i, j in zip(line, line[1:]):
                if i not in pred[j]:
                    pred[j].add(i)
                    inline.add((i, j))
        succ = [[] for _ in range(n)]
        for i in range(n):
            for j in pred[i]:
                succ[j].append(i)
        banks = [[key(x)[0] for x in c[2] + c[3] if bank(key(x)[0])] for c in calls]
        left, early, free, held = [len(p) for p in pred], [0.0] * n, {q: 0.0 for q in queues}, {}
        ready = {q: [i for i in range(n) if calls[i][0] == q and not left[i]] for q in queues}

        def start(i):
            return max([early[i], free[calls[i][0]]] + [held[b][1] + WAKE for b in banks[i] if b in held and held[b][0] != calls[i][0]])
        for _ in range(n):
            best = None
            for q in queues:
                if ready[q]:
                    at = {i: start(i) for i in ready[q]}
                    i = min(ready[q])
                    while True:
                        fit = [j for j in ready[q] if j > i and at[j] < at[i] and at[j] + calls[j][4] <= at[i] + FIT[q]]
                        if not fit:
                            break
                        i = min(fit)
                    if best is None or at[i] < best[0]:
                        best = (at[i], i)
            t0, i = best
            q = calls[i][0]
            ready[q].remove(i)
            free[q] = t0 + calls[i][4]
            for b in banks[i]:
                held[b] = (q, t0 + calls[i][5])
            for j in succ[i]:
                early[j] = max(early[j], t0 + calls[i][5] + (0 if q == calls[j][0] == "t" or (i, j) in inline else WAKE))
                left[j] -= 1
                if not left[j]:
                    ready[calls[j][0]].append(j)
            calls[i][1]()

    V, S, E = g.vector, g.scalar, g.tensor

    def pa(x):
        return x[3][0] if len(x) > 3 else T[x[0]][:, x[1]:x[2]]

    def ks(*xs):
        return [x[:3] for x in xs if isinstance(x, tuple)] + [x[4] for x in xs if isinstance(x, tuple) and len(x) > 4]

    def ns(o, rate, *xs):
        if any(len(x) > 4 for x in xs):
            return 55 + 0.83 * 1.56 * (o[2] - o[1])
        return 0.83 * max(64, rate * (o[3][1] if len(o) > 3 else o[2] - o[1]))

    def short(*xs):
        return 0.5 if all(SCRATCH[x[0]][2] in ("bfloat16", "uint16") for x in xs) else 1

    def v_tt(o, a, b, f, more=()):
        op("v", lambda: V.tensor_tensor(pa(o), pa(a), pa(b), f), ks(a, b) + list(more), ks(o), ns(o, 1 if bank(a[0]) or bank(b[0]) else 2, a))

    def v_ts(o, a, x, f, y=None, f2=None, more=()):
        x1 = pa(x) if isinstance(x, tuple) else x
        if f2 is None:
            op("v", lambda: V.tensor_scalar(pa(o), pa(a), x1, None, f), ks(a, x) + list(more), ks(o), ns(o, short(o, a), a))
        else:
            op("v", lambda: V.tensor_scalar(pa(o), pa(a), x1, y, f, f2), ks(a, x), ks(o), ns(o, short(o, a), a))

    def v_cp(o, a):
        op("v", lambda: V.tensor_copy(pa(o), pa(a)), ks(a), ks(o), ns(o, short(o, a), a))

    def v_scan(o, d0, d1, init, f, f2):
        op("v", lambda: V.tensor_tensor_scan(pa(o), pa(d0), pa(d1), init, f, f2), ks(d0, d1), ks(o), ns(o, short(o, d0, d1)))

    def v_ms(o, c):
        op("v", lambda: V.memset(pa(o), c), [], ks(o), ns(o, short(o)))

    def s_act(o, a, f):
        op("s", lambda: S.activation(pa(o), pa(a), f), ks(a), ks(o), ns(o, 1, a) + (10 if len(a) > 4 else 60))

    def s_sign(o, a, bias):
        op("s", lambda: S.activation(pa(o), pa(a), F.Sign, bias=pa(bias)), ks(a, bias), ks(o), ns(o, 1) + 60)

    def mm(o, l, r, start, stop):
        n = max(64, o[3][1] if len(o) > 3 else o[2] - o[1]) * (4 if SCRATCH[l[0]][2] == "float32" else 1)
        op("t", lambda: E.matmul(pa(o), pa(l), pa(r), start, stop), ks(l, r), ks(o), 0.42 * n, (start, stop))

    def iota(o, pattern, base, cm):
        flag = {} if SCRATCH[o[0]][2] == "int32" else {"allow_small_or_imprecise_dtypes": True}
        op("p", lambda: g.iota(pa(o), pattern, base, cm, **flag), [], ks(o), ns(o, 2) + 130)

    def pick_of(o, src, pattern, how, fill, base_, cm):
        op("p", lambda: g.affine_select(pa(o), pa(src), pattern, how, fill, base_, cm), ks(src), ks(o), ns(o, 2) + 170)

    def ind(w, u):
        return (w[0], w[1], w[2], (T[w[0]][:, w[1]:w[2]].indirect(T[u[0]][:, u[1]:u[2]]), 16 * (u[2] - u[1])), u[:3])

    def st(b, lo, hi, step):
        return (b, lo, hi, (T[b][:, lo:hi:step], len(range(lo, hi, step))))

    def rev(b, lo, hi):
        return (b, lo, hi, (T[b][:, hi - 1:lo - 1:-1] if lo else T[b][:, hi - 1::-1], hi - lo))

    def full(b):
        return SMALL[b] if b in SMALL else (b, 0, int(SCRATCH[b][1][-1]))

    def h8(b, h):
        x = full(b)
        return (x[0], x[1] + h * 8, x[1] + h * 8 + 8)

    def half(b, h, at=0):
        return (b, at + h * H, at + h * H + H)

    def part(b, h, i=0, n=LO):
        return (b, 2048 * h + 128 * i, 2048 * h + 128 * (i + n))

    def kh(t, h):
        return ("Kl%d" % t, KZ + (KZ + H) * h, (KZ + H) * (h + 1))

    for t in range(1, R):
        for sm, src, x in (("Ka", prv, kh(t, 0)), ("Kb", prv, kh(t, 1)), ("Pa", nxt, half("Pl%d" % t, 0)), ("Pb", nxt, half("Pl%d" % t, 1))):
            cnt[sm + str(t)] = len(topo.engines(src, core))
            recs.setdefault(x[0], []).append((x[1], x[2], "r", sm + str(t), cnt[sm + str(t)], True))
    dmas("y", "dp", [(T.PI[:], T.ph[:])], [], ["PI"], 128)
    dmas("y", "dk", [(T.KI[:], T.ka[:])], [], ["KI"], 256)
    dmas("y", "dx", [(T.X[:, 0:4096], T.x0[:])], [], [("X", 0, 4096)], 1024)

    ZF, ZB, FQ = ("ZF", 0, 128), ("ZB", 0, 128), FW // 4
    v_ms(("W", 0, FQ), 0.0)
    v_ms(full("ZF"), 0.0)
    v_ms(full("ZB"), 0.0)
    v_ms(full("Q"), 0.0)
    iota(full("q"), [[0, 16]], 0, 1)
    iota(full("o1"), [[128, 2], [2, 8]], 0, 0)
    pick_of(full("If"), ZF, [[1, 128]], A.not_equal, 1.0, 0, -1)
    pick_of(full("L16"), ZF, [[16, 8], [0, 16]], A.not_equal, 1.0, 15, -1)
    pick_of(full("Ib"), ZB, [[1, 128]], A.not_equal, 1.0, 0, -1)
    iota(full("J4"), [[0, 8], [4096, 16]], 0, 0)
    for n, w in enumerate((-65536.0, 131072.0, 1.0, 65536.0)):
        x = st("Q", 144 * n + 15, 144 * n + 144, 16)
        pick_of(x, x, [[16, 9]], A.is_gt, w, 0, -1)
    x = st("Q", 15, 576, 16)
    pick_of(x, x, [[0, 4], [16, 9]], A.is_ge, 0.0, 15, -1)
    iota(full("o2"), [[16, 16]], 0, 0)
    iota(full("C16"), [[0, 2], [16, 8]], 0, 0)
    iota(full("CK"), [[2048, 2], [16, 8]], 0, 0)
    pick_of(full("RS"), ZF, [[0, 8], [1, 16]], A.not_equal, BIG, 0, 0)
    pick_of(full("L15"), full("L16"), [[0, 8], [1, 16]], A.not_equal, 0.0, 0, 0)
    pick_of(full("I32"), ZF, [[1, 128]], A.not_equal, 32.0, 0, -1)
    for n in range(1, 4):
        s_act(("W", n * FQ, n * FQ + FQ), ("W", 0, FQ), F.Copy)
    dmas("y", "dz2", [(T.FF[:], T.W[:, 0:FW])], [("W", 0, FW), ("X", 0, 4096)], ["FF", "Wz"], 2176)
    v_ts(full("a"), full("q"), 7, A.bitwise_and)
    v_ts(full("sg"), full("q"), 3, A.arith_shift_right, 1, A.bitwise_and)
    v_ts(full("k"), full("q"), 15, A.bitwise_and)
    v_ts(full("a1"), full("a"), 16.0, A.mult)
    v_tt(full("s2"), full("sg"), full("o1"), A.add)
    v_ms(full("NB"), -864.0 * 65536)
    for t in range(R):
        v_ms(("Kl%d" % t, 0, KZ), 0.0)
        if t == 0:
            v_tt(full("dl"), full("a1"), full("s2"), A.add)
        v_ms(("Kl%d" % t, KZ + H, 2 * KZ + H), 0.0)
        if t == 1:
            v_cp(full("uP"), full("dl"))
    v_cp(full("Pu"), ind(full("PI"), full("uP")))
    v_cp(full("Ku"), ind(full("KI"), full("uP")))
    v_cp(kh(0, 0), half("KI", 0))
    v_cp(kh(0, 1), half("KI", 1))
    v_tt(full("LD"), full("If"), full("L16"), A.subtract)
    v_cp(full("Pl0"), full("PI"))
    dmas("y", "dz", [(T.kd[:, 0:1, :], T.ZF[0:8, 0:256])], ["ZF"], ["kz"], 8)
    iota(full("N23"), [[0, 128]], -2 ** 23, 0)
    for n in range(8):
        pick_of(("EX", 256 * n, 256 * n + 256), full("ZB"), [[1, 2], [16, 8], [0, 16]], A.not_equal, -1.0, 2 * n, -1)
    iota(("W", FW, WW), [[0, 16]], 8192, 0)
    iota(full("RC"), [[0, 256]], -4096, 0)
    pick_of(full("L0"), ZF, [[16, 8], [0, 16]], A.not_equal, 1.0, 0, -1)
    pick_of(full("OD"), full("ZB"), [[0, 16], [1, 16]], A.not_equal, OFF, 0, -1)
    pick_of(full("NL"), ZB, [[0, 8], [1, 16]], A.is_equal, 1.0, 0, -1)
    pick_of(full("I256"), ZB, [[1, 128]], A.not_equal, -256.0, 0, -1)
    pick_of(full("BK"), ZB, [[16, 8], [0, 16]], A.is_gt, 8192.0, 0, -1)
    pick_of(full("BK"), full("BK"), [[16, 8], [0, 16]], A.is_ge, 0.0, 15, -1)
    iota(("X", 4096, XW), [[0, 256]], 0, 0)
    v_tt(full("o2"), full("o2"), full("k"), A.add)
    v_ts(full("a"), full("k"), 128.0, A.mult)
    v_ms(full("RN"), 0.125)
    v_ms(("FD", 0, 1), 0.0)
    v_ms(full("thr"), 160.0 * 65536 - 1)
    v_tt(full("C16"), full("C16"), full("a"), A.add)
    v_tt(full("CK"), full("CK"), full("a"), A.add)
    v_ms(full("cn"), -1023.5)
    v_ms(full("cy"), -127.5)
    v_ts(st("RN", 0, 128, 16), ("ZB", 0, 8), 4.0, A.add)
    v_ts(full("CL"), full("o2"), 1.0 / 256, A.mult)
    v_ts(full("CW"), full("o2"), 1.0 / 256, A.mult, 16.0, A.add)
    v_ts(full("CU"), full("o2"), 1.0 / 2048, A.mult, 1.0, A.add)

    KEY = [("b0", 0, 128), ("b1", 0, 128)]
    ND = [("b1", 128, 256), ("b1", 256, 384)]
    XP = [("b0", 128, 256), ("b5", 384, 512)]
    VP, CN = ("b0", 256, 512), ("b1", 384, 400)
    NEAR = ("b2", "b3", "b4", "b6")
    LP, LQ, P32 = ("b5", 0, 256), ("b5", 256, 512), ("b5", 0, 256)
    VE, ME = ("b7", 0, 256), ("b7", 256, 512)

    def lanes(w, i):
        n = 144 * ("QN", "QR", "Q1", "QP").index(w)
        return ("Q", n + 15 - i, n + 143 - i)

    def send(x, to, sm, dst):
        rid, pid, _ = topo.addr(dst)

        def issue():
            sync("p", [x], [])
            g.remote_dma(pa(to), pa(x), T.sem[sm], T.sem.ls, pid, rid, topo.mask(core, dst))
            cnt["ls"] = cnt.get("ls", 0) + len(topo.engines(core, dst))
        calls.append(("p", issue, [x], [to], 500, FAR + 4 * (x[2] - x[1]), None, now[0]))

    FK, WK = ["Fy", "Fg"], ["W0", "W16", "W"]
    nb = [0]

    def keys(h, i0, n, scalar):
        if scalar:
            s_act(part("RA", h, i0, n), part("D", h, i0, n), F.Abs)
        else:
            for i in range(i0, i0 + n):
                mm(KEY[h], lanes("QN", i), part("D", h, i, 1), False, False)
            v_ts(part("RA", h, i0, n), part("D", h, i0, n), 0.0, A.max)
        for i in range(i0, i0 + n):
            mm(KEY[h], lanes("QP" if scalar else "QR", i), part("RA", h, i, 1), False, False)
            mm(KEY[h], lanes("Q1", i), part("D", h, i, 1), False, i == LO - 1)

    def gathers(h):
        mm(KEY[h], full("Ib"), full("NB"), True, False)
        mm(KEY[h], full("Ib"), full("J4"), False, False)
        a = 0
        for n in YP[h]:
            s_act(part("Y", h, a, n), ind(("X", 0, 4096), ("Pu", H * h + 8 * a, H * h + 8 * (a + n))), F.Copy)
            a += n
        a, b, todo = 0, 0, list(KP[h])
        for n in DP[h] + (0,):
            if n:
                v_tt(part("D", h, a, n), ind(("X", 0, 4096), ("Ku", H * h + 8 * a, H * h + 8 * (a + n))), part("Y", h, a, n), A.subtract)
            while todo and b + abs(todo[0]) <= a:
                keys(h, b, abs(todo[0]), todo[0] < 0)
                b += abs(todo.pop(0))
            a += n

    def pick(t, h):
        q, k, sg, a, s2, a1, dl, fs, f, o1 = [h8(n, h) for n in ("q", "k", "sg", "a", "s2", "a1", "dl", "fs", "f", "o1")]
        v_scan(half("KM", h), full("RS"), KEY[h], BIG, A.add, A.min)
        v_ts(q, st("KM", h * H + 15, h * H + H, 16), 2047.0, A.add)
        v_ts(sg, q, 10, A.arith_shift_right, 2, A.bitwise_and)
        v_ts(a, q, 16, A.arith_shift_right, 3, A.bitwise_and)
        v_ts(k, q, 12, A.arith_shift_right, 15, A.bitwise_and)
        v_ts(h8("kl%d" % t, h), q, 0.0, A.is_lt, 32.0, A.mult)
        v_tt(h8("klc", h), h8("kl%d" % t, h), h8("CL", h), A.add)
        v_ts(s2, sg, -1.0, A.add)
        v_ts(a1, a, 1.0, A.add)
        v_tt(dl, s2, a1, A.mult)
        v_tt(fs, k, dl, A.add)
        v_ts(f, fs, 15, A.bitwise_and)
        v_tt(o1, f, h8("C16", h), A.add)
        v_cp(h8("uf", h), o1)

    def x_n(h):
        s_act(half("SF", h), ind(part("Y", h), h8("uf", h)), F.Copy)
        mm(XP[h], half("SF", h), full("Ib"), True, True)
        s_act(half("XT", h), XP[h], F.Copy)

    def near(h):
        for c in range(4):
            b = (NEAR[nb[0] % 4], 0, 512)
            nb[0] += 1
            mm(b, full("Ib"), part("Y", h, 4 * c, 4), True, False)
            mm(b, full("Ib"), part("D", h, 4 * c, 4), False, False)
            mm(b, half("XT", h), ("EX", 512 * c, 512 * c + 512), False, True)
            s_act(part("NA", h, 4 * c, 4), b, F.Abs)
            for i in range(4 * c, 4 * c + 4):
                mm(ND[h], lanes("Q1", i), part("NA", h, i, 1), i == 0, False)

    def new_arrays(t, h):
        x = st(ND[h][0], ND[h][1], ND[h][2], 16)
        mm(x, full("I256"), h8("kl%d" % t, h), False, False)
        mm(x, full("I256"), h8("g1", h), False, True)
        s_sign(half("pen", h), ND[h], full("cn"))
        ko = half("Ko%d" % t, h)
        v_scan(rev("ts", h * H, h * H + H), full("RN"), rev("pen", h * H, h * H + H), 4.0, A.add, A.min)
        v_tt(h8("uy", h), st("ts", h * H, h * H + H, 16), h8("CU", h), A.add)
        v_ts(h8("uu", h), h8("uy", h), 2048.0, A.mult)
        v_tt(ko, ind(full("FF"), h8("uu", h)), half("BA", h), A.add, FK)
        if t < R - 1:
            send(ko, kh(t + 1, h), ("Ka", "Kb")[h] + str(t + 1), nxt)
        else:
            dmas("y", "dy%d" % h, [(T.yk[:, h * H:h * H + H], pa(ko))], [ko], ["yk%d" % h], 64)

    def windows(t):
        dmas("y", "dw", [(T.W[0::16, 0:4096], T["Pl%d" % t][:])], ["Pl%d" % t, "Wz"], ["W0"], 128)
        for h in range(2):
            mm(half(LP[0], h, LP[1]), full("LD"), kh(t, h), True, True)
        s_act(full("KD"), LP, F.Copy)
        for h in range(2):
            mm(half(LQ[0], h, LQ[1]), full("L15"), kh(t, h), True, True)
        s_act(full("K15"), LQ, F.Copy)
        dmas("y", "dkd", [(T.kd[:, 1:17, :], T.KD[:])], ["KD"], ["kd"], 128)
        dmas("y", "dw2", [(T.W[0::16, 4096 + h * H:4096 + h * H + H], T[kh(t, h)[0]][0::16, kh(t, h)[1]:kh(t, h)[2]]) for h in range(2)],
             ["Kl%d" % t, "Wz"], ["W16"], 8)
        runs = [(T.FF[j::16, 0:(15 - j) * 256], T.kd[:, j + 1:16, :]) for j in range(1, 15)] + [(T.FF[:, 16 * 256:FW], T.kd[:, 0:16, :])]
        dmas("y", "df", runs[NG:], ["kd", "kz", "FF"], ["Fy"], 500)
        dmas("p", "dg", runs[:NG], ["kd", "FF"], ["Fg"], 500)
        for h in range(2):
            mm(half(P32[0], h, P32[1]), full("I32"), half("Pl%d" % t, h), True, False)
            mm(half(P32[0], h, P32[1]), full("Ib"), full("N23"), False, True)

    def k_list(t, h):
        v_cp(half("Ku", h), ind(kh(t, h), h8("uP", 0)))

    def p_list(t, h):
        v_cp(half("Pu", h), ind(half("Pl%d" % t, h), h8("uP", 0)))

    def phages(t, h):
        po = half("Po%d" % t, h)
        v_ts(h8("uK", h), h8("klc", h), KZ / 256.0 - 32.0 - h / 2.0, A.add, 256.0, A.mult)
        v_tt(half("kp", h), ind(("Kl%d" % t, (KZ + H) * h, (KZ + H) * (h + 1)), h8("uK", h)), half("Pl%d" % t, h), A.mult)
        v_tt(half("p1", h), half("kp", h), half(P32[0], h, P32[1]), A.add)
        v_ts(half("p2", h), half("p1", h), 5, A.arith_shift_right, 4095, A.bitwise_and)
        v_cp(po, half("p2", h))
        if t < R - 1:
            send(po, half("Pl%d" % (t + 1), h), ("Pa", "Pb")[h] + str(t + 1), prv)
        elif h:
            dmas("y", "dy2", [(T.yp[:], T["Po%d" % t][:])], ["Po%d" % t], ["yp"], 128)

    def thresh(t):
        for u in range(t):
            mm(CN, full("BK"), full("kl%d" % u), u == 0, u == t - 1)
        op("s", lambda: S.activation(pa(full("junk")), pa(CN), F.Copy, accum_out=pa(full("cnt"))), [CN], [full("junk"), full("cnt")], 200)
        v_cp(full("Ai"), full("cnt"))
        v_ts(full("Am"), full("Ai"), 15 << 18, A.bitwise_and)
        v_ts(full("thr"), full("Am"), 160.0 * 65536 - 1, A.add)

    def base():
        v_tt(full("av"), full("klc"), full("g1"), A.add)
        v_tt(full("oN"), full("f"), full("av"), A.add)
        v_tt(full("oM"), full("oN"), full("CW"), A.min)
        v_ts(full("uN"), full("oM"), 256.0, A.mult)
        v_tt(full("BA"), ind(full("W"), full("uN")), full("K15"), A.add, WK)

    def marked(x, stop):
        mm(x, full("NL"), full("OD"), True, False)
        mm(x, full("L0h"), full("VG"), False, stop)

    def equals():
        todo, at = [c for c in range(LO) if c % SC < SC - 1], 0
        for c in todo:
            lo, hi = 16 * c + 16, 16 * SC * (c // SC + 1)
            v_ts(("EQ", at, at + hi - lo), (VP[0], VP[1] + lo, VP[1] + hi), ("RU", 16 * c + 15, 16 * c + 16), A.is_equal)
            mm((ME[0], ME[1] + lo, ME[1] + hi), full("BK"), ("EQ", at, at + hi - lo), False, c == todo[-1])
            at += hi - lo

    def scatter(c):
        u, x = full("uX")[1] + SC * c, (16 * SC * c, 16 * SC * (c + 1))
        xs = T.X[:, 0:XW].indirect(T.LU[:, u:u + SC])
        op("v", lambda: V.tensor_tensor(xs, pa(("YK",) + x), pa(("wg",) + x), A.add), [("LU", u, u + SC), ("YK",) + x, ("wg",) + x], ["X"], 55 + 50 * SC)

    for t in range(R):
        now[0] = t
        last = t == R - 1
        if t:
            p_list(t, 0)
            k_list(t, 0)
            p_list(t, 1)
            thresh(t)
        gathers(0)
        if t:
            k_list(t, 1)
        windows(t)
        pick(t, 0)
        x_n(0)
        if t == 0:
            v_ts(st("RC", 0, 256, 16), full("CW"), 256.0, A.mult, -2048.0, A.add)
            v_cp(full("L0h"), full("L0"))
        gathers(1)
        phages(t, 0)
        pick(t, 1)
        v_ts(full("g1"), full("q"), full("thr"), A.is_ge, 32.0, A.mult)
        v_tt(full("oN"), full("k"), full("g1"), A.add)
        v_tt(full("oV"), full("oN"), full("klc"), A.add)
        v_ts(full("uV"), full("oV"), 17.0, A.min, 256.0, A.mult)
        v_ts(full("VG"), ind(full("W"), full("uV")), -2048.0, A.add, more=WK)
        x_n(1)
        marked(VE, True)
        mm(VP, full("L0h"), full("VG"), True, True)
        v_scan(full("RU"), full("RC"), VE, -4096.0, A.max, A.min)
        near(0)
        if not last:
            phages(t, 1)
            base()
            new_arrays(t, 0)
        v_tt(full("o2"), full("k"), full("CK"), A.add)
        v_cp(full("uk"), full("o2"))
        marked(ME, False)
        v_tt(("FD", 1, 256), (VP[0], VP[1] + 1, VP[2]), ("RU", 0, 255), A.is_equal)
        mm(ME, full("BK"), full("FD"), False, False)
        equals()
        sign = VE if last else P32
        s_act(full("YK"), ind(full("Y"), full("uk")), F.Copy)
        s_sign(sign, full("YK"), full("cy"))
        s_act(full("AD"), ind(full("D"), full("uk")), F.Abs)
        v_scan(full("SE"), full("RC"), ME, -4096.0, A.max, A.min)
        v_ts(full("uX"), st("SE", 15, 256, 16), 2048.0, A.add)
        v_ts(full("w2"), full("AD"), 32.0, A.is_le, -128.0, A.mult)
        v_tt(full("wg"), full("w2"), sign, A.mult)
        for c in range(LO // SC - 1, -1, -1):
            scatter(c)
        if last:
            dmas("y", "dy3", [(T.yx[:], T.X[:, 0:4096])], ["X"], ["yx"], 1024)
            phages(t, 1)
            base()
            new_arrays(t, 0)
        near(1)
        new_arrays(t, 1)
    schedule()
    for sm, val in sorted(cnt.items()):
        g.wait_ge(T.sem[sm], val)
